import numpy as np, ml_dtypes
CORES = [8,136,40,168]
N = 4
BF = ml_dtypes.bfloat16
def gentries(a):
    return np.ascontiguousarray(a.reshape(8, 16, -1).transpose(0, 2, 1)).reshape(8, -1)
def gtable(e):
    e = np.asarray(e); return np.ascontiguousarray(e.reshape(8, -1, 16).transpose(0, 2, 1)).reshape(128, -1).astype(np.int32)
L, M, B, P = 5, 256, 32, 4
H, F, E, G, LN = (N - 1) * B, (L - 1) * M, L * M, (L - 1) * (N - 1) * B, M // 2
NONE = E + G
LEV = np.concatenate([np.arange(E) // M, np.arange(G) // H, np.array([-1])])
DL = np.broadcast_to((np.arange(F) // M + 1)[:, None], (N, 8, F, 16)); SL = np.broadcast_to(np.concatenate([np.arange(F) // M, np.arange(G) // H]), (N, 8, F + G))
GM = [np.arange(8), 7 - np.arange(8), (8 - np.arange(8)) % 8]
def names(rng, lv, low):
    x = np.where(rng.random(lv.shape) < low, 0, (rng.random(lv.shape) * lv).astype(np.int64))
    y = rng.integers(0, M + H, lv.shape)
    return np.where(y < M, x * M + y, E + x * H + y - M)
def parts(rng):
    A = np.minimum((256 * rng.random((N, 8, E, 16)) ** 0.1666).astype(np.int64), 255); c = np.arange(E)[:, None]
    tight = rng.random((N, 8, E, 1)) < np.where(c < M, 0.0, np.where(c < F, 0.12, 0.3))
    A = np.where(tight, (A * (0.3 + 0.5 * rng.random((N, 8, E, 1)))).astype(np.int64), A)
    dp = names(rng, DL, 0.6); dp = np.where(rng.random(dp.shape) < rng.choice(np.array([0.0, 0.25, 0.5]), (N, 8, 1, 1)), NONE, dp)
    sb = names(rng, SL + 1, 0.3); sb = np.where(rng.random(sb.shape) < 0.0625, NONE, sb)
    return A, dp, sb, rng.integers(0, M, (N, 8, L - 1, N - 1, B)), rng.integers(40, 161, (N, 8, M))
def pack(A, dp, sb, bd, th):
    return {"av": np.ascontiguousarray(A.transpose(0, 1, 3, 2)).reshape(N, 128, E).astype(np.float32).astype(BF),
            "dp": np.ascontiguousarray(dp.transpose(0, 1, 3, 2)).reshape(N, 128, F).astype(np.int32), "sb": np.ascontiguousarray(sb).astype(np.int32),
            "bd": np.stack([gtable(a.reshape(8, -1)) for a in bd]), "th": np.ascontiguousarray(th).astype(np.int32)}
def setup_inputs(rng):
    A, dp, sb, bd, th = parts(rng)
    return pack(A, dp, sb, bd, th)
def setup_inputs_spread(rng):
    A, dp, sb, bd, th = parts(rng)
    A = np.where(rng.random((N, 8, E, 1)) < 0.1, np.exp2(8 * rng.random(A.shape)).astype(np.int64) - 1, 256 - np.exp2(7 * rng.random(A.shape)).astype(np.int64))
    dp = np.where(rng.random(dp.shape) < rng.choice(np.array([0.3, 0.6, 0.9]), (N, 8, F, 1)), NONE, dp)
    bd = np.where(rng.random(bd.shape) < 0.5, (M * rng.random(bd.shape) ** 4).astype(np.int64), bd)
    th = np.where(rng.random(th.shape) < 0.5, np.exp2(8 * rng.random(th.shape)).astype(np.int64) - 1, rng.integers(0, 256, th.shape))
    return pack(A, dp, sb, bd, th)
def setup_inputs_ends(rng):
    A, dp, sb, bd, th = parts(rng)
    A = np.where(rng.random((N, 8, E, 1)) < 0.1, rng.integers(16, 255, A.shape), np.where(rng.random(A.shape) < rng.choice(np.array([0.02, 0.06, 0.15]), (N, 8, 1, 1)), 0, 255))
    A[:, :, 0] = np.where(rng.random((N, 8, 16)) < 0.5, 0, 255)
    c = rng.random((N, 8, F, 1)); x = names(rng, DL, 0.6)
    z = np.where((c > 0.4) & (c < 0.6) & (rng.random(x.shape) < 0.5), 0, NONE)
    dp = np.where(rng.random(x.shape) < np.where(c < 0.6, 0.125, 0.5), x, z)
    sb = np.where(rng.random(sb.shape) < 0.7, np.where(rng.random(sb.shape) < 0.5, 0, NONE), sb)
    bd = np.where(rng.random(bd.shape) < 0.75, np.where(rng.random(bd.shape) < 0.5, 0, M - 1), bd)
    e = np.where(rng.random(th.shape) < 0.5, 0, 255); th = np.where(rng.random(th.shape) < 0.8, e, rng.integers(1, 255, th.shape))
    for j in (F, F + 1, E - 2, E - 1):
        A[:, :, j] = 255; dp[:, :, j - M] = NONE; th[:, :, j - F] = e[:, :, j - F]
    for j in (F, E - 2): dp[:, :, j - M, 15] = NONE - 1
    for j in (F + 1, E - 1): dp[:, :, j - M, 14:] = F - 1
    A[:, :, F - 1] = 0; A[:, :, F - 1, 15] = 254; dp[:, :, F - 1 - M] = NONE
    for j in (F + 2, E - 3): A[:, :, j] = 0; th[:, :, j - F] = e[:, :, j - F]
    for j in (F + 4, E - 5): A[:, :, j] = 255; dp[:, :, j - M] = NONE; th[:, :, j - F] = e[:, :, j - F]
    return pack(A, dp, sb, bd, th)
def couples(rng):
    o = np.concatenate([np.array([0, LN - 1, LN - 3, LN - 2]), 1 + rng.permutation(LN - 4)]).reshape(-1, 2)
    return np.min(o, axis=1), np.max(o, axis=1)
def setup_inputs_crowd(rng):
    A, dp, sb, bd, th = parts(rng); i = np.arange(M)
    for r in range(N):
        for g in range(8):
            kind = (r + g) % 7; z = rng.permutation(M)[:17]; A[r, g, F:] = 10; A[r, g, F + i, rng.integers(0, 16, M)] = 255
            if kind < 2:
                hub = int(z[16]); A[r, g, hub] = rng.integers(70, 121, 16); th[r, g] = rng.integers(0, 21, M)
            elif kind < 4:
                hub = F - M + int(rng.integers(0, M)); dp[r, g, hub - M] = z[:16]; A[r, g, hub] = 255
                A[r, g, z[:16]] = 255; A[r, g, z[:16], rng.permutation(16)] = rng.integers(60, 121, 16); th[r, g] = rng.integers(200, 256, M)
            elif kind == 4:
                hub = F - M + int(rng.integers(0, M)); dp[r, g, hub - M] = z[:16]; dates = rng.permutation(16)
                A[r, g, hub] = 255; A[r, g, hub, dates[:8]] = rng.integers(60, 121, 8)
                A[r, g, z[:16]] = 255; A[r, g, z[:16], np.concatenate([dates[8:], dates[8:]])] = rng.integers(60, 121, 16)
                th[r, g] = np.where(rng.random(M) < 0.5, rng.integers(0, 21, M), rng.integers(200, 256, M))
            else:
                a, b = couples(rng); n = len(a); u = 1 + rng.permutation(M - 1); u[2] = 0
                za, zb = u[:n], u[n:2 * n]; y = rng.random(n) < 0.25; da, db = 2 * rng.integers(0, 8, n), 2 * rng.integers(0, 8, n) + 1
                if kind == 5:
                    y[:2] = False; y[2] = True; da[y] = 0
                w = np.zeros(LN, np.int64); w[a] = np.arange(n); w[b] = np.arange(n)
                dt = np.zeros(LN, np.int64); dt[a] = da; dt[b] = db
                A[r, g, F:] = 10; A[r, g, F + i, dt[i >> 1]] = 255
                if kind == 5:
                    hub = za; A[r, g, hub] = rng.integers(70, 121, (n, 16)); th[r, g] = rng.integers(0, 21, M); A[r, g, za[y], 0] = 0
                    for h in (0, 1):
                        j = 2 * a[y] + h; A[r, g, F + j] = 0; A[r, g, F + j, 0] = 255; th[r, g, j] = 0
                else:
                    y[0] = True; y[1] = False; hub = F - M + 1 + rng.permutation(M - 1)[:n]; hub[1] = M
                    A[r, g, hub] = 255; A[r, g, za] = 255; A[r, g, zb] = 255
                    A[r, g, za, da] = rng.integers(60, 121, n); A[r, g, zb, db] = rng.integers(60, 121, n)
                    s = np.argsort(rng.random((n, 16)), axis=1); dp[r, g, hub - M] = NONE
                    dp[r, g, hub - M, s[:, 0]] = za; dp[r, g, hub - M, s[:, 1]] = zb
                    sb[r, g, za[y]] = za[y]; sb[r, g, zb[0]] = NONE; sb[r, g, za[1]] = NONE
                    bk = rng.random(n) < 0.25; bk[:2] = False; bk[2] = True
                    th[r, g] = np.where(bk[w[i >> 1]], rng.integers(0, 13, M), rng.integers(200, 256, M))
                hub = hub[w[i >> 1]][:, None]
            m = rng.random((M, 16)) < 0.2; m[i, rng.integers(0, 16, M)] = True
            dp[r, g, F - M:] = np.where(m, hub, NONE)
            if kind in (1, 3):
                j = 2 * int(rng.choice(np.array([0, LN - 1, rng.integers(0, LN)]))); dp[r, g, F - M + j:F - M + j + 2] = NONE
    return pack(A, dp, sb, bd, th)
def setup_inputs_chains(rng):
    A, dp, sb, bd, th = parts(rng)
    A[:, :, M:] = rng.integers(254, 256, (N, 8, F, 16)); A[:, :, :M] = rng.choice(np.array([0, 15, 16, 50, 51, 100, 101] + [253] * 20), (N, 8, M, 16))
    odd = ((np.arange(N)[:, None] + np.arange(8)) % 2 == 1)[:, :, None, None]
    x = np.where(odd & (rng.random(DL.shape) < 0.25), E + (DL - 1) * H + rng.integers(0, H, DL.shape), (DL - 1) * M + rng.integers(0, M, DL.shape))
    x = np.where(rng.random((N, 8, F, 1)) < 0.25, x[..., :1], x); k = np.arange(16)
    m = (k == rng.integers(0, 16, (N, 8, F, 1))) | (k == rng.choice(np.array([0, 7, 15]), (N, 8, F, 1)))
    dp = np.where(m, x, NONE); u = rng.integers(0, 4, SL.shape)
    own = np.concatenate([np.arange(F), E + np.arange(G)])
    sb = np.where(u == 0, NONE, np.where(u == 1, own, np.where(u == 2, E + (SL + 1) * H - 1, sb)))
    th = rng.choice(np.array([0, 16, 50, 51, 52, 100, 101, 102, 253, 254, 255]), (N, 8, M))
    return pack(A, dp, sb, bd, th)
def setup_inputs_calm(rng):
    A, dp, sb, bd, th = parts(rng); base = np.array([16, 17, 18, 19, 33, 35, 254, 255]); i = np.arange(LN)
    for r in range(N):
        for g in range(8):
            a = np.where(rng.random(LN) < 0.7, base[(r + g) % 8], rng.choice(base, LN)); z = rng.permutation(M)[:LN]
            A[r, g, z] = np.maximum(a - 64, 0)[:, None]; A[r, g, z, rng.integers(0, 16, LN)] = a
            A[r, g, F:] = 255; A[r, g, F - M + i] = 255
            dp[r, g, F - 2 * M + i] = NONE; dp[r, g, F - 2 * M + i, rng.integers(0, 16, LN)] = z
            hub = np.where(i % 2 == 1, F - M + i, z)
            for h in (0, 1):
                dp[r, g, F - M + 2 * i + h] = NONE; dp[r, g, F - M + 2 * i + h, rng.integers(0, 16, LN)] = hub
            w = i[rng.random(LN) < 0.125]; dp[r, g, F - M + 2 * w + 1, rng.integers(0, 16, len(w))] = E + rng.integers(0, H, len(w))
            th[r, g, 2 * i] = np.maximum(a - rng.choice(np.array([15, 16, 31, 32]), LN), 0); th[r, g, 2 * i + 1] = np.maximum(a - rng.choice(np.array([15, 16, 17]), LN), 0)
    return pack(A, dp, sb, bd, th)
def check_inputs(d):
    bad = []
    for k, lo, hi in (("av", 0, 255), ("dp", 0, NONE), ("sb", 0, NONE), ("bd", 0, M - 1), ("th", 0, 255)):
        x = np.asarray(d[k]).astype(np.float64)
        if not np.all((x >= lo) & (x <= hi)): bad.append("range of " + k)
        elif not np.all(x == np.floor(x)): bad.append("whole numbers in " + k)
    if np.any(LEV[np.clip(np.asarray(d["dp"]).astype(np.int64), 0, NONE)] > np.arange(F) // M): bad.append("levels of dp")
    if np.any(LEV[np.clip(np.asarray(d["sb"]).astype(np.int64), 0, NONE)] > SL): bad.append("levels of sb")
    return bad
def first(want, at):
    lo = np.full((N, 8, E), LN); n, g, i = np.nonzero(want); np.minimum.at(lo, (n, g, at[want]), i)
    return want & (np.take_along_axis(lo, np.where(want, at, 0), 2) == np.arange(LN))
def reference(av, dp, sb, bd, th):
    A = np.ascontiguousarray(av.astype(np.int32).reshape(N, 8, 16, E).transpose(0, 1, 3, 2))
    D = np.ascontiguousarray(dp.astype(np.int64).reshape(N, 8, 16, F).transpose(0, 1, 3, 2))
    S = sb.astype(np.int64); t0 = th.astype(np.int64)
    bl = np.stack([gentries(a) for a in bd]).astype(np.int64).reshape(N, 8, L - 1, N - 1, B)
    ni = np.arange(N)[:, None, None]; gi = np.arange(8)[None, :, None]
    for t in range(P):
        R = np.full((N, 8, NONE + 1, 16), 255, np.int32)
        for l in range(L):
            a = A[:, :, l * M:(l + 1) * M]
            if l > 0:
                ix = D[:, :, (l - 1) * M:l * M].reshape(N, 8, M * 16)
                a = np.minimum(a, np.min(R[ni, gi, ix].reshape(N, 8, M, 16, 16), axis=3))
            R[:, :, l * M:(l + 1) * M] = a
            if l < L - 1:
                for r in range(N):
                    for d in range(1, N):
                        q = r ^ d; h = GM[d % 3]; s = E + l * H + (d - 1) * B
                        R[r, :, s:s + B] = R[q, h[:, None], l * M + bl[q, h, l, d - 1]]
        e = np.broadcast_to(F + 2 * np.arange(LN) + (t & 1), (N, 8, LN))
        re = R[ni, gi, e]; p = np.argmax(re, axis=3); v = np.max(re, axis=3)
        f = e; q = np.full((N, 8, LN), -1); k = np.zeros((N, 8, LN), np.int64)
        for step in range(L - 1):
            go = (f < E) & (A[ni, gi, np.where(f < E, f, 0), p] != v)
            c = D[ni, gi, np.where(go, f - M, 0)]
            k1 = np.argmax(R[ni[..., None], gi[..., None], c, p[..., None]] == v[..., None], axis=3)
            to = np.take_along_axis(c, k1[..., None], 3)[..., 0]
            q = np.where(go, f, q); k = np.where(go, k1, k); f = np.where(go, to, f)
        b = np.take_along_axis(t0, e - F, 2); ok = v >= b
        wa = first((ok & (f < E)) | (~ok & (f == e)), f); wd = first(~ok & (f != e), q)
        na = np.where(ok, np.maximum(v - 16, 0), b); nd = S[ni, gi, np.where(f != e, np.where(f < E, f, f - M), 0)]
        n, g, i = np.nonzero(wa); A[n, g, f[wa], p[wa]] = na[wa]
        n, g, i = np.nonzero(wd); D[n, g, q[wd] - M, k[wd]] = nd[wd]
    return {"ya": np.ascontiguousarray(A.transpose(0, 1, 3, 2)).reshape(N, 128, E).astype(np.float32).astype(BF),
            "yd": np.ascontiguousarray(D.transpose(0, 1, 3, 2)).reshape(N, 128, F).astype(np.float32),
            "yr": np.ascontiguousarray(R[:, :, F:E].transpose(0, 1, 3, 2)).reshape(N, 128, M).astype(np.float32).astype(BF)}

@@ -1,0 +1,612 @@
+from concourse.bass import DstId, RemoteDMATransfer
+from concourse.mybir import AluOpType, ActivationFunctionType
+
+ALU = AluOpType
+ACT = ActivationFunctionType
+
+H = "float16"
+MAG = 12582912.0
+AOFF = 127.984375
+AB = 1280
+NP = 4
+STAG = False
+NVC = 0
+LCUT = [0, 70, 110, 170, 214, 256]
+TCUT = [0, 52, 104, 128]
+
+f32, bf, i32, u16 = "float32", "bfloat16", "int32", "uint16"
+
+
+def _sb(n, d):
+    return ("sbuf", [128, n], d)
+
+
+SCRATCH = {
+    "avs": _sb(1280, bf), "dpi": _sb(1024, i32), "bdi": _sb(24, i32), "sbi": _sb(88, i32), "thi": _sb(16, i32),
+    "s16a": _sb(88, H), "th16a": _sb(16, H), "wd0": _sb(32, f32), "wd1": _sb(16, f32),
+    "AD": _sb(2944, f32), "W": _sb(1672, f32), "K": _sb(1664, f32), "SR": _sb(1672, f32),
+    "s16": _sb(1408, H), "th16": _sb(256, H), "nf": _sb(1408, f32), "one32": _sb(128, f32),
+    "bdu": _sb(24, u16), "bd2": _sb(24, u16), "du": _sb(1024, u16), "dupo": _sb(288, u16), "adup": _sb(288, bf),
+    "gd": _sb(1536, bf), "sd": _sb(1536, bf), "gm": _sb(4096, bf), "sm": _sb(4096, H),
+    "gt": _sb(2048, bf), "st": _sb(2048, H), "ge": _sb(2048, bf),
+    "rl": _sb(16 * 96, bf), "snd": _sb(16 * 64, bf), "gl": _sb(16 * 96, bf),
+    "J": _sb(128, f32), "JG": _sb(128, f32), "JR": _sb(128, f32), "X1i": _sb(128, f32), "X2i": _sb(128, i32),
+    "pi": _sb(8, i32), "col": _sb(16, f32), "tmp": _sb(128, f32), "tmp2": _sb(128, f32),
+    "BO": _sb(128, H), "BOm": _sb(128, H), "IDh": _sb(128, H), "sel": _sb(128, H), "CU": _sb(256, H),
+    "BOb": _sb(128, bf), "BOn": _sb(128, bf), "BOp": _sb(128, bf), "IDb": _sb(128, bf), "IDn": _sb(128, bf),
+    "P1": _sb(128, bf), "P2": _sb(128, bf), "ia2": _sb(128, bf), "wt": _sb(256, f32), "dum2": _sb(8, f32),
+    "d0t": _sb(1216, bf), "d0p": _sb(768, bf), "d0n": _sb(128, bf), "DD": _sb(128, bf), "DQ": _sb(576, bf),
+    "l15": _sb(8, u16), "lend": _sb(8, u16), "dum": _sb(8, f32),
+    "mt": _sb(128, f32), "wtm": _sb(128, f32), "k2": _sb(128, f32), "tt": _sb(128, f32), "ss": _sb(128, f32),
+    "mT": _sb(128, bf), "mask": _sb(128, bf), "xv": _sb(128, H), "xs": _sb(128, H),
+    "yg": _sb(128, f32), "yp": _sb(128, H), "z": _sb(512, H), "sf": _sb(128, f32), "fl": _sb(8, u16),
+    "md0": _sb(768, bf), "md1": _sb(768, bf), "ms": _sb(768, bf),
+    "r16": _sb(128, bf), "mn": _sb(128, bf), "nm": _sb(128, bf), "nok": _sb(128, bf), "na": _sb(128, bf),
+    "ia": _sb(128, bf), "q": _sb(128, f32), "tf": _sb(256, f32), "tfs": _sb(256, f32), "tw": _sb(8, f32),
+    "tl": _sb(16, u16), "cmp": _sb(576, bf), "cs": _sb(576, bf), "win": _sb(16, f32), "l1": _sb(8, f32),
+    "l2": _sb(8, f32), "ll": _sb(8, u16), "old": _sb(128, f32), "yy": _sb(128, f32),
+    "yab": _sb(1280, bf), "yrb": _sb(256, bf),
+}
+for _b in range(8):
+    SCRATCH["ps%d" % _b] = ("psum", [128, 512], f32)
+
+SEMAPHORES = ["cv", "ca", "cp", "cg", "l_av0", "l_av1", "l_dp", "l_bd", "l_sb", "l_th", "r_sb", "r_th", "sent", "st"] + \
+             ["arr%d" % i for i in range(16)]
+
+
+def rank_program(g, core, T, topo):
+    rank = T.rank_of(core)
+    if rank is None:
+        return
+    Q = {"v": g.vector, "a": g.scalar, "p": g.tensor, "g": g, "s": g.sync}
+    SEM = {"v": "cv", "a": "ca", "p": "cp", "g": "cg"}
+    cnt = {"v": 0, "a": 0, "p": 0, "g": 0}
+    seen = {e: {} for e in Q}
+    tok = {}
+
+    def wait(e, ev):
+        if ev is not None and seen[e].get(ev[0], 0) < ev[1]:
+            Q[e].wait_ge(T.sem[ev[0]], ev[1])
+            seen[e][ev[0]] = ev[1]
+
+    def sync(e, reads, writes):
+        own = SEM.get(e)
+        for r in reads:
+            t = tok.setdefault(r, {"w": None, "r": {}})
+            wait(e, t["w"])
+            if r.startswith("ps"):
+                for s, v in t["r"].items():
+                    if s != own:
+                        wait(e, (s, v))
+        for w in writes:
+            t = tok.setdefault(w, {"w": None, "r": {}})
+            if t["w"] is not None and (e != "p" or t["w"][0] != own):
+                wait(e, t["w"])
+            for s, v in t["r"].items():
+                if e != "p" or s != own:
+                    wait(e, (s, v))
+
+    def mark(ev, reads, writes):
+        for r in reads:
+            tok.setdefault(r, {"w": None, "r": {}})["r"][ev[0]] = ev[1]
+        for w in writes:
+            tok[w] = {"w": ev, "r": {}}
+
+    def op(e, fn, reads, writes):
+        sync(e, reads, writes)
+        ins = fn()
+        cnt[e] += 1
+        ins.then_inc(T.sem[SEM[e]], 1)
+        mark((SEM[e], cnt[e]), reads, writes)
+
+    def mm(bank, out, terms, start=True, stop=True):
+        allr = []
+        for i, (l, r, rd) in enumerate(terms):
+            sync("p", rd, [bank] if i == 0 else [])
+            ins = g.tensor.matmul(out, l, r, start and i == 0, stop and i == len(terms) - 1)
+            allr += rd
+        cnt["p"] += 1
+        ins.then_inc(T.sem.cp, 1)
+        mark(("cp", cnt["p"]), allr, [bank])
+
+    def dma(e, out, in_, sem, reads, writes, val=16):
+        sync(e, reads, writes)
+        Q[e].dma_start(out, in_).then_inc(T.sem[sem], 16)
+        mark((sem, val), reads, writes)
+
+    V = g.vector
+
+    def ts(out, in0, s1, o0, reads, writes, s2=None, o1=None):
+        if o1 is None:
+            op("v", lambda: V.tensor_scalar(out, in0, s1, None, o0), reads, writes)
+        else:
+            op("v", lambda: V.tensor_scalar(out, in0, s1, s2, o0, o1), reads, writes)
+
+    def tt(out, a, b, o, reads, writes):
+        op("v", lambda: V.tensor_tensor(out, a, b, o), reads, writes)
+
+    def cp(out, a, reads, writes):
+        op("v", lambda: V.tensor_copy(out, a), reads, writes)
+
+    def scan(out, d0, d1, o0, o1, reads, writes):
+        op("v", lambda: V.tensor_tensor_scan(out, d0, d1, 0.0, o0, o1), reads, writes)
+
+    def ms(ap, c, writes):
+        op("v", lambda: V.memset(ap, c), [], writes)
+
+    def act(out, in_, func, reads, writes, bias=0.0, scale=1.0):
+        op("a", lambda: g.scalar.activation(out, in_, func, bias=bias, scale=scale), reads, writes)
+
+    def iota(out, pat, base, cm, writes, fl=True):
+        if fl:
+            op("g", lambda: g.iota(out, pat, base, cm, allow_small_or_imprecise_dtypes=True), [], writes)
+        else:
+            op("g", lambda: g.iota(out, pat, base, cm), [], writes)
+
+    ADD, SUB, MUL, MAX, MIN = ALU.add, ALU.subtract, ALU.mult, ALU.max, ALU.min
+    EQ, NE = ALU.is_equal, ALU.not_equal
+    ps = [T["ps%d" % b] for b in range(8)]
+    ADT = ["ADj", "ADd", "ADa0", "ADa", "ADk"]
+    WT = ["W0", "W1", "W2", "W3", "Wg0", "Wg1", "Wg2", "Wg3", "Wx", "Wy", "Wb1", "Wb2", "Wb3"]
+    KT = ["Kx0", "Kx", "K1", "K2", "K3", "Ka1", "Ka2", "Ka3"]
+    SRT = ["SR0", "SR512", "SR1024", "SRa", "SRb"]
+
+    dma("s", T.avs[:, 0:256], T.av[:, 0:256], "l_av0", [], ["av0"])
+    dma("a", T.bdi[:], T.bd[:], "l_bd", [], ["bdi"])
+    dma("s", T.dpi[:], T.dp[:], "l_dp", [], ["dpi"])
+    dma("a", T.avs[:, 256:1280], T.av[:, 256:1280], "l_av1", [], ["av1"])
+    dma("s", T.sbi[:], T.sb[:], "l_sb", [], ["sbi"])
+    dma("s", T.thi[:], T.th[:], "l_th", [], ["thi"])
+
+    def sel(out, in_, pat, cmp_, fill, base, cm, reads, writes):
+        op("g", lambda: g.affine_select(out, in_, pat, cmp_, fill, base, cm), reads, writes)
+
+    iota(T.X1i[:], [[-16, 8], [1, 16]], 112, -1, ["X1i"])
+    iota(T.X2i[:], [[-16, 8], [1, 16]], 128, -1, ["X2i"], fl=False)
+    iota(T.pi[:, 0:1], [[1, 1]], 0, 1, ["pi0"], fl=False)
+    iota(T.J[:], [[1, 128]], 0, 0, ["J"])
+    iota(T.JG[:], [[1, 8], [0, 16]], 0, 0, ["JG"])
+    iota(T.JR[:], [[0, 8], [1, 16]], 0, 0, ["JR"])
+    ms(T.d0p[:], 0.0, ["d0p"])
+    ms(T.d0t[:], -0.0625, ["d0t"])
+    ms(T.d0p[:, 0::16], 8192.0, ["d0p"])
+    ms(T.d0t[:, 0::16], 8192.0, ["d0t"])
+    ts(T.P1[:], T.X1i[:], 0.0, EQ, ["X1i"], ["P1"])
+    ts(T.X2i[:], T.X2i[:], 127, ALU.bitwise_and, ["X2i"], ["X2i"])
+    ts(T.P2[:], T.X2i[:], 0.0, EQ, ["X2i"], ["P2"])
+
+    peers = [T.cores[rank ^ d] for d in (1, 2, 3)]
+
+    def emask(es):
+        m = 0
+        for e in es:
+            m |= 1 << e
+        return m
+
+    def send(x):
+        r0 = 96 * x
+        rid, pid = topo.addr(peers[2], core)
+        sync("g", ["rl%d" % x], [])
+        g.remote_dma(T.gl[:, r0 + 64:r0 + 96], T.rl[:, r0 + 64:r0 + 96], T.sem["arr%d" % x], T.sem.sent,
+                     pid, rid, topo.mask(core, peers[2]))
+        trs = []
+        n = len(topo.engines(core, peers[2]))
+        for d in (1, 2):
+            es = topo.engines(core, peers[d - 1])
+            h = len(es) // 2
+            es = es[:h] if d == 1 else es[h:]
+            n += len(es)
+            rid, pid = topo.addr(peers[d - 1], core)
+            trs.append(RemoteDMATransfer(dst_ids=[DstId(rid=rid, pnc=pid)], dma_engine_mask=emask(es),
+                                         remote_sem=T.sem["arr%d" % x],
+                                         src=T.snd[:, 64 * x + 32 * (d - 1):64 * x + 32 * d],
+                                         dst=T.gl[:, r0 + 32 * (d - 1):r0 + 32 * d]))
+        sync("g", ["snd%d" % x], [])
+        g.remote_dma_fused(trs, local_sem=T.sem.sent)
+        tok["gl%d" % x] = {"w": ("arr%d" % x, n), "r": {}}
+        return n
+
+    def send1(x, d):
+        c0 = 32 * (d - 1)
+        src = T.rl[:, 96 * x + c0:96 * x + c0 + 32] if d == 3 else T.snd[:, 64 * x + c0:64 * x + c0 + 32]
+        rid, pid = topo.addr(peers[d - 1], core)
+        sync("g", [("rl%d_%d" if d == 3 else "snd%d_%d") % (x, d)], [])
+        g.remote_dma(T.gl[:, 96 * x + c0:96 * x + c0 + 32], src, T.sem["arr%d" % x], T.sem.sent,
+                     pid, rid, topo.mask(core, peers[d - 1]))
+        return len(topo.engines(core, peers[d - 1]))
+
+    def perm1(x, d):
+        c0 = 32 * (d - 1)
+        bank = 7 if d == 1 else 6
+        mm("ps%d" % bank, ps[bank][:, 0:32], [(T["P%d" % d][:], T.rl[:, 96 * x + c0:96 * x + c0 + 32],
+                                               ["P%d" % d, "rl%d_%d" % (x, d)])])
+        act(T.snd[:, 64 * x + c0:64 * x + c0 + 32], ps[bank][:, 0:32], ACT.Identity, ["ps%d" % bank], ["snd%d_%d" % (x, d)])
+
+    def perm(x):
+        r0 = 96 * x
+        mm("ps7", ps[7][:, 0:32], [(T.P1[:], T.rl[:, r0:r0 + 32], ["P1", "rl%d" % x])])
+        mm("ps7", ps[7][:, 32:64], [(T.P2[:], T.rl[:, r0 + 32:r0 + 64], ["P2", "rl%d" % x])])
+
+    def evac(x):
+        act(T.snd[:, 64 * x:64 * x + 64], ps[7][:, 0:64], ACT.Identity, ["ps7"], ["snd%d" % x])
+
+    def ghosts(x, l):
+        act(T.W[:, 1280 + 96 * l:1376 + 96 * l], T.gl[:, 96 * x:96 * x + 96], ACT.Identity,
+            ["gl%d" % x], ["Wg%d" % l], bias=MAG)
+
+    def gat(e, out, offs, otok, wtok):
+        src = T.W[:, 0:1672].indirect(offs)
+        if e == "v":
+            ts(out, src, -MAG, ADD, WT + otok, wtok)
+        else:
+            act(out, src, ACT.Identity, WT + otok, wtok, bias=-MAG)
+
+    col = T.col
+    c_pr, c_pg, c_p, c_p16, c_k, c_fix, c_win, c_pr1, c_np16 = [col[:, i:i + 1] for i in range(9)]
+
+    def setup_rest():
+        ts(T.pi[:, 1:2], T.pi[:, 0:1], 15, ALU.bitwise_and, ["pi0"], ["pi1"])
+        ts(T.pi[:, 2:3], T.pi[:, 0:1], 4, ALU.arith_shift_right, ["pi0"], ["pi2"])
+        cp(c_p, T.pi[:, 0:1], ["pi0"], ["c_p"])
+        cp(col[:, 0:2], T.pi[:, 1:3], ["pi1", "pi2"], ["c_r"])
+        ts(c_p16, c_pr, 0.0625, MUL, ["c_r"], ["c_p16"])
+        ts(c_np16, c_pr, -0.0625, MUL, ["c_r"], ["c_np16"])
+        ts(c_k, c_pr, -15.0, ADD, ["c_r"], ["c_k"], 0.0625, MUL)
+        ts(c_fix, c_pr, 15.0, ALU.is_lt, ["c_r"], ["c_fix"], 8192.0, MUL)
+        ts(c_win, c_pr, -15.0, ADD, ["c_r"], ["c_win"], 1.0 / 128, MUL)
+        ts(c_pr1, c_pr, 1.0, ADD, ["c_r"], ["c_pr1"])
+        ts(col[:, 9:10], c_pr, 7.0, MIN, ["c_r"], ["c9"], 1.0, ADD)
+        ts(col[:, 10:11], col[:, 9:10], 1.0, ADD, ["c9"], ["c10"], 8.0, MUL)
+        tt(col[:, 11:12], col[:, 9:10], col[:, 10:11], MUL, ["c9", "c10"], ["c11"])
+        ts(T.lend[:, 0:1], col[:, 11:12], -1.0, ADD, ["c11"], ["lend"])
+        ts(T.BO[:], T.JG[:], c_pg, EQ, ["JG", "c_r"], ["BO"])
+        ts(T.BOm[:], T.JG[:], c_pg, EQ, ["JG", "c_r"], ["BOm"], -1.0, MUL)
+        ts(T.BOp[:], T.JG[:], c_pg, EQ, ["JG", "c_r", "c_np16"], ["BOp"], c_np16, MUL)
+        ts(T.IDh[:], T.J[:], c_p, EQ, ["J", "c_p"], ["IDh"])
+        ts(T.sel[:], T.JG[:], c_p, EQ, ["JG", "c_p"], ["sel"])
+        ts(T.CU[:, 0:128], T.J[:], 2.0, MUL, ["J"], ["CU0"], -1024.0, ADD)
+        ts(T.CU[:, 128:256], T.J[:], 2.0, MUL, ["J"], ["CU1"], -1023.0, ADD)
+        cp(T.l15[:], T.J[:, 15::16], ["J"], ["l15"])
+        ts(T.dum[:], T.J[:, 0::16], c_pr, ADD, ["J", "c_r"], ["dum"])
+        ts(T.tmp[:], T.JR[:], c_pr, EQ, ["JR", "c_r"], ["tmp"], 16384.0, MUL)
+        ts(T.tmp2[:], T.JR[:], c_pr1, EQ, ["JR", "c_pr1"], ["tmp2"], -8192.0, MUL)
+        cp(T.wd1[:, 1::2], T.dum[:], ["dum"], ["wd1c"])
+        ts(T.dum2[:], T.dum[:], -3328.0, ADD, ["dum"], ["dum2"])
+        tt(T.DD[:], T.tmp[:], T.tmp2[:], ADD, ["tmp", "tmp2"], ["DD"])
+
+    def setup_g(part):
+        if part == 0:
+            iota(T.nf[0:1, 0:1024], [[-1, 1024]], 0, 0, ["nf0"])
+            iota(T.nf[0:1, 1024:1408], [[-1, 384]], -1280, 0, ["nf1"])
+        if part == 1:
+            iota(T.K[:, 0:256], [[0, 256]], 1000, 0, ["Kx0"])
+            iota(T.K[:, 1024:1664], [[0, 640]], 1000, 0, ["Kx"])
+            for nme, c in (("IDb", 1), ("IDn", -1)):
+                iota(T[nme][:], [[0, 128]], c, 0, [nme])
+                sel(T[nme][:], T[nme][:], [[-1, 128]], EQ, 0.0, 0, 1, [nme], [nme])
+        if part == 2:
+            iota(T.AD[:, 0:256], [[0, 256]], 0, 0, ["ADj"])
+            iota(T.AD[:, AB + 1280:2944], [[0, 384]], 0, 0, ["ADk"])
+            iota(T.SR[:, 1024:1280], [[0, 256]], 1, 0, ["SRa"])
+            iota(T.SR[:, 1664:1672], [[0, 8]], 1, 0, ["SRb"])
+            iota(T.one32[0:1, :], [[0, 128]], 1, 0, ["one32"])
+            iota(T.d0n[:], [[0, 128]], -8192, 0, ["d0n"])
+            sel(T.d0n[:], T.d0n[:], [[0, 8], [1, 16]], EQ, 0.0, 0, 0, ["d0n"], ["d0n"])
+            iota(T.md0[:, 0::6], [[0, 128]], 0, 0, ["md0c"])
+            iota(T.md0[:, 5::6], [[0, 128]], -1, 0, ["md0d"])
+            iota(T.wd0[:, 0::2], [[0, 16]], 0, 0, ["wd0c"])
+        if part == 3:
+            for nme, c in (("BOb", 1), ("BOn", -2048)):
+                iota(T[nme][:], [[0, 128]], c, 0, [nme])
+                sel(T[nme][:], T[nme][:], [[-16, 8], [0, 16]], ALU.is_ge, 0.0, 0, 1, [nme], [nme])
+                sel(T[nme][:], T[nme][:], [[16, 8], [0, 16]], ALU.is_ge, 0.0, 15, -1, [nme], [nme])
+            iota(T.DQ[:], [[0, 576]], 8192, 0, ["DQ"])
+            for a in range(8):
+                o, n = 8 * a * (a + 1), 16 * (a + 1)
+                sel(T.DQ[:, o:o + n], T.DQ[:, o:o + n], [[1, n]], EQ, -1.0 / 128, 0, 0, ["DQ"], ["DQ%d" % a])
+
+    mt, k2, yp = ps[4][:, 0:128], ps[4][:, 128:256], ps[4][:, 256:384]
+    DQT = ["DQ%d" % a for a in range(8)]
+    sent = [0]
+
+    def negv():
+        return [(T.BOm[:], T.xv[:], ["BOm", "xv"]), (T.BOp[:], T.mask[:], ["BOp", "mask"])]
+
+    for t in range(NP):
+        par = t & 1
+        x = 4 * t
+        last = t == NP - 1
+        if t == 0:
+            cp(T.bdu[:], T.bdi[:], ["bdi"], ["bdu"])
+            ts(T.rl[:, 0:96], T.avs[:, 0:256].indirect(T.bdu[:, 0:6]), -127.0, ADD, ["av0", "bdu"], ["rl0"])
+        else:
+            ts(T.rl[:, 96 * x:96 * x + 96], T.AD[:, AB:AB + 256].indirect(T.bdu[:, 0:6]), 0.984375, ADD,
+               ["ADa0", "bdu"], ["rl%d" % x])
+        perm(x)
+        evac(x)
+        sent[0] += send(x)
+        if t == 0:
+            setup_g(0)
+            for l in range(3):
+                ts(T.bd2[:, 6 * l:6 * l + 6], T.bdi[:, 6 * l + 6:6 * l + 12], float(256 * l), ADD, ["bdi"], ["bd2%d" % l])
+            ts(T.W[:, 0:256], T.avs[:, 0:256], MAG - 127.0, ADD, ["av0"], ["W0"])
+            BD2 = ["bd20", "bd21", "bd22"]
+            setup_rest()
+            cp(T.dupo[:], T.dpi[:, 0:768].indirect(T.bd2[:, 0:18]), ["dpi"] + BD2, ["dupo"])
+            act(T.adup[:], T.avs[:, 256:1024].indirect(T.bd2[:, 0:18]), ACT.Identity, ["av1"] + BD2, ["adup"], bias=-127.0)
+            act(T.W[:, 256:1280], T.avs[:, 256:1280], ACT.Identity, ["av1"], ["W1", "W2", "W3", "Wx", "Wb1", "Wb2", "Wb3"],
+                bias=MAG + 128.0, scale=0.0)
+            act(T.W[:, 1376:1672], T.avs[:, 256:552], ACT.Identity, ["av1"], ["Wg1", "Wg2", "Wg3", "Wy"],
+                bias=MAG + 128.0, scale=0.0)
+            act(ps[1][:], T.avs[:, 256:768], ACT.Identity, ["av1"], ["ps1"], bias=-AOFF)
+            act(ps[2][:, 0:256], T.avs[:, 768:1024], ACT.Identity, ["av1"], ["ps2"], bias=-AOFF)
+            act(ps[2][:, 256:384], T.avs[:, 1024::2], ACT.Identity, ["av1"], ["ps2"], bias=-AOFF)
+            act(T.AD[:, AB:AB + 1280], T.avs[:], ACT.Identity, ["av0", "av1"], ["ADa0", "ADa"], bias=-AOFF)
+            cp(T.du[:, 0:768], T.dpi[:, 0:768], ["dpi"], ["du"])
+            cp(T.du[:, 768:896], T.dpi[:, 768::2], ["dpi"], ["dut"])
+            ts(T.th16a[:], T.thi[:], -127.0, ADD, ["thi"], ["th16a"])
+            cp(T.s16a[:], T.sbi[:], ["sbi"], ["s16a"])
+            dma("s", T.th16[0:8, :], T.th16a[:], "r_th", ["th16a"], ["th16"])
+            dma("s", T.s16[0:8, :], T.s16a[:], "r_sb", ["s16a"], ["s16"])
+            cp(T.AD[:, 256:1280], T.dpi[:], ["dpi"], ["ADd"])
+        else:
+            cp(T.dupo[:], T.AD[:, 256:1024].indirect(T.bd2[:, 0:18]), ["ADd"] + BD2, ["dupo"])
+            act(T.adup[:], T.AD[:, AB + 256:AB + 1024].indirect(T.bd2[:, 0:18]), ACT.Identity, ["ADa"] + BD2,
+                ["adup"], bias=0.984375)
+            act(ps[1][:], T.AD[:, AB + 256:AB + 768], ACT.Identity, ["ADa"], ["ps1"])
+            act(ps[2][:, 0:256], T.AD[:, AB + 768:AB + 1024], ACT.Identity, ["ADa"], ["ps2"])
+            act(ps[2][:, 256:384], T.AD[:, AB + 1024 + par:AB + 1280:2], ACT.Identity, ["ADa"], ["ps2"])
+            ts(T.W[:, 0:256], T.AD[:, AB:AB + 256], 0.984375, ADD, ["ADa0"], ["W0"], MAG, ADD)
+            cp(T.du[:, 0:768], T.AD[:, 256:1024], ["ADd"], ["du"])
+            cp(T.du[:, 768:896], T.AD[:, 1024 + par:1280:2], ["ADd"], ["dut"])
+            if last:
+                cp(T.du[:, 896:1024], T.AD[:, 1025 - par:1280:2], ["ADd"], ["duo"])
+        CUp = T.CU[:, 128 * par:128 * par + 128]
+        CUt = "CU%d" % par
+
+        def first_links(part):
+            if part == 0:
+                mm("ps3", ps[3][:, 0:128], [(T.IDh[:], CUp, ["IDh", CUt])])
+                act(T.yg[:], T.AD[:, 1024 + par:1280:2], ACT.Identity, ["ADd"], ["yg"], bias=-2048.0)
+            else:
+                tt(yp, T.yg[:], ps[3][:, 0:128], SUB, ["yg", "ps3"], ["yp"])
+
+        if t > 0:
+            first_links(0)
+            first_links(1)
+        ghosts(x, 0)
+
+        for l in (1, 2, 3):
+            xl = x + l
+            o = 96 * (l - 1)
+            cuts = LCUT
+            b = 256 * (l - 1)
+
+            def gm(e, i):
+                gat(e, T.gm[:, 16 * cuts[i]:16 * cuts[i + 1]], T.du[:, b + cuts[i]:b + cuts[i + 1]], ["du"], ["gm%d" % i])
+
+            def sm(i):
+                n = 16 * (cuts[i + 1] - cuts[i])
+                scan(T.sm[:, 16 * cuts[i]:16 * cuts[i + 1]], T.d0t[:, 0:n], T.gm[:, 16 * cuts[i]:16 * cuts[i + 1]],
+                     ADD, MIN, ["d0t", "gm%d" % i], ["sm%d" % i])
+
+            def mn(c0, c1, rd, wr):
+                ab, ao = (1, 256 * (l - 1)) if l < 3 else (2, 0)
+                tt(T.K[:, 256 * l + c0:256 * l + c1], T.sm[:, 16 * c0 + 15:16 * c1:16],
+                   ps[ab][:, ao + c0:ao + c1], MIN, rd + ["ps%d" % ab], wr)
+
+            if STAG:
+                def rel(d):
+                    c0 = 32 * (d - 1)
+                    scan(T.sd[:, 16 * c0:16 * c0 + 512], T.d0p[:, 0:512], T.gd[:, 16 * c0:16 * c0 + 512], ADD, MIN,
+                         ["d0p", "gd%d" % d], ["sd%d" % d])
+                    tt(T.rl[:, 96 * xl + c0:96 * xl + c0 + 32], T.sd[:, 16 * c0 + 15:16 * c0 + 512:16],
+                       T.adup[:, o + c0:o + c0 + 32], MIN, ["sd%d" % d, "adup"], ["rl%d_%d" % (xl, d)])
+
+                for e, d in (("v", 3), ("a", 1), ("a", 2)):
+                    c0 = 32 * (d - 1)
+                    gat(e, T.gd[:, 16 * c0:16 * c0 + 512], T.dupo[:, o + c0:o + c0 + 32], ["dupo"], ["gd%d" % d])
+                rel(3)
+                n = send1(xl, 3)
+                rel(1)
+                perm1(xl, 1)
+                n += send1(xl, 1)
+                gm("a", 1)
+                rel(2)
+                perm1(xl, 2)
+                n += send1(xl, 2)
+                tok["gl%d" % xl] = {"w": ("arr%d" % xl, n), "r": {}}
+                sent[0] += n
+            else:
+                gat("v", T.gd[:, 0:768], T.dupo[:, o:o + 48], ["dupo"], ["gd0"])
+                gat("a", T.gd[:, 768:1536], T.dupo[:, o + 48:o + 96], ["dupo"], ["gd1"])
+                gm("a", 1)
+                scan(T.sd[:, 0:768], T.d0p[:, 0:768], T.gd[:, 0:768], ADD, MIN, ["d0p", "gd0"], ["sd0"])
+                scan(T.sd[:, 768:1536], T.d0p[:, 0:768], T.gd[:, 768:1536], ADD, MIN, ["d0p", "gd1"], ["sd1"])
+                tt(T.rl[:, 96 * xl:96 * xl + 96], T.sd[:, 15::16], T.adup[:, o:o + 96], MIN,
+                   ["sd0", "sd1", "adup"], ["rl%d" % xl])
+                perm(xl)
+                evac(xl)
+                sent[0] += send(xl)
+            if t == 0:
+                setup_g(l)
+            gm("a", 2)
+            gm("a", 3)
+            gm("a", 4)
+            gm("v", 0)
+            sm(0)
+            sm(1)
+            sm(2)
+            sm(3)
+            c4 = cuts[4]
+            mn(0, c4, ["sm0", "sm1", "sm2", "sm3"], ["Ka%d" % l])
+            ts(T.wt[:, 0:c4], T.K[:, 256 * l:256 * l + c4], 0.4921875, ADD, ["Ka%d" % l], ["wt"], MAG, ADD)
+            act(T.W[:, 256 * l:256 * l + c4], T.wt[:, 0:c4], ACT.Identity, ["wt"], ["W%d" % l])
+            ghosts(xl, l)
+            if t == 0 and l < 3:
+                first_links(l - 1)
+            sm(4)
+            mn(c4, 256, ["sm4"], ["K%d" % l])
+            ts(T.W[:, 256 * l + c4:256 * l + 256], T.K[:, 256 * l + c4:256 * l + 256], 0.4921875, ADD,
+               ["K%d" % l], ["Wb%d" % l], MAG, ADD)
+
+        cuts = TCUT
+        for e, i in (("v", 0), ("a", 1), ("a", 2)):
+            gat(e, T.gt[:, 16 * cuts[i]:16 * cuts[i + 1]], T.du[:, 768 + cuts[i]:768 + cuts[i + 1]], ["dut"],
+                ["gt%d" % i])
+        for i in range(3):
+            n = 16 * (cuts[i + 1] - cuts[i])
+            scan(T.st[:, 16 * cuts[i]:16 * cuts[i + 1]], T.d0t[:, 0:n], T.gt[:, 16 * cuts[i]:16 * cuts[i + 1]],
+                 ADD, MIN, ["d0t", "gt%d" % i], ["st%d" % i])
+        spare = []
+        if t == 0:
+            def sr_part(c0, n, dst, nft):
+                def run():
+                    mm("ps7", ps[7][:, 0:n], [(T.sel[0:8, :], T.s16[0:8, c0:c0 + n], ["sel", "s16"]),
+                                              (T.one32[0:1, :], T.nf[0:1, c0:c0 + n], ["one32", nft])])
+                    act(T.SR[:, dst:dst + n], ps[7][:, 0:n], ACT.Identity, ["ps7"], ["SR%d" % c0])
+                return run
+            spare = [sr_part(0, 512, 0, "nf0"), sr_part(512, 512, 512, "nf0"), sr_part(1024, 384, 1280, "nf1")]
+        if last:
+            def ex_part(i):
+                def run():
+                    gat("a", T.ge[:, 512 * i:512 + 512 * i], T.du[:, 896 + 32 * i:928 + 32 * i], ["duo"], ["ge%d" % i])
+                return run
+            spare = [ex_part(i) for i in range(4)]
+
+        def gap():
+            if spare:
+                spare.pop(0)()
+
+        gap()
+        gap()
+        if t == 0:
+            gap()
+        tt(mt, T.st[:, 15::16], ps[2][:, 256:384], MIN, ["st0", "st1", "st2", "ps2"], ["mt"])
+        ts(T.wtm[:], mt, 0.4921875, ADD, ["mt"], ["wtm"], MAG, ADD)
+        ts(k2, T.wtm[:], MAG, SUB, ["wtm", "c_p16"], ["k2"], c_p16, SUB)
+        op("v", lambda: V.transpose(T.tt[:], k2), ["k2"], ["tt"])
+        scan(T.ss[:], T.d0n[:], T.tt[:], ADD, MAX, ["d0n", "tt"], ["ss"])
+        tt(T.mT[:], T.ss[:, 0:128].indirect(T.l15[:, 0:8]), T.tt[:], EQ, ["ss", "l15", "tt"], ["mT"])
+        op("v", lambda: V.transpose(T.mask[:], T.mT[:]), ["mT"], ["mask"])
+        tt(T.xv[:], k2, T.mask[:], MUL, ["k2", "mask"], ["xv"])
+        tt(T.xs[:], mt, T.mask[:], MUL, ["mt", "mask"], ["xs"])
+
+        CUm = (T.IDh[:], CUp, ["IDh", CUt])
+        thm = (T.sel[0:8, :], T.th16[0:8, par::2], ["sel", "th16"])
+        IA = (T.IDb[:], T.ia2[:], ["IDb", "ia2"])
+        NM = (T.IDb[:], T.nm[:], ["IDb", "nm"])
+
+        def E(s):
+            return T.md1[:, s - 1::6]
+
+        def Zm(s):
+            return (T.BO[:], T.z[:, 128 * (s - 1):128 * s], ["BO", "z%d" % s])
+
+        def ym(s):
+            return [CUm, IA] + [Zm(j) for j in range(1, s)]
+
+        def En(s):
+            return (T.BOn[:], E(s), ["BOn", "E%d" % s])
+
+        for s in (1, 2, 3, 4):
+            fb = 1 + (s + 1) % 2
+            pb = 1 + s % 2
+            if s > 1:
+                tt(T.xs[:], T.K[:, 0:1664].indirect(T.fl[:, 0:8]), T.mask[:], MUL, KT + ["fl", "mask"], ["xs"])
+                act(T.yg[:], T.AD[:, 0:1664].indirect(T.fl[:, 0:8]), ACT.Identity, ADT[0:4] + ["fl"], ["yg"], bias=-2048.0)
+            else:
+                mm("ps0", ps[0][:, 0:128], negv(), stop=False)
+            mm("ps0", ps[0][:, 0:128], [(T.BO[:], T.xs[:], ["BO", "xs"])], start=False)
+            if s == 1:
+                mm("ps5", ps[5][:, 0:128], [thm] + negv())
+                mm("ps5", ps[5][:, 128:256], negv())
+                mm("ps1", ps[1][:, 0:128], [CUm], stop=False)
+                act(T.r16[:], ps[5][:, 0:128], ACT.Relu, ["ps5"], ["r16"], scale=16.0)
+                act(T.md0[:, 4::6], T.r16[:], ACT.Sign, ["r16"], ["md04"])
+                act(T.mn[:], ps[5][:, 128:256], ACT.Relu, ["ps5"], ["mn"], bias=-111.0)
+                act(T.nm[:], T.mask[:], ACT.Identity, ["mask"], ["nm"], bias=-512.0, scale=512.0)
+            if s == 2:
+                mm("ps6", ps[6][:, 0:128], [(T.BOb[:], E(1), ["BOb", "E1"]), (T.IDb[:], T.md0[:, 4::6], ["IDb", "md04"])])
+                act(T.na[:], ps[6][:, 0:128], ACT.Relu, ["ps6"], ["na"], bias=-1.0)
+                act(T.ia2[:], T.na[:], ACT.Identity, ["na"], ["ia2"], bias=4096.0, scale=-3328.0)
+                mm("ps7", ps[7][:, 0:128], [thm] + negv() + [En(1), NM])
+                act(T.md1[:, 4::6], ps[7][:, 0:128], ACT.Relu, ["ps7"], ["md14"])
+            if s == 3:
+                mm("ps6", ps[6][:, 0:128], [CUm, En(1), IA])
+                act(T.q[:], ps[6][:, 0:128], ACT.Identity, ["ps6"], ["q"])
+                mm("ps3", ps[3][:, 0:128], [En(2)] + ym(2))
+                act(T.md1[:, 5::6], ps[7][:, 0:128], ACT.Relu, ["ps7"], ["md15"], bias=16.0)
+            if s == 4:
+                mm("ps6", ps[6][:, 0:128], ym(4), stop=False)
+                act(T.ia[:], T.na[:], ACT.Identity, ["na"], ["ia"], bias=-384.0, scale=-1664.0)
+            if s > 1:
+                tt(yp, T.yg[:], ps[pb][:, 0:128], SUB, ["yg", "ps%d" % pb], ["yp"])
+            ts(E(s), ps[0][:, 0:128], c_k, EQ, ["ps0", "c_k"], ["E%d" % s])
+            if s == 4:
+                mm("ps6", ps[6][:, 0:128], [En(4)], start=False)
+            tt(T.z[:, 128 * (s - 1):128 * s], E(s), yp, MUL, ["E%d" % s, "yp"], ["z%d" % s])
+            mm("ps%d" % fb, ps[fb][:, 0:128], [Zm(s)], start=False)
+            if s > 1:
+                mm("ps5", ps[5][:, 0:128], [(T.BOb[:], E(s), ["BOb", "E%d" % s])])
+                act(T.md0[:, s - 1::6], ps[5][:, 0:128], ACT.Identity, ["ps5"], ["md0%d" % (s - 1)], bias=1.0, scale=-1.0)
+            if s == 1 and last:
+                ts(T.yrb[:, par::2], T.wtm[:], 127.0 - MAG, ADD, ["wtm"], ["yr0"])
+            if s >= 3:
+                tt(T.q[:], T.q[:], ps[3][:, 0:128], MIN, ["q", "ps3"], ["q"])
+            if s == 4:
+                tt(T.q[:], T.q[:], ps[6][:, 0:128], MIN, ["q", "ps6"], ["q"])
+            if s < 4:
+                mm("ps0", ps[0][:, 0:128], negv(), stop=False)
+                mm("ps%d" % pb, ps[pb][:, 0:128], [CUm] + [Zm(j) for j in range(1, s + 1)], stop=False)
+                if s == 2:
+                    mm("ps7", ps[7][:, 0:128], [(T.IDn[:], T.mn[:], ["IDn", "mn"]), (T.IDn[:], T.r16[:], ["IDn", "r16"]), NM])
+                if s == 3:
+                    mm("ps3", ps[3][:, 0:128], ym(3) + [En(3)])
+                scan(T.sf[:], T.DD[:, 0:128], ps[fb][:, 0:128], ADD, MIN, ["DD", "ps%d" % fb], ["sf"])
+                ts(T.fl[:], T.sf[:, 15::16], c_fix, ADD, ["sf", "c_fix"], ["fl"], 2048.0, ADD)
+
+        tt(T.tf[:, 0:128], T.q[:], ps[2][:, 0:128], MIN, ["q", "ps2"], ["tf0"])
+        scan(T.tfs[:, 0:128], T.DD[:], T.tf[:, 0:128], ADD, MIN, ["DD", "tf0"], ["tfs"])
+        tt(T.tf[:, 128:256], T.ia[:], ps[2][:, 0:128], MAX, ["ia", "ps2"], ["tf1"])
+        ts(T.tw[:], T.tfs[:, 15:128:16], c_fix, ADD, ["tfs", "c_fix"], ["tw"])
+        for a in range(NVC, 8):
+            o, n = 8 * a * (a + 1), 16 * (a + 1)
+            op("a", lambda: g.scalar.activation(T.cmp[:, o:o + n], T.tf[:, 0:n], ACT.Abs, bias=T.tw[:, a:a + 1], scale=-1.0),
+               ["tf0", "tw"], ["cmp%d" % a])
+        ts(T.tl[:, 0:8], T.tfs[:, 15:128:16], c_fix, ADD, ["tfs", "c_fix"], ["tl"], 3328.0, ADD)
+        scan(T.tfs[:, 128:256], T.DD[:], T.tf[:, 128:256], ADD, MIN, ["DD", "tf1"], ["tfs2"])
+        tt(T.wd1[:, 0::2], T.tw[:], T.dum2[:], SUB, ["tw", "dum2"], ["wd1"])
+        ts(T.tl[:, 8:16], T.tfs[:, 143::16], c_fix, ADD, ["tfs2", "c_fix"], ["tl2"], 2048.0, ADD)
+        act(T.old[:], T.AD[:, 0:2944].indirect(T.tl[:, 0:8]), ACT.Identity, ADT + ["tl"], ["old"])
+        gap()
+        gap()
+        for a in range(NVC):
+            o, n = 8 * a * (a + 1), 16 * (a + 1)
+            ts(T.cmp[:, o:o + n], T.tf[:, 0:n], T.tw[:, a:a + 1], NE, ["tf0", "tw"], ["cmp%d" % a])
+        scan(T.ms[:], T.md0[:], T.md1[:], MUL, ADD,
+             ["md0c", "md0d", "md01", "md02", "md03", "md04", "md14", "md15", "E1", "E2", "E3", "E4"], ["ms"])
+        tt(T.yy[:], T.SR[:, 0:1672].indirect(T.tl[:, 8:16]), T.ms[:, 5::6], MUL, SRT + ["tl2", "ms"], ["yy"])
+        scan(T.cs[:], T.DQ[:], T.cmp[:], ADD, MIN, DQT + ["cmp%d" % a for a in range(8)], ["cs"])
+        ts(T.wd0[:, 1::2], T.cs[:, 0:576].indirect(T.lend[:, 0:1]), c_win, EQ, ["cs", "lend", "c_win"], ["win"])
+        scan(T.win[:], T.wd0[:, 0:16], T.wd1[:], MUL, ADD, ["win", "wd0c", "wd1", "wd1c"], ["l2"])
+        cp(T.ll[:], T.win[:, 1::2], ["l2"], ["ll"])
+        tt(T.AD[:, 0:2944].indirect(T.ll[:, 0:8]), T.old[:], T.yy[:], SUB, ["ll", "old", "yy"] + ADT, ADT)
+
+    dma("s", T.yd[:], T.AD[:, 256:1280], "st", ["ADd"], [], 16)
+    for i in range(2):
+        act(T.yab[:, 640 * i:640 * i + 640], T.AD[:, AB + 640 * i:AB + 640 * i + 640], ACT.Identity, ["ADa0", "ADa"],
+            ["yab%d" % i], bias=AOFF)
+        dma("s", T.ya[:, 640 * i:640 * i + 640], T.yab[:, 640 * i:640 * i + 640], "st", ["yab%d" % i], [], 32 + 16 * i)
+    for i in range(2):
+        scan(T.sm[:, 1024 * i:1024 * i + 1024], T.d0t[:, 0:1024], T.ge[:, 1024 * i:1024 + 1024 * i], ADD, MIN,
+             ["d0t", "ge%d" % (2 * i), "ge%d" % (2 * i + 1)], ["se%d" % i])
+    opar = 1 - ((NP - 1) & 1)
+    tt(mt, T.sm[:, 15:2048:16], T.AD[:, AB + 1024 + opar:AB + 1280:2], MIN, ["se0", "se1", "ADa"], ["mt"])
+    ts(T.wtm[:], mt, 0.4921875, ADD, ["mt"], ["wtm"], MAG, ADD)
+    ts(T.yrb[:, opar::2], T.wtm[:], 127.0 - MAG, ADD, ["wtm"], ["yr1"])
+    dma("a", T.yr[:], T.yrb[:], "st", ["yr0", "yr1"], [], 64)
+    g.wait_ge(T.sem.sent, sent[0])
+    for e in ("v", "a", "p", "g"):
+        g.wait_ge(T.sem[SEM[e]], cnt[e])
+    g.wait_ge(T.sem.st, 64)

@@ -9,10 +9,11 @@ MAG = 12582912.0
 AOFF = 127.984375
 AB = 1280
 NP = 4
-STAG = False
+STAG = True
+PRE = 12
 NVC = 0
-LCUT = [0, 70, 110, 170, 214, 256]
-TCUT = [0, 52, 104, 128]
+LCUT = [0, 82, 122, 178, 220, 256]
+TCUT = [0, 26, 64, 90, 128]
 
 f32, bf, i32, u16 = "float32", "bfloat16", "int32", "uint16"
 
@@ -34,8 +35,8 @@ SCRATCH = {
     "pi": _sb(8, i32), "col": _sb(16, f32), "tmp": _sb(128, f32), "tmp2": _sb(128, f32),
     "BO": _sb(128, H), "BOm": _sb(128, H), "IDh": _sb(128, H), "sel": _sb(128, H), "CU": _sb(256, H),
     "BOb": _sb(128, bf), "BOn": _sb(128, bf), "BOp": _sb(128, bf), "IDb": _sb(128, bf), "IDn": _sb(128, bf),
-    "P1": _sb(128, bf), "P2": _sb(128, bf), "ia2": _sb(128, bf), "wt": _sb(256, f32), "dum2": _sb(8, f32),
-    "d0t": _sb(1216, bf), "d0p": _sb(768, bf), "d0n": _sb(128, bf), "DD": _sb(128, bf), "DQ": _sb(576, bf),
+    "P1": _sb(128, bf), "P2": _sb(128, bf), "P3": _sb(128, bf), "ia2": _sb(128, bf), "wt": _sb(256, f32), "dum2": _sb(8, f32),
+    "d0t": _sb(1408, bf), "d0p": _sb(768, bf), "d0n": _sb(128, bf), "DD": _sb(128, bf), "DQ": _sb(576, bf),
     "l15": _sb(8, u16), "lend": _sb(8, u16), "dum": _sb(8, f32),
     "mt": _sb(128, f32), "wtm": _sb(128, f32), "k2": _sb(128, f32), "tt": _sb(128, f32), "ss": _sb(128, f32),
     "mT": _sb(128, bf), "mask": _sb(128, bf), "xv": _sb(128, H), "xs": _sb(128, H),
@@ -64,12 +65,28 @@ def rank_program(g, core, T, topo):
     seen = {e: {} for e in Q}
     tok = {}
 
-    def wait(e, ev):
-        if ev is not None and seen[e].get(ev[0], 0) < ev[1]:
-            Q[e].wait_ge(T.sem[ev[0]], ev[1])
-            seen[e][ev[0]] = ev[1]
+    know = {}
 
     def sync(e, reads, writes):
+        need = {}
+
+        def wait(e, ev):
+            if ev is not None and need.get(ev[0], 0) < ev[1]:
+                need[ev[0]] = ev[1]
+
+        collect(e, reads, writes, wait)
+        for s in list(need):
+            if any(know.get((s2, v2), {}).get(s, 0) >= need[s] for s2, v2 in need.items() if s2 != s):
+                need[s] = 0
+        for s, v in need.items():
+            if seen[e].get(s, 0) < v:
+                Q[e].wait_ge(T.sem[s], v)
+                seen[e][s] = v
+                for s2, v2 in know.get((s, v), {}).items():
+                    if seen[e].get(s2, 0) < v2:
+                        seen[e][s2] = v2
+
+    def collect(e, reads, writes, wait):
         own = SEM.get(e)
         for r in reads:
             t = tok.setdefault(r, {"w": None, "r": {}})
@@ -97,6 +114,7 @@ def rank_program(g, core, T, topo):
         ins = fn()
         cnt[e] += 1
         ins.then_inc(T.sem[SEM[e]], 1)
+        know[(SEM[e], cnt[e])] = dict(seen[e])
         mark((SEM[e], cnt[e]), reads, writes)
 
     def mm(bank, out, terms, start=True, stop=True):
@@ -107,6 +125,7 @@ def rank_program(g, core, T, topo):
             allr += rd
         cnt["p"] += 1
         ins.then_inc(T.sem.cp, 1)
+        know[("cp", cnt["p"])] = dict(seen["p"])
         mark(("cp", cnt["p"]), allr, [bank])
 
     def dma(e, out, in_, sem, reads, writes, val=16):
@@ -174,6 +193,8 @@ def rank_program(g, core, T, topo):
     ts(T.P1[:], T.X1i[:], 0.0, EQ, ["X1i"], ["P1"])
     ts(T.X2i[:], T.X2i[:], 127, ALU.bitwise_and, ["X2i"], ["X2i"])
     ts(T.P2[:], T.X2i[:], 0.0, EQ, ["X2i"], ["P2"])
+    iota(T.P3[:], [[0, 128]], 1, 0, ["P3"])
+    sel(T.P3[:], T.P3[:], [[-1, 128]], EQ, 0.0, 0, 1, ["P3"], ["P3"])
 
     peers = [T.cores[rank ^ d] for d in (1, 2, 3)]
 
@@ -185,10 +206,7 @@ def rank_program(g, core, T, topo):
 
     def send(x):
         r0 = 96 * x
-        rid, pid = topo.addr(peers[2], core)
         sync("g", ["rl%d" % x], [])
-        g.remote_dma(T.gl[:, r0 + 64:r0 + 96], T.rl[:, r0 + 64:r0 + 96], T.sem["arr%d" % x], T.sem.sent,
-                     pid, rid, topo.mask(core, peers[2]))
         trs = []
         n = len(topo.engines(core, peers[2]))
         for d in (1, 2):
@@ -199,18 +217,20 @@ def rank_program(g, core, T, topo):
             rid, pid = topo.addr(peers[d - 1], core)
             trs.append(RemoteDMATransfer(dst_ids=[DstId(rid=rid, pnc=pid)], dma_engine_mask=emask(es),
                                          remote_sem=T.sem["arr%d" % x],
-                                         src=T.snd[:, 64 * x + 32 * (d - 1):64 * x + 32 * d],
+                                         src=T.rl[:, r0 + 32 * (d - 1):r0 + 32 * d],
                                          dst=T.gl[:, r0 + 32 * (d - 1):r0 + 32 * d]))
-        sync("g", ["snd%d" % x], [])
         g.remote_dma_fused(trs, local_sem=T.sem.sent)
+        rid, pid = topo.addr(peers[2], core)
+        g.remote_dma(T.gl[:, r0 + 64:r0 + 96], T.rl[:, r0 + 64:r0 + 96], T.sem["arr%d" % x], T.sem.sent,
+                     pid, rid, topo.mask(core, peers[2]))
         tok["gl%d" % x] = {"w": ("arr%d" % x, n), "r": {}}
         return n
 
     def send1(x, d):
         c0 = 32 * (d - 1)
-        src = T.rl[:, 96 * x + c0:96 * x + c0 + 32] if d == 3 else T.snd[:, 64 * x + c0:64 * x + c0 + 32]
+        src = T.rl[:, 96 * x + c0:96 * x + c0 + 32]
         rid, pid = topo.addr(peers[d - 1], core)
-        sync("g", [("rl%d_%d" if d == 3 else "snd%d_%d") % (x, d)], [])
+        sync("g", ["rl%d_%d" % (x, d)], [])
         g.remote_dma(T.gl[:, 96 * x + c0:96 * x + c0 + 32], src, T.sem["arr%d" % x], T.sem.sent,
                      pid, rid, topo.mask(core, peers[d - 1]))
         return len(topo.engines(core, peers[d - 1]))
@@ -231,8 +251,13 @@ def rank_program(g, core, T, topo):
         act(T.snd[:, 64 * x:64 * x + 64], ps[7][:, 0:64], ACT.Identity, ["ps7"], ["snd%d" % x])
 
     def ghosts(x, l):
-        act(T.W[:, 1280 + 96 * l:1376 + 96 * l], T.gl[:, 96 * x:96 * x + 96], ACT.Identity,
-            ["gl%d" % x], ["Wg%d" % l], bias=MAG)
+        act(T.W[:, 1280 + 96 * l:1376 + 96 * l], ps[7][:, 0:96], ACT.Identity, ["ps7"], ["Wg%d" % l], bias=MAG)
+
+    def landed(x):
+        for d in (1, 2, 3):
+            c0 = 32 * (d - 1)
+            mm("ps7", ps[7][:, c0:c0 + 32], [(T["P%d" % d][:], T.gl[:, 96 * x + c0:96 * x + c0 + 32],
+                                              ["P%d" % d, "gl%d" % x])])
 
     def gat(e, out, offs, otok, wtok):
         src = T.W[:, 0:1672].indirect(offs)
@@ -310,7 +335,7 @@ def rank_program(g, core, T, topo):
     sent = [0]
 
     def negv():
-        return [(T.BOm[:], T.xv[:], ["BOm", "xv"]), (T.BOp[:], T.mask[:], ["BOp", "mask"])]
+        return [(T.BOm[:], T.xv[:], ["BOm", "xv", "xv_0"]), (T.BOp[:], T.mask[:], ["BOp", "mask_0", "mask_1"])]
 
     for t in range(NP):
         par = t & 1
@@ -322,8 +347,6 @@ def rank_program(g, core, T, topo):
         else:
             ts(T.rl[:, 96 * x:96 * x + 96], T.AD[:, AB:AB + 256].indirect(T.bdu[:, 0:6]), 0.984375, ADD,
                ["ADa0", "bdu"], ["rl%d" % x])
-        perm(x)
-        evac(x)
         sent[0] += send(x)
         if t == 0:
             setup_g(0)
@@ -367,13 +390,14 @@ def rank_program(g, core, T, topo):
         def first_links(part):
             if part == 0:
                 mm("ps3", ps[3][:, 0:128], [(T.IDh[:], CUp, ["IDh", CUt])])
-                act(T.yg[:], T.AD[:, 1024 + par:1280:2], ACT.Identity, ["ADd"], ["yg"], bias=-2048.0)
+                act(T.yg[:], T.AD[:, 1024 + par:1280:2], ACT.Identity, ["ADd"], ["yg_0", "yg_1"], bias=-2048.0)
             else:
-                tt(yp, T.yg[:], ps[3][:, 0:128], SUB, ["yg", "ps3"], ["yp"])
+                tt(yp, T.yg[:], ps[3][:, 0:128], SUB, ["yg_0", "yg_1", "ps3"], ["yp_0", "yp_1"])
 
         if t > 0:
             first_links(0)
             first_links(1)
+        landed(x)
         ghosts(x, 0)
 
         for l in (1, 2, 3):
@@ -388,7 +412,7 @@ def rank_program(g, core, T, topo):
             def sm(i):
                 n = 16 * (cuts[i + 1] - cuts[i])
                 scan(T.sm[:, 16 * cuts[i]:16 * cuts[i + 1]], T.d0t[:, 0:n], T.gm[:, 16 * cuts[i]:16 * cuts[i + 1]],
-                     ADD, MIN, ["d0t", "gm%d" % i], ["sm%d" % i])
+                     ADD, MIN, ["d0t", "gm%d" % i] + (["gmx", "gmy"] if i == 0 else []), ["sm%d" % i])
 
             def mn(c0, c1, rd, wr):
                 ab, ao = (1, 256 * (l - 1)) if l < 3 else (2, 0)
@@ -396,68 +420,65 @@ def rank_program(g, core, T, topo):
                    ps[ab][:, ao + c0:ao + c1], MIN, rd + ["ps%d" % ab], wr)
 
             if STAG:
-                def rel(d):
+                def rel(d, part):
                     c0 = 32 * (d - 1)
-                    scan(T.sd[:, 16 * c0:16 * c0 + 512], T.d0p[:, 0:512], T.gd[:, 16 * c0:16 * c0 + 512], ADD, MIN,
-                         ["d0p", "gd%d" % d], ["sd%d" % d])
+                    if part == 0:
+                        scan(T.sd[:, 16 * c0:16 * c0 + 512], T.d0p[:, 0:512], T.gd[:, 16 * c0:16 * c0 + 512], ADD, MIN,
+                             ["d0p", "gd%d" % d], ["sd%d" % d])
+                        return
                     tt(T.rl[:, 96 * xl + c0:96 * xl + c0 + 32], T.sd[:, 16 * c0 + 15:16 * c0 + 512:16],
                        T.adup[:, o + c0:o + c0 + 32], MIN, ["sd%d" % d, "adup"], ["rl%d_%d" % (xl, d)])
 
                 for e, d in (("v", 3), ("a", 1), ("a", 2)):
                     c0 = 32 * (d - 1)
                     gat(e, T.gd[:, 16 * c0:16 * c0 + 512], T.dupo[:, o + c0:o + c0 + 32], ["dupo"], ["gd%d" % d])
-                rel(3)
+                gat("v", T.gm[:, 0:8 * PRE], T.du[:, b:b + PRE // 2], ["du"], ["gmx"])
+                rel(3, 0)
+                rel(1, 0)
+                rel(3, 1)
                 n = send1(xl, 3)
-                rel(1)
-                perm1(xl, 1)
+                rel(2, 0)
+                rel(1, 1)
                 n += send1(xl, 1)
                 gm("a", 1)
-                rel(2)
-                perm1(xl, 2)
+                gat("v", T.gm[:, 8 * PRE:16 * PRE], T.du[:, b + PRE // 2:b + PRE], ["du"], ["gmy"])
+                rel(2, 1)
                 n += send1(xl, 2)
                 tok["gl%d" % xl] = {"w": ("arr%d" % xl, n), "r": {}}
                 sent[0] += n
-            else:
-                gat("v", T.gd[:, 0:768], T.dupo[:, o:o + 48], ["dupo"], ["gd0"])
-                gat("a", T.gd[:, 768:1536], T.dupo[:, o + 48:o + 96], ["dupo"], ["gd1"])
-                gm("a", 1)
-                scan(T.sd[:, 0:768], T.d0p[:, 0:768], T.gd[:, 0:768], ADD, MIN, ["d0p", "gd0"], ["sd0"])
-                scan(T.sd[:, 768:1536], T.d0p[:, 0:768], T.gd[:, 768:1536], ADD, MIN, ["d0p", "gd1"], ["sd1"])
-                tt(T.rl[:, 96 * xl:96 * xl + 96], T.sd[:, 15::16], T.adup[:, o:o + 96], MIN,
-                   ["sd0", "sd1", "adup"], ["rl%d" % xl])
-                perm(xl)
-                evac(xl)
-                sent[0] += send(xl)
             if t == 0:
                 setup_g(l)
             gm("a", 2)
             gm("a", 3)
             gm("a", 4)
-            gm("v", 0)
-            sm(0)
+            gat("v", T.gm[:, 16 * PRE:16 * cuts[1]], T.du[:, b + PRE:b + cuts[1]], ["du"], ["gm0"])
             sm(1)
+            sm(0)
             sm(2)
             sm(3)
-            c4 = cuts[4]
-            mn(0, c4, ["sm0", "sm1", "sm2", "sm3"], ["Ka%d" % l])
+            c4 = cuts[3]
+            mn(0, c4, ["sm0", "sm1", "sm2"], ["Ka%d" % l])
+            sm(4)
             ts(T.wt[:, 0:c4], T.K[:, 256 * l:256 * l + c4], 0.4921875, ADD, ["Ka%d" % l], ["wt"], MAG, ADD)
-            act(T.W[:, 256 * l:256 * l + c4], T.wt[:, 0:c4], ACT.Identity, ["wt"], ["W%d" % l])
+            landed(xl)
             ghosts(xl, l)
+            act(T.W[:, 256 * l:256 * l + c4], T.wt[:, 0:c4], ACT.Identity, ["wt"], ["W%d" % l])
             if t == 0 and l < 3:
                 first_links(l - 1)
-            sm(4)
-            mn(c4, 256, ["sm4"], ["K%d" % l])
+            mn(c4, 256, ["sm3", "sm4"], ["K%d" % l])
             ts(T.W[:, 256 * l + c4:256 * l + 256], T.K[:, 256 * l + c4:256 * l + 256], 0.4921875, ADD,
                ["K%d" % l], ["Wb%d" % l], MAG, ADD)
 
         cuts = TCUT
-        for e, i in (("v", 0), ("a", 1), ("a", 2)):
+        for e, i in (("v", 0), ("a", 1), ("v", 2), ("a", 3)):
             gat(e, T.gt[:, 16 * cuts[i]:16 * cuts[i + 1]], T.du[:, 768 + cuts[i]:768 + cuts[i + 1]], ["dut"],
                 ["gt%d" % i])
-        for i in range(3):
+
+        def st(i):
             n = 16 * (cuts[i + 1] - cuts[i])
             scan(T.st[:, 16 * cuts[i]:16 * cuts[i + 1]], T.d0t[:, 0:n], T.gt[:, 16 * cuts[i]:16 * cuts[i + 1]],
                  ADD, MIN, ["d0t", "gt%d" % i], ["st%d" % i])
+
         spare = []
         if t == 0:
             def sr_part(c0, n, dst, nft):
@@ -482,15 +503,30 @@ def rank_program(g, core, T, topo):
         gap()
         if t == 0:
             gap()
-        tt(mt, T.st[:, 15::16], ps[2][:, 256:384], MIN, ["st0", "st1", "st2", "ps2"], ["mt"])
-        ts(T.wtm[:], mt, 0.4921875, ADD, ["mt"], ["wtm"], MAG, ADD)
-        ts(k2, T.wtm[:], MAG, SUB, ["wtm", "c_p16"], ["k2"], c_p16, SUB)
-        op("v", lambda: V.transpose(T.tt[:], k2), ["k2"], ["tt"])
-        scan(T.ss[:], T.d0n[:], T.tt[:], ADD, MAX, ["d0n", "tt"], ["ss"])
-        tt(T.mT[:], T.ss[:, 0:128].indirect(T.l15[:, 0:8]), T.tt[:], EQ, ["ss", "l15", "tt"], ["mT"])
-        op("v", lambda: V.transpose(T.mask[:], T.mT[:]), ["mT"], ["mask"])
-        tt(T.xv[:], k2, T.mask[:], MUL, ["k2", "mask"], ["xv"])
-        tt(T.xs[:], mt, T.mask[:], MUL, ["mt", "mask"], ["xs"])
+        def date(h):
+            a, b = 64 * h, 64 * h + 64
+            mth, k2h, s = ps[4][:, a:b], ps[4][:, 128 + a:128 + b], "_%d" % h
+            return [
+                lambda: tt(mth, T.st[:, 16 * a + 15:16 * b:16], ps[2][:, 256 + a:256 + b], MIN,
+                           ["st%d" % (2 * h), "st%d" % (2 * h + 1), "ps2"], ["mt" + s]),
+                lambda: ts(T.wtm[:, a:b], mth, 0.4921875, ADD, ["mt" + s], ["wtm" + s], MAG, ADD),
+                lambda: ts(k2h, T.wtm[:, a:b], MAG, SUB, ["wtm" + s, "c_p16"], ["k2" + s], c_p16, SUB),
+                lambda: op("v", lambda: V.transpose(T.tt[:, a:b], k2h), ["k2" + s], ["tt" + s]),
+                lambda: scan(T.ss[:, a:b], T.d0n[:, 0:64], T.tt[:, a:b], ADD, MAX, ["d0n", "tt" + s], ["ss" + s]),
+                lambda: tt(T.mT[:, a:b], T.ss[:, a:b].indirect(T.l15[:, 0:4]), T.tt[:, a:b], EQ,
+                           ["ss" + s, "l15", "tt" + s], ["mT" + s]),
+                lambda: op("v", lambda: V.transpose(T.mask[:, a:b], T.mT[:, a:b]), ["mT" + s], ["mask" + s]),
+            ]
+
+        d0, d1 = date(0), date(1)
+        for f in (lambda: st(0), lambda: st(1), lambda: st(2), d0[0], lambda: st(3), d0[1], d1[0], d0[2], d1[1], d0[3],
+                  d1[2], d0[4], d1[3], d0[5], d1[4], d0[6], d1[5]):
+            f()
+        tt(T.xv[:, 0:64], ps[4][:, 128:192], T.mask[:, 0:64], MUL, ["k2_0", "mask_0"], ["xv_0"])
+        d1[6]()
+        tt(T.xs[:, 0:64], ps[4][:, 0:64], T.mask[:, 0:64], MUL, ["mt_0", "mask_0"], ["xs_0"])
+        tt(T.xv[:, 64:128], ps[4][:, 192:256], T.mask[:, 64:128], MUL, ["k2_1", "mask_1"], ["xv"])
+        tt(T.xs[:, 64:128], ps[4][:, 64:128], T.mask[:, 64:128], MUL, ["mt_1", "mask_1"], ["xs"])
 
         CUm = (T.IDh[:], CUp, ["IDh", CUt])
         thm = (T.sel[0:8, :], T.th16[0:8, par::2], ["sel", "th16"])
@@ -509,15 +545,137 @@ def rank_program(g, core, T, topo):
         def En(s):
             return (T.BOn[:], E(s), ["BOn", "E%d" % s])
 
+        BB, FB = (0, 3), (1, 2)
+        XV, XS = ("xv_0", "xv"), ("xs_0", "xs")
+
+        def both(n):
+            return [n + "_0", n + "_1"]
+
+        def Ef(s, m, mt_):
+            return (m, E(s), [mt_] + both("E%d" % s))
+
+        def yf(s):
+            return [CUm, IA] + [(T.BO[:], T.z[:, 128 * (j - 1):128 * j], ["BO"] + both("z%d" % j)) for j in range(1, s)]
+
+        def half(s, h):
+            a, b, x = 64 * h, 64 * h + 64, "_%d" % h
+            pB, pF, tB, tF = ps[BB[h]][:, 0:64], ps[FB[h]][:, 0:64], "ps%d" % BB[h], "ps%d" % FB[h]
+            Eh, yph, lst = T.md1[:, 6 * a + s - 1:6 * b:6], ps[4][:, 256 + a:256 + b], T.fl[:, 4 * h:4 * h + 4]
+
+            def zm(j):
+                return (T.BO[:], T.z[:, 128 * (j - 1) + a:128 * (j - 1) + b], ["BO", "z%d" % j + x])
+
+            def nv():
+                mm(tB, pB, [(T.BOm[:], T.xv[:, a:b], ["BOm", XV[h]]), (T.BOp[:], T.mask[:, a:b], ["BOp", "mask" + x])], stop=False)
+
+            def A():
+                if s > 1:
+                    tt(T.xs[:, a:b], T.K[:, 0:1664].indirect(lst), T.mask[:, a:b], MUL, KT + ["fl" + x, "mask" + x], [XS[h]])
+                    act(T.yg[:, a:b], T.AD[:, 0:1664].indirect(lst), ACT.Identity, ADT[0:4] + ["fl" + x], ["yg" + x],
+                        bias=-2048.0)
+                else:
+                    nv()
+                mm(tB, pB, [(T.BO[:], T.xs[:, a:b], ["BO", XS[h]])], start=False)
+
+            def Y():
+                if s > 1:
+                    tt(yph, T.yg[:, a:b], pF, SUB, ["yg" + x, tF], ["yp" + x])
+                mm(tF, pF, [(T.IDh[:], T.CU[:, 128 * par + a:128 * par + b], ["IDh", CUt])] + [zm(j) for j in range(1, s)],
+                   stop=False)
+
+            def Eq():
+                ts(Eh, pB, c_k, EQ, [tB, "c_k"], ["E%d" % s + x])
+                if s < 4:
+                    nv()
+
+            def Z():
+                tt(T.z[:, 128 * (s - 1) + a:128 * (s - 1) + b], Eh, yph, MUL, ["E%d" % s + x, "yp" + x], ["z%d" % s + x])
+                mm(tF, pF, [zm(s)], start=False)
+
+            def S():
+                scan(T.sf[:, a:b], T.DD[:, 0:64], pF, ADD, MIN, ["DD", tF], ["sf" + x])
+
+            def L():
+                ts(lst, T.sf[:, a + 15:b:16], c_fix, ADD, ["sf" + x, "c_fix"], ["fl" + x], 2048.0, ADD)
+            return A, Y, Eq, Z, S, L
+
+        def nstep(s, c0):
+            mm("ps5", ps[5][:, c0:c0 + 128], [Ef(s, T.BOb[:], "BOb")])
+
+        def nact(s, c0):
+            act(T.md0[:, s - 1::6], ps[5][:, c0:c0 + 128], ACT.Identity, ["ps5"], ["md0%d" % (s - 1)], bias=1.0, scale=-1.0)
+
+        def qmin(bank):
+            tt(T.q[:], T.q[:], ps[bank][:, 0:128], MIN, ["q", "ps%d" % bank], ["q"])
+
         for s in (1, 2, 3, 4):
+            h0, h1 = half(s, 0), half(s, 1)
+            h0[0]()
+            if s == 1:
+                h0[1]()
+            h1[0]()
+            if s == 1:
+                h1[1]()
+                mm("ps5", ps[5][:, 0:128], [thm] + negv())
+                mm("ps5", ps[5][:, 128:256], negv())
+                act(T.r16[:], ps[5][:, 0:128], ACT.Relu, ["ps5"], ["r16"], scale=16.0)
+                act(T.mn[:], ps[5][:, 128:256], ACT.Relu, ["ps5"], ["mn"], bias=-111.0)
+                act(T.md0[:, 4::6], T.r16[:], ACT.Sign, ["r16"], ["md04"])
+                act(T.nm[:], T.mask[:], ACT.Identity, ["mask_0", "mask_1"], ["nm"], bias=-512.0, scale=512.0)
+            else:
+                if s == 2:
+                    act(T.na[:], ps[7][:, 0:128], ACT.Relu, ["ps7"], ["na"], bias=-1.0)
+                    act(T.ia2[:], T.na[:], ACT.Identity, ["na"], ["ia2"], bias=4096.0, scale=-3328.0)
+                if s == 3:
+                    act(T.q[:], ps[7][:, 0:128], ACT.Identity, ["ps7"], ["q"])
+                    act(T.md1[:, 4::6], ps[5][:, 0:128], ACT.Relu, ["ps5"], ["md14"])
+                if s == 4:
+                    act(T.md1[:, 5::6], ps[7][:, 0:128], ACT.Relu, ["ps7"], ["md15"], bias=16.0)
+                    act(T.ia[:], T.na[:], ACT.Identity, ["na"], ["ia"], bias=-384.0, scale=-1664.0)
+                    nact(2, 0)
+                    nact(3, 128)
+                h0[1]()
+                h1[1]()
+            h0[2]()
+            h1[2]()
+            if s == 4:
+                mm("ps7", ps[7][:, 0:128], yf(4) + [Ef(4, T.BOn[:], "BOn")])
+            h0[3]()
+            h1[3]()
+            if s == 1:
+                mm("ps7", ps[7][:, 0:128], [Ef(1, T.BOb[:], "BOb"), (T.IDb[:], T.md0[:, 4::6], ["IDb", "md04"])])
+                if last:
+                    ts(T.yrb[:, par::2], T.wtm[:], 127.0 - MAG, ADD, ["wtm_0", "wtm_1"], ["yr0"])
+            if s == 2:
+                mm("ps5", ps[5][:, 0:128], [thm] + negv() + [Ef(1, T.BOn[:], "BOn"), NM])
+                mm("ps7", ps[7][:, 0:128], [CUm, Ef(1, T.BOn[:], "BOn"), IA])
+                mm("ps6", ps[6][:, 0:128], [Ef(2, T.BOn[:], "BOn")] + yf(2))
+            if s == 3:
+                qmin(6)
+                mm("ps7", ps[7][:, 0:128], [(T.IDn[:], T.mn[:], ["IDn", "mn"]), (T.IDn[:], T.r16[:], ["IDn", "r16"]), NM])
+                mm("ps6", ps[6][:, 0:128], yf(3) + [Ef(3, T.BOn[:], "BOn")])
+                nstep(2, 0)
+                nstep(3, 128)
+            if s == 4:
+                nstep(4, 0)
+                nact(4, 0)
+                qmin(6)
+                qmin(7)
+            else:
+                h0[4]()
+                h1[4]()
+                h0[5]()
+                h1[5]()
+
+        for s in ():
             fb = 1 + (s + 1) % 2
             pb = 1 + s % 2
             if s > 1:
-                tt(T.xs[:], T.K[:, 0:1664].indirect(T.fl[:, 0:8]), T.mask[:], MUL, KT + ["fl", "mask"], ["xs"])
+                tt(T.xs[:], T.K[:, 0:1664].indirect(T.fl[:, 0:8]), T.mask[:], MUL, KT + ["fl", "mask_0", "mask_1"], ["xs", "xs_0"])
                 act(T.yg[:], T.AD[:, 0:1664].indirect(T.fl[:, 0:8]), ACT.Identity, ADT[0:4] + ["fl"], ["yg"], bias=-2048.0)
             else:
                 mm("ps0", ps[0][:, 0:128], negv(), stop=False)
-            mm("ps0", ps[0][:, 0:128], [(T.BO[:], T.xs[:], ["BO", "xs"])], start=False)
+            mm("ps0", ps[0][:, 0:128], [(T.BO[:], T.xs[:], ["BO", "xs", "xs_0"])], start=False)
             if s == 1:
                 mm("ps5", ps[5][:, 0:128], [thm] + negv())
                 mm("ps5", ps[5][:, 128:256], negv())
@@ -525,7 +683,7 @@ def rank_program(g, core, T, topo):
                 act(T.r16[:], ps[5][:, 0:128], ACT.Relu, ["ps5"], ["r16"], scale=16.0)
                 act(T.md0[:, 4::6], T.r16[:], ACT.Sign, ["r16"], ["md04"])
                 act(T.mn[:], ps[5][:, 128:256], ACT.Relu, ["ps5"], ["mn"], bias=-111.0)
-                act(T.nm[:], T.mask[:], ACT.Identity, ["mask"], ["nm"], bias=-512.0, scale=512.0)
+                act(T.nm[:], T.mask[:], ACT.Identity, ["mask_0", "mask_1"], ["nm"], bias=-512.0, scale=512.0)
             if s == 2:
                 mm("ps6", ps[6][:, 0:128], [(T.BOb[:], E(1), ["BOb", "E1"]), (T.IDb[:], T.md0[:, 4::6], ["IDb", "md04"])])
                 act(T.na[:], ps[6][:, 0:128], ACT.Relu, ["ps6"], ["na"], bias=-1.0)
@@ -551,7 +709,7 @@ def rank_program(g, core, T, topo):
                 mm("ps5", ps[5][:, 0:128], [(T.BOb[:], E(s), ["BOb", "E%d" % s])])
                 act(T.md0[:, s - 1::6], ps[5][:, 0:128], ACT.Identity, ["ps5"], ["md0%d" % (s - 1)], bias=1.0, scale=-1.0)
             if s == 1 and last:
-                ts(T.yrb[:, par::2], T.wtm[:], 127.0 - MAG, ADD, ["wtm"], ["yr0"])
+                ts(T.yrb[:, par::2], T.wtm[:], 127.0 - MAG, ADD, ["wtm_0", "wtm_1"], ["yr0"])
             if s >= 3:
                 tt(T.q[:], T.q[:], ps[3][:, 0:128], MIN, ["q", "ps3"], ["q"])
             if s == 4:
@@ -566,16 +724,18 @@ def rank_program(g, core, T, topo):
                 scan(T.sf[:], T.DD[:, 0:128], ps[fb][:, 0:128], ADD, MIN, ["DD", "ps%d" % fb], ["sf"])
                 ts(T.fl[:], T.sf[:, 15::16], c_fix, ADD, ["sf", "c_fix"], ["fl"], 2048.0, ADD)
 
-        tt(T.tf[:, 0:128], T.q[:], ps[2][:, 0:128], MIN, ["q", "ps2"], ["tf0"])
-        scan(T.tfs[:, 0:128], T.DD[:], T.tf[:, 0:128], ADD, MIN, ["DD", "tf0"], ["tfs"])
-        tt(T.tf[:, 128:256], T.ia[:], ps[2][:, 0:128], MAX, ["ia", "ps2"], ["tf1"])
+        tt(T.tf[:, 0:64], T.q[:, 0:64], ps[1][:, 0:64], MIN, ["q", "ps1"], ["tf0a"])
+        tt(T.tf[:, 64:128], T.q[:, 64:128], ps[2][:, 0:64], MIN, ["q", "ps2"], ["tf0"])
+        tt(T.tf[:, 128:192], T.ia[:, 0:64], ps[1][:, 0:64], MAX, ["ia", "ps1"], ["tf1a"])
+        scan(T.tfs[:, 0:128], T.DD[:], T.tf[:, 0:128], ADD, MIN, ["DD", "tf0", "tf0a"], ["tfs"])
+        tt(T.tf[:, 192:256], T.ia[:, 64:128], ps[2][:, 0:64], MAX, ["ia", "ps2"], ["tf1"])
         ts(T.tw[:], T.tfs[:, 15:128:16], c_fix, ADD, ["tfs", "c_fix"], ["tw"])
         for a in range(NVC, 8):
             o, n = 8 * a * (a + 1), 16 * (a + 1)
             op("a", lambda: g.scalar.activation(T.cmp[:, o:o + n], T.tf[:, 0:n], ACT.Abs, bias=T.tw[:, a:a + 1], scale=-1.0),
-               ["tf0", "tw"], ["cmp%d" % a])
+               ["tf0", "tf0a", "tw"], ["cmp%d" % a])
         ts(T.tl[:, 0:8], T.tfs[:, 15:128:16], c_fix, ADD, ["tfs", "c_fix"], ["tl"], 3328.0, ADD)
-        scan(T.tfs[:, 128:256], T.DD[:], T.tf[:, 128:256], ADD, MIN, ["DD", "tf1"], ["tfs2"])
+        scan(T.tfs[:, 128:256], T.DD[:], T.tf[:, 128:256], ADD, MIN, ["DD", "tf1", "tf1a"], ["tfs2"])
         tt(T.wd1[:, 0::2], T.tw[:], T.dum2[:], SUB, ["tw", "dum2"], ["wd1"])
         ts(T.tl[:, 8:16], T.tfs[:, 143::16], c_fix, ADD, ["tfs2", "c_fix"], ["tl2"], 2048.0, ADD)
         act(T.old[:], T.AD[:, 0:2944].indirect(T.tl[:, 0:8]), ACT.Identity, ADT + ["tl"], ["old"])
@@ -585,7 +745,7 @@ def rank_program(g, core, T, topo):
             o, n = 8 * a * (a + 1), 16 * (a + 1)
             ts(T.cmp[:, o:o + n], T.tf[:, 0:n], T.tw[:, a:a + 1], NE, ["tf0", "tw"], ["cmp%d" % a])
         scan(T.ms[:], T.md0[:], T.md1[:], MUL, ADD,
-             ["md0c", "md0d", "md01", "md02", "md03", "md04", "md14", "md15", "E1", "E2", "E3", "E4"], ["ms"])
+             ["md0c", "md0d", "md01", "md02", "md03", "md04", "md14", "md15"] + both("E1") + both("E2") + both("E3") + both("E4"), ["ms"])
         tt(T.yy[:], T.SR[:, 0:1672].indirect(T.tl[:, 8:16]), T.ms[:, 5::6], MUL, SRT + ["tl2", "ms"], ["yy"])
         scan(T.cs[:], T.DQ[:], T.cmp[:], ADD, MIN, DQT + ["cmp%d" % a for a in range(8)], ["cs"])
         ts(T.wd0[:, 1::2], T.cs[:, 0:576].indirect(T.lend[:, 0:1]), c_win, EQ, ["cs", "lend", "c_win"], ["win"])
@@ -602,8 +762,8 @@ def rank_program(g, core, T, topo):
         scan(T.sm[:, 1024 * i:1024 * i + 1024], T.d0t[:, 0:1024], T.ge[:, 1024 * i:1024 + 1024 * i], ADD, MIN,
              ["d0t", "ge%d" % (2 * i), "ge%d" % (2 * i + 1)], ["se%d" % i])
     opar = 1 - ((NP - 1) & 1)
-    tt(mt, T.sm[:, 15:2048:16], T.AD[:, AB + 1024 + opar:AB + 1280:2], MIN, ["se0", "se1", "ADa"], ["mt"])
-    ts(T.wtm[:], mt, 0.4921875, ADD, ["mt"], ["wtm"], MAG, ADD)
+    tt(mt, T.sm[:, 15:2048:16], T.AD[:, AB + 1024 + opar:AB + 1280:2], MIN, ["se0", "se1", "ADa"], ["mt", "mt_0", "mt_1"])
+    ts(T.wtm[:], mt, 0.4921875, ADD, ["mt"], ["wtm", "wtm_0", "wtm_1"], MAG, ADD)
     ts(T.yrb[:, opar::2], T.wtm[:], 127.0 - MAG, ADD, ["wtm"], ["yr1"])
     dma("a", T.yr[:], T.yrb[:], "st", ["yr0", "yr1"], [], 64)
     g.wait_ge(T.sem.sent, sent[0])

@@ -6,14 +6,20 @@ ACT = ActivationFunctionType
 
 H = "float16"
 MAG = 12582912.0
-AOFF = 127.984375
+AFR = 0.4921875
+AOFF = 127.0 + AFR
+EPS = 0.0078125
+VOFF = 1152.0
+M16 = 786432.0
 AB = 1280
 NP = 4
-STAG = True
-PRE = 12
-NVC = 0
-LCUT = [0, 82, 122, 178, 220, 256]
-TCUT = [0, 26, 64, 90, 128]
+NVC = 3
+PAIRS = "ab"
+SEG = [("a", 88), ("b", 68), ("w", 76), ("e", 24)]
+GRP = {"a": ("ab", 0), "b": ("w", 1)}
+ORDER = "v3 h2 h1 l2 k3 l1 c2 r3 c1 r2 Ha Hb Pw La Pe r1 S Lb Ca Cb Ga Cw Gb Ma Ce Mb A Me W We Wg"
+LH = "a"
+TCUT = [0, 48, 84, 112, 128]
 
 f32, bf, i32, u16 = "float32", "bfloat16", "int32", "uint16"
 
@@ -26,26 +32,30 @@ SCRATCH = {
     "avs": _sb(1280, bf), "dpi": _sb(1024, i32), "bdi": _sb(24, i32), "sbi": _sb(88, i32), "thi": _sb(16, i32),
     "s16a": _sb(88, H), "th16a": _sb(16, H), "wd0": _sb(32, f32), "wd1": _sb(16, f32),
     "AD": _sb(2944, f32), "W": _sb(1672, f32), "K": _sb(1664, f32), "SR": _sb(1672, f32),
-    "s16": _sb(1408, H), "th16": _sb(256, H), "nf": _sb(1408, f32), "one32": _sb(128, f32),
-    "bdu": _sb(24, u16), "bd2": _sb(24, u16), "du": _sb(1024, u16), "dupo": _sb(288, u16), "adup": _sb(288, bf),
-    "gd": _sb(1536, bf), "sd": _sb(1536, bf), "gm": _sb(4096, bf), "sm": _sb(4096, H),
+    "s16": _sb(1408, H), "th16": _sb(256, H), "nf": _sb(88, f32), "nf2": _sb(88, f32), "nf3": _sb(88, f32),
+    "one": _sb(128, bf), "cst": _sb(256, bf), "lh": _sb(768, H), "hi": _sb(2048, bf), "lo": _sb(2048, bf),
+    "h32": _sb(512, f32), "l32": _sb(512, f32), "s32": _sb(512, f32), "SL": _sb(512, H), "d0e": _sb(704, bf),
+    "bdu": _sb(24, u16), "bd2": _sb(24, u16), "du": _sb(1024, u16), "dupo": _sb(288, u16), "dh": _sb(192, H), "adup": _sb(288, bf),
+    "gd": _sb(1536, bf), "sd": _sb(1536, bf), "gm": _sb(2048, bf), "sm": _sb(2048, H), "sp": _sb(2048, H),
     "gt": _sb(2048, bf), "st": _sb(2048, H), "ge": _sb(2048, bf),
-    "rl": _sb(16 * 96, bf), "snd": _sb(16 * 64, bf), "gl": _sb(16 * 96, bf),
-    "J": _sb(128, f32), "JG": _sb(128, f32), "JR": _sb(128, f32), "X1i": _sb(128, f32), "X2i": _sb(128, i32),
-    "pi": _sb(8, i32), "col": _sb(16, f32), "tmp": _sb(128, f32), "tmp2": _sb(128, f32),
+    "rl": _sb(16 * 96, bf), "gl": _sb(16 * 96, bf),
+    "J": _sb(128, bf), "JG": _sb(128, bf), "JR": _sb(128, bf),
+    "pi": _sb(8, i32), "col": _sb(24, f32), "tmp": _sb(128, f32), "tmp2": _sb(128, f32),
     "BO": _sb(128, H), "BOm": _sb(128, H), "IDh": _sb(128, H), "sel": _sb(128, H), "CU": _sb(256, H),
-    "BOb": _sb(128, bf), "BOn": _sb(128, bf), "BOp": _sb(128, bf), "IDb": _sb(128, bf), "IDn": _sb(128, bf),
-    "P1": _sb(128, bf), "P2": _sb(128, bf), "P3": _sb(128, bf), "ia2": _sb(128, bf), "wt": _sb(256, f32), "dum2": _sb(8, f32),
-    "d0t": _sb(1408, bf), "d0p": _sb(768, bf), "d0n": _sb(128, bf), "DD": _sb(128, bf), "DQ": _sb(576, bf),
+    "BOb": _sb(128, bf), "BOn": _sb(128, bf), "BOp": _sb(128, H), "IDb": _sb(128, bf), "IDn": _sb(128, bf),
+    "P1": _sb(128, bf), "P2": _sb(128, bf), "P3": _sb(128, bf), "ia2": _sb(128, bf), "dum2": _sb(8, f32),
+    "d0t": _sb(1216, bf), "d0z": _sb(512, bf), "d0p": _sb(256, bf), "d0n": _sb(64, bf), "DD": _sb(128, bf), "DQ": _sb(576, bf),
     "l15": _sb(8, u16), "lend": _sb(8, u16), "dum": _sb(8, f32),
-    "mt": _sb(128, f32), "wtm": _sb(128, f32), "k2": _sb(128, f32), "tt": _sb(128, f32), "ss": _sb(128, f32),
-    "mT": _sb(128, bf), "mask": _sb(128, bf), "xv": _sb(128, H), "xs": _sb(128, H),
-    "yg": _sb(128, f32), "yp": _sb(128, H), "z": _sb(512, H), "sf": _sb(128, f32), "fl": _sb(8, u16),
+    "wtm": _sb(128, H), "tt": _sb(128, H), "ss": _sb(128, f32), "adj": _sb(128, f32),
+    "mT": _sb(128, H), "mask": _sb(128, H), "xv": _sb(128, H), "xs": _sb(128, H),
+    "yg": _sb(128, f32), "z": _sb(512, H), "sf": _sb(128, f32), "fl": _sb(8, u16),
     "md0": _sb(768, bf), "md1": _sb(768, bf), "ms": _sb(768, bf),
-    "r16": _sb(128, bf), "mn": _sb(128, bf), "nm": _sb(128, bf), "nok": _sb(128, bf), "na": _sb(128, bf),
-    "ia": _sb(128, bf), "q": _sb(128, f32), "tf": _sb(256, f32), "tfs": _sb(256, f32), "tw": _sb(8, f32),
-    "tl": _sb(16, u16), "cmp": _sb(576, bf), "cs": _sb(576, bf), "win": _sb(16, f32), "l1": _sb(8, f32),
-    "l2": _sb(8, f32), "ll": _sb(8, u16), "old": _sb(128, f32), "yy": _sb(128, f32),
+    "r16": _sb(128, bf), "mn": _sb(128, bf), "nm": _sb(128, bf), "na": _sb(128, bf),
+    "ia": _sb(128, bf), "q": _sb(128, f32), "tf": _sb(128, f32), "tfs": _sb(256, f32),
+    "IDm": _sb(128, bf), "IDp": _sb(128, bf), "IDk": _sb(128, H), "row": _sb(256, bf), "ok": _sb(128, bf),
+    "fs": _sb(384, H), "vr": _sb(128, bf), "t3": _sb(128, H), "n3": _sb(128, H), "oky": _sb(128, H), "w4": _sb(128, H),
+    "tl": _sb(16, u16), "cmp": _sb(576, bf), "cs": _sb(576, bf), "win": _sb(16, f32),
+    "ll": _sb(8, u16), "old": _sb(128, f32), "yy": _sb(128, f32),
     "yab": _sb(1280, bf), "yrb": _sb(256, bf),
 }
 for _b in range(8):
@@ -162,13 +172,25 @@ def rank_program(g, core, T, topo):
         else:
             op("g", lambda: g.iota(out, pat, base, cm), [], writes)
 
+    def sel(out, in_, pat, cmp_, fill, base, cm, reads, writes):
+        op("g", lambda: g.affine_select(out, in_, pat, cmp_, fill, base, cm), reads, writes)
+
     ADD, SUB, MUL, MAX, MIN = ALU.add, ALU.subtract, ALU.mult, ALU.max, ALU.min
     EQ, NE = ALU.is_equal, ALU.not_equal
+    ID = ACT.Identity
     ps = [T["ps%d" % b] for b in range(8)]
     ADT = ["ADj", "ADd", "ADa0", "ADa", "ADk"]
     WT = ["W0", "W1", "W2", "W3", "Wg0", "Wg1", "Wg2", "Wg3", "Wx", "Wy", "Wb1", "Wb2", "Wb3"]
-    KT = ["Kx0", "Kx", "K1", "K2", "K3", "Ka1", "Ka2", "Ka3"]
+    KT = ["Kx0", "Kx"] + ["K%s%d" % (k, l) for k in "abe" for l in (1, 2, 3)]
     SRT = ["SR0", "SR512", "SR1024", "SRa", "SRb"]
+    BD2 = ["bd20", "bd21", "bd22", "bd30", "bd31", "bd32"]
+
+    at, size = {}, dict(SEG)
+    c0 = 0
+    for k, n in SEG:
+        at[k] = c0
+        c0 += n
+    npair = sum(size[k] for k in PAIRS if k in size) // 2
 
     dma("s", T.avs[:, 0:256], T.av[:, 0:256], "l_av0", [], ["av0"])
     dma("a", T.bdi[:], T.bd[:], "l_bd", [], ["bdi"])
@@ -177,24 +199,15 @@ def rank_program(g, core, T, topo):
     dma("s", T.sbi[:], T.sb[:], "l_sb", [], ["sbi"])
     dma("s", T.thi[:], T.th[:], "l_th", [], ["thi"])
 
-    def sel(out, in_, pat, cmp_, fill, base, cm, reads, writes):
-        op("g", lambda: g.affine_select(out, in_, pat, cmp_, fill, base, cm), reads, writes)
-
-    iota(T.X1i[:], [[-16, 8], [1, 16]], 112, -1, ["X1i"])
-    iota(T.X2i[:], [[-16, 8], [1, 16]], 128, -1, ["X2i"], fl=False)
     iota(T.pi[:, 0:1], [[1, 1]], 0, 1, ["pi0"], fl=False)
+    iota(T.col[:, 20:23], [[8, 3]], -8, 1, ["c_p"])
     iota(T.J[:], [[1, 128]], 0, 0, ["J"])
     iota(T.JG[:], [[1, 8], [0, 16]], 0, 0, ["JG"])
     iota(T.JR[:], [[0, 8], [1, 16]], 0, 0, ["JR"])
-    ms(T.d0p[:], 0.0, ["d0p"])
-    ms(T.d0t[:], -0.0625, ["d0t"])
-    ms(T.d0p[:, 0::16], 8192.0, ["d0p"])
-    ms(T.d0t[:, 0::16], 8192.0, ["d0t"])
-    ts(T.P1[:], T.X1i[:], 0.0, EQ, ["X1i"], ["P1"])
-    ts(T.X2i[:], T.X2i[:], 127, ALU.bitwise_and, ["X2i"], ["X2i"])
-    ts(T.P2[:], T.X2i[:], 0.0, EQ, ["X2i"], ["P2"])
-    iota(T.P3[:], [[0, 128]], 1, 0, ["P3"])
-    sel(T.P3[:], T.P3[:], [[-1, 128]], EQ, 0.0, 0, 1, ["P3"], ["P3"])
+    iota(T.nf[:], [[1, 88]], 0, 88, ["nf"])
+    steps = (("d0p", 0.0, 8), ("d0z", 0.0, 16), ("d0t", -0.0625, 16), ("d0e", -0.0625, 8))
+    for nme, c, m in steps:
+        ms(T[nme][:], c, [nme])
 
     peers = [T.cores[rank ^ d] for d in (1, 2, 3)]
 
@@ -235,23 +248,8 @@ def rank_program(g, core, T, topo):
                      pid, rid, topo.mask(core, peers[d - 1]))
         return len(topo.engines(core, peers[d - 1]))
 
-    def perm1(x, d):
-        c0 = 32 * (d - 1)
-        bank = 7 if d == 1 else 6
-        mm("ps%d" % bank, ps[bank][:, 0:32], [(T["P%d" % d][:], T.rl[:, 96 * x + c0:96 * x + c0 + 32],
-                                               ["P%d" % d, "rl%d_%d" % (x, d)])])
-        act(T.snd[:, 64 * x + c0:64 * x + c0 + 32], ps[bank][:, 0:32], ACT.Identity, ["ps%d" % bank], ["snd%d_%d" % (x, d)])
-
-    def perm(x):
-        r0 = 96 * x
-        mm("ps7", ps[7][:, 0:32], [(T.P1[:], T.rl[:, r0:r0 + 32], ["P1", "rl%d" % x])])
-        mm("ps7", ps[7][:, 32:64], [(T.P2[:], T.rl[:, r0 + 32:r0 + 64], ["P2", "rl%d" % x])])
-
-    def evac(x):
-        act(T.snd[:, 64 * x:64 * x + 64], ps[7][:, 0:64], ACT.Identity, ["ps7"], ["snd%d" % x])
-
     def ghosts(x, l):
-        act(T.W[:, 1280 + 96 * l:1376 + 96 * l], ps[7][:, 0:96], ACT.Identity, ["ps7"], ["Wg%d" % l], bias=MAG)
+        act(T.W[:, 1280 + 96 * l:1376 + 96 * l], ps[7][:, 0:96], ID, ["ps7"], ["Wg%d" % l])
 
     def landed(x):
         for d in (1, 2, 3):
@@ -259,83 +257,126 @@ def rank_program(g, core, T, topo):
             mm("ps7", ps[7][:, c0:c0 + 32], [(T["P%d" % d][:], T.gl[:, 96 * x + c0:96 * x + c0 + 32],
                                               ["P%d" % d, "gl%d" % x])])
 
-    def gat(e, out, offs, otok, wtok):
-        src = T.W[:, 0:1672].indirect(offs)
+    Wall = T.W[:, 0:1672]
+
+    def gat(e, out, offs, otok, wtok, bias=0.0):
         if e == "v":
-            ts(out, src, -MAG, ADD, WT + otok, wtok)
+            cp(out, Wall.indirect(offs), WT + otok, wtok)
         else:
-            act(out, src, ACT.Identity, WT + otok, wtok, bias=-MAG)
+            act(out, Wall.indirect(offs), ID, WT + otok, wtok, bias=bias)
 
     col = T.col
-    c_pr, c_pg, c_p, c_p16, c_k, c_fix, c_win, c_pr1, c_np16 = [col[:, i:i + 1] for i in range(9)]
+    c_pr, c_pg, c_sb, c_p16, c_k, c_fix, c_win, c_pr1, c_np16 = [col[:, i:i + 1] for i in range(9)]
+    c_lo, c_hi, c_k2, c_g1, c_g2 = [col[:, i:i + 1] for i in range(12, 17)]
+    c_dn, c_p, c_up = [col[:, i:i + 1] for i in range(20, 23)]
 
-    def setup_rest():
+    def setup_first():
         ts(T.pi[:, 1:2], T.pi[:, 0:1], 15, ALU.bitwise_and, ["pi0"], ["pi1"])
         ts(T.pi[:, 2:3], T.pi[:, 0:1], 4, ALU.arith_shift_right, ["pi0"], ["pi2"])
-        cp(c_p, T.pi[:, 0:1], ["pi0"], ["c_p"])
-        cp(col[:, 0:2], T.pi[:, 1:3], ["pi1", "pi2"], ["c_r"])
-        ts(c_p16, c_pr, 0.0625, MUL, ["c_r"], ["c_p16"])
-        ts(c_np16, c_pr, -0.0625, MUL, ["c_r"], ["c_np16"])
-        ts(c_k, c_pr, -15.0, ADD, ["c_r"], ["c_k"], 0.0625, MUL)
-        ts(c_fix, c_pr, 15.0, ALU.is_lt, ["c_r"], ["c_fix"], 8192.0, MUL)
-        ts(c_win, c_pr, -15.0, ADD, ["c_r"], ["c_win"], 1.0 / 128, MUL)
-        ts(c_pr1, c_pr, 1.0, ADD, ["c_r"], ["c_pr1"])
-        ts(col[:, 9:10], c_pr, 7.0, MIN, ["c_r"], ["c9"], 1.0, ADD)
-        ts(col[:, 10:11], col[:, 9:10], 1.0, ADD, ["c9"], ["c10"], 8.0, MUL)
-        tt(col[:, 11:12], col[:, 9:10], col[:, 10:11], MUL, ["c9", "c10"], ["c11"])
-        ts(T.lend[:, 0:1], col[:, 11:12], -1.0, ADD, ["c11"], ["lend"])
-        ts(T.BO[:], T.JG[:], c_pg, EQ, ["JG", "c_r"], ["BO"])
-        ts(T.BOm[:], T.JG[:], c_pg, EQ, ["JG", "c_r"], ["BOm"], -1.0, MUL)
-        ts(T.BOp[:], T.JG[:], c_pg, EQ, ["JG", "c_r", "c_np16"], ["BOp"], c_np16, MUL)
         ts(T.IDh[:], T.J[:], c_p, EQ, ["J", "c_p"], ["IDh"])
+
+    def setup_cols():
+        cp(col[:, 0:2], T.pi[:, 1:3], ["pi1", "pi2"], ["c_r"])
+        for nme, c, m in steps:
+            ms(T[nme][:, 0::m], 8192.0, [nme])
+        for c, scale, bias, nme in ((c_k, 0.0625, -0.9375, "c_k"), (c_k2, 0.0625, M16 - 0.4375, "c_k2"),
+                                    (c_win, 1.0 / 128, -15.0 / 128, "c_win"), (c_pr1, 1.0, 1.0, "c_pr1")):
+            act(c, c_pr, ID, ["c_r"], [nme], bias=bias, scale=scale)
+        act(c_sb, c_pg, ID, ["c_r"], ["c_sb"], scale=-1408.0)
+        act(T.wd1[:, 1::2], T.J[:, 0::16], ID, ["J", "c_r"], ["wd1c"], bias=c_pr)
+        act(T.dum2[:], T.wd1[:, 1::2], ID, ["wd1c"], ["dum2"], bias=-8192.0 - AB)
+
+    def setup_lists():
+        ts(c_lo, c_pr, 8.0, ALU.is_lt, ["c_r"], ["c_lo"])
+        ts(c_hi, c_pr, 8.0, ALU.is_ge, ["c_r"], ["c_hi"])
+        for l in range(3):
+            ts(T.bd2[:, 4 * l:4 * l + 4], T.bdi[:, 6 * l + 6:6 * l + 10], float(256 * l), ADD, ["bdi"], ["bd2%d" % l])
+            ts(T.bd2[:, 12 + 2 * l:14 + 2 * l], T.bdi[:, 6 * l + 10:6 * l + 12], float(256 * l), ADD, ["bdi"], ["bd3%d" % l])
+        for i, (a, b) in enumerate(((c_p, c_lo), (c_up, c_lo), (c_dn, c_hi), (c_p, c_hi))):
+            ts(T.SL[:, 128 * i:128 * i + 128], T.J[:], a, EQ, ["J", "c_p", "c_lo", "c_hi"], ["SL%d" % i], b, MUL)
+        ts(c_g1, c_pr, 2.0, MUL, ["c_r", "c_p"], ["c_g1"], c_p, SUB)
+        ts(c_g2, c_pg, 0.0, EQ, ["c_r"], ["c_g2"], -128.0, MUL)
+        ts(col[:, 9:10], c_pr, 7.0, MIN, ["c_r"], ["c9"], 1.0, ADD)
+        ms(T.cst[0:1, 0:2 * npair], -EPS, ["cst0"])
+        ms(T.one[0:1, :], 1.0, ["one"])
+        ms(T.cst[0:1, 2 * npair:256], AFR, ["cst"])
+        ts(T.P3[:], T.J[:], c_p, EQ, ["J", "c_p"], ["P3"])
+        ts(T.P1[:], T.J[:], -112.0, ADD, ["J", "c_g1"], ["P1"], c_g1, EQ)
+        ts(c_g2, c_g2, c_g1, ADD, ["c_g1", "c_g2"], ["c_g2"])
+        ts(col[:, 10:11], col[:, 9:10], 1.0, ADD, ["c9"], ["c10"], 8.0, MUL)
+        ts(c_fix, c_pr, 15.0, ALU.is_lt, ["c_r"], ["c_fix"], 8192.0, MUL)
+        ts(T.BO[:], T.JG[:], c_pg, EQ, ["JG", "c_r"], ["BO"])
+        ts(ps[4][:, 384:448], T.JR[:, 0:64], -0.0625, MUL, ["JR"], ["ramp"], 0.9375, ADD)
         ts(T.sel[:], T.JG[:], c_p, EQ, ["JG", "c_p"], ["sel"])
-        ts(T.CU[:, 0:128], T.J[:], 2.0, MUL, ["J"], ["CU0"], -1024.0, ADD)
-        ts(T.CU[:, 128:256], T.J[:], 2.0, MUL, ["J"], ["CU1"], -1023.0, ADD)
+        ts(T.P2[:], T.J[:], -128.0, ADD, ["J", "c_g2"], ["P2"], c_g2, EQ)
+        ts(col[:, 11:12], col[:, 9:10], col[:, 10:11], MUL, ["c9", "c10"], ["c11"], -1.0, ADD)
+        ts(T.row[0:1, 0:128], T.JR[0:1, :], 15.0, EQ, ["JR"], ["row0"], -8192.0, MUL)
+        ms(T.row[0:1, 128:256], -8192.0, ["row"])
         cp(T.l15[:], T.J[:, 15::16], ["J"], ["l15"])
-        ts(T.dum[:], T.J[:, 0::16], c_pr, ADD, ["J", "c_r"], ["dum"])
-        ts(T.tmp[:], T.JR[:], c_pr, EQ, ["JR", "c_r"], ["tmp"], 16384.0, MUL)
-        ts(T.tmp2[:], T.JR[:], c_pr1, EQ, ["JR", "c_pr1"], ["tmp2"], -8192.0, MUL)
-        cp(T.wd1[:, 1::2], T.dum[:], ["dum"], ["wd1c"])
-        ts(T.dum2[:], T.dum[:], -3328.0, ADD, ["dum"], ["dum2"])
-        tt(T.DD[:], T.tmp[:], T.tmp2[:], ADD, ["tmp", "tmp2"], ["DD"])
+        ts(T.r16[:], T.JR[:], c_pr, EQ, ["JR", "c_r"], ["r16"], 16384.0, MUL)
+        ts(T.mn[:], T.JR[:], c_pr1, EQ, ["JR", "c_pr1"], ["mn"], -8192.0, MUL)
+        cp(T.lend[:, 0:1], col[:, 11:12], ["c11"], ["lend"])
+        ts(T.nf2[:], T.nf[:], c_sb, ADD, ["nf", "c_sb"], ["nf2"])
+
+    def setup_s(part):
+        if part == 1:
+            mm("ps3", ps[3][:, 128:256], [(T.P3[:], T.r16[:], ["P3", "r16"]), (T.P3[:], T.mn[:], ["P3", "mn"])])
+            act(T.DD[:], ps[3][:, 128:256], ID, ["ps3"], ["DD"])
+            act(T.CU[:, 128:256], T.J[:], ID, ["J"], ["CU1"], bias=1025.0, scale=2.0)
+        made = ((("IDk", "P3", -1.0), ("IDn", "P3", -1.0)), (("BOm", "BO", -1.0), ("BOb", "BO", 1.0), ("BOn", "BO", -2048.0)),
+                (("IDm", "P3", -float(AB)), ("IDp", "P3", 4096.0)))
+        for nme, src, c in made[part - 1]:
+            act(T[nme][:], T[src][:], ID, [src], [nme], scale=c)
+
+    def setup_sub():
+        ts(T.th16a[:], T.thi[:], -127.0, ADD, ["thi"], ["th16a"])
+        ts(T.nf[:], T.nf2[:], 1024.0, ALU.is_ge, ["nf2"], ["nf"], 256.0, MUL)
+        tt(T.nf3[:], T.sbi[:], T.nf2[:], SUB, ["sbi", "nf2"], ["nf3"])
+        dma("s", T.th16[0:8, :], T.th16a[:], "r_th", ["th16a"], ["th16"])
+        cp(T.AD[:, 256:1280], T.dpi[:], ["dpi"], ["ADd"])
+        tt(T.s16a[:], T.nf3[:], T.nf[:], SUB, ["nf3", "nf"], ["s16a"])
+        dma("s", T.s16[0:8, :], T.s16a[:], "r_sb", ["s16a"], ["s16"])
 
     def setup_g(part):
-        if part == 0:
-            iota(T.nf[0:1, 0:1024], [[-1, 1024]], 0, 0, ["nf0"])
-            iota(T.nf[0:1, 1024:1408], [[-1, 384]], -1280, 0, ["nf1"])
         if part == 1:
             iota(T.K[:, 0:256], [[0, 256]], 1000, 0, ["Kx0"])
             iota(T.K[:, 1024:1664], [[0, 640]], 1000, 0, ["Kx"])
-            for nme, c in (("IDb", 1), ("IDn", -1)):
-                iota(T[nme][:], [[0, 128]], c, 0, [nme])
-                sel(T[nme][:], T[nme][:], [[-1, 128]], EQ, 0.0, 0, 1, [nme], [nme])
         if part == 2:
             iota(T.AD[:, 0:256], [[0, 256]], 0, 0, ["ADj"])
             iota(T.AD[:, AB + 1280:2944], [[0, 384]], 0, 0, ["ADk"])
+            iota(T.d0n[:], [[0, 64]], -8192, 0, ["d0n"])
+            sel(T.d0n[:], T.d0n[:], [[0, 4], [1, 16]], EQ, 0.0625, 0, 0, ["d0n"], ["d0n"])
+        if part == 3:
             iota(T.SR[:, 1024:1280], [[0, 256]], 1, 0, ["SRa"])
             iota(T.SR[:, 1664:1672], [[0, 8]], 1, 0, ["SRb"])
-            iota(T.one32[0:1, :], [[0, 128]], 1, 0, ["one32"])
-            iota(T.d0n[:], [[0, 128]], -8192, 0, ["d0n"])
-            sel(T.d0n[:], T.d0n[:], [[0, 8], [1, 16]], EQ, 0.0, 0, 0, ["d0n"], ["d0n"])
             iota(T.md0[:, 0::6], [[0, 128]], 0, 0, ["md0c"])
             iota(T.md0[:, 5::6], [[0, 128]], -1, 0, ["md0d"])
             iota(T.wd0[:, 0::2], [[0, 16]], 0, 0, ["wd0c"])
-        if part == 3:
-            for nme, c in (("BOb", 1), ("BOn", -2048)):
-                iota(T[nme][:], [[0, 128]], c, 0, [nme])
-                sel(T[nme][:], T[nme][:], [[-16, 8], [0, 16]], ALU.is_ge, 0.0, 0, 1, [nme], [nme])
-                sel(T[nme][:], T[nme][:], [[16, 8], [0, 16]], ALU.is_ge, 0.0, 15, -1, [nme], [nme])
             iota(T.DQ[:], [[0, 576]], 8192, 0, ["DQ"])
             for a in range(8):
                 o, n = 8 * a * (a + 1), 16 * (a + 1)
                 sel(T.DQ[:, o:o + n], T.DQ[:, o:o + n], [[1, n]], EQ, -1.0 / 128, 0, 0, ["DQ"], ["DQ%d" % a])
 
-    mt, k2, yp = ps[4][:, 0:128], ps[4][:, 128:256], ps[4][:, 256:384]
+    mt, yp = ps[4][:, 0:128], ps[4][:, 256:384]
     DQT = ["DQ%d" % a for a in range(8)]
     sent = [0]
 
     def negv():
-        return [(T.BOm[:], T.xv[:], ["BOm", "xv", "xv_0"]), (T.BOp[:], T.mask[:], ["BOp", "mask_0", "mask_1"])]
+        return [(T.BOm[:], T.xv[:], ["BOm", "xv", "xv_0"])]
+
+    def pairs(bank, o, src, b, n, tk):
+        for half in (0, 1):
+            mm("ps%d" % bank, ps[bank][:, o + half * n:o + half * n + n],
+               [(T.SL[:, 128 * (2 * half + i):128 * (2 * half + i) + 128], src[:, b + i:b + 2 * n:2],
+                 ["SL%d" % (2 * half + i), tk]) for i in (0, 1)])
+
+    def pair_mm(l):
+        bank, o, b = (5, 0, 0) if l == 1 else (6, 256 * (l - 2), 256 * (l - 1))
+        pairs(bank, o, T.lh, b, npair, "lh%d" % l)
+
+    def pair_cp(l):
+        bank, o, b = (5, 0, 0) if l == 1 else (6, 256 * (l - 2), 256 * (l - 1))
+        cp(T.du[:, b:b + 2 * npair], ps[bank][:, o:o + 2 * npair], ["ps%d" % bank], ["du%d" % l])
 
     for t in range(NP):
         par = t & 1
@@ -343,134 +384,161 @@ def rank_program(g, core, T, topo):
         last = t == NP - 1
         if t == 0:
             cp(T.bdu[:], T.bdi[:], ["bdi"], ["bdu"])
+            setup_first()
             ts(T.rl[:, 0:96], T.avs[:, 0:256].indirect(T.bdu[:, 0:6]), -127.0, ADD, ["av0", "bdu"], ["rl0"])
         else:
-            ts(T.rl[:, 96 * x:96 * x + 96], T.AD[:, AB:AB + 256].indirect(T.bdu[:, 0:6]), 0.984375, ADD,
+            ts(T.rl[:, 96 * x:96 * x + 96], T.AD[:, AB:AB + 256].indirect(T.bdu[:, 0:6]), AFR, ADD,
                ["ADa0", "bdu"], ["rl%d" % x])
         sent[0] += send(x)
+        links, lo_, ltok = (T.dpi, 0, "dpi") if t == 0 else (T.AD, 256, "ADd")
+
+        def lh(l):
+            a, n = 256 * (l - 1), 2 * npair
+            if t == 0 or LH == "v":
+                cp(T.lh[:, a:a + n], links[:, lo_ + a:lo_ + a + n], [ltok], ["lh%d" % l])
+            else:
+                act(T.lh[:, a:a + n], links[:, lo_ + a:lo_ + a + n], ID, [ltok], ["lh%d" % l])
+
+        def whole(l):
+            a = 256 * (l - 1) + 2 * npair
+            cp(T.du[:, a:256 * l], links[:, lo_ + a:lo_ + 256 * l], [ltok], ["dw%d" % l])
+
         if t == 0:
-            setup_g(0)
-            for l in range(3):
-                ts(T.bd2[:, 6 * l:6 * l + 6], T.bdi[:, 6 * l + 6:6 * l + 12], float(256 * l), ADD, ["bdi"], ["bd2%d" % l])
-            ts(T.W[:, 0:256], T.avs[:, 0:256], MAG - 127.0, ADD, ["av0"], ["W0"])
-            BD2 = ["bd20", "bd21", "bd22"]
-            setup_rest()
-            cp(T.dupo[:], T.dpi[:, 0:768].indirect(T.bd2[:, 0:18]), ["dpi"] + BD2, ["dupo"])
-            act(T.adup[:], T.avs[:, 256:1024].indirect(T.bd2[:, 0:18]), ACT.Identity, ["av1"] + BD2, ["adup"], bias=-127.0)
-            act(T.W[:, 256:1280], T.avs[:, 256:1280], ACT.Identity, ["av1"], ["W1", "W2", "W3", "Wx", "Wb1", "Wb2", "Wb3"],
-                bias=MAG + 128.0, scale=0.0)
-            act(T.W[:, 1376:1672], T.avs[:, 256:552], ACT.Identity, ["av1"], ["Wg1", "Wg2", "Wg3", "Wy"],
-                bias=MAG + 128.0, scale=0.0)
-            act(ps[1][:], T.avs[:, 256:768], ACT.Identity, ["av1"], ["ps1"], bias=-AOFF)
-            act(ps[2][:, 0:256], T.avs[:, 768:1024], ACT.Identity, ["av1"], ["ps2"], bias=-AOFF)
-            act(ps[2][:, 256:384], T.avs[:, 1024::2], ACT.Identity, ["av1"], ["ps2"], bias=-AOFF)
-            act(T.AD[:, AB:AB + 1280], T.avs[:], ACT.Identity, ["av0", "av1"], ["ADa0", "ADa"], bias=-AOFF)
-            cp(T.du[:, 0:768], T.dpi[:, 0:768], ["dpi"], ["du"])
-            cp(T.du[:, 768:896], T.dpi[:, 768::2], ["dpi"], ["dut"])
-            ts(T.th16a[:], T.thi[:], -127.0, ADD, ["thi"], ["th16a"])
-            cp(T.s16a[:], T.sbi[:], ["sbi"], ["s16a"])
-            dma("s", T.th16[0:8, :], T.th16a[:], "r_th", ["th16a"], ["th16"])
-            dma("s", T.s16[0:8, :], T.s16a[:], "r_sb", ["s16a"], ["s16"])
-            cp(T.AD[:, 256:1280], T.dpi[:], ["dpi"], ["ADd"])
-        else:
-            cp(T.dupo[:], T.AD[:, 256:1024].indirect(T.bd2[:, 0:18]), ["ADd"] + BD2, ["dupo"])
-            act(T.adup[:], T.AD[:, AB + 256:AB + 1024].indirect(T.bd2[:, 0:18]), ACT.Identity, ["ADa"] + BD2,
-                ["adup"], bias=0.984375)
-            act(ps[1][:], T.AD[:, AB + 256:AB + 768], ACT.Identity, ["ADa"], ["ps1"])
-            act(ps[2][:, 0:256], T.AD[:, AB + 768:AB + 1024], ACT.Identity, ["ADa"], ["ps2"])
-            act(ps[2][:, 256:384], T.AD[:, AB + 1024 + par:AB + 1280:2], ACT.Identity, ["ADa"], ["ps2"])
-            ts(T.W[:, 0:256], T.AD[:, AB:AB + 256], 0.984375, ADD, ["ADa0"], ["W0"], MAG, ADD)
-            cp(T.du[:, 0:768], T.AD[:, 256:1024], ["ADd"], ["du"])
-            cp(T.du[:, 768:896], T.AD[:, 1024 + par:1280:2], ["ADd"], ["dut"])
-            if last:
-                cp(T.du[:, 896:1024], T.AD[:, 1025 - par:1280:2], ["ADd"], ["duo"])
+            act(T.W[:, 0:256], T.avs[:, 0:256], ID, ["av0"], ["W0"], bias=-127.0)
+            setup_cols()
+            setup_lists()
+            act(T.adup[:], T.avs[:, 256:1024].indirect(T.bd2[:, 0:18]), ID, ["av1"] + BD2, ["adup"], bias=-127.0)
+            act(T.W[:, 256:1280], T.avs[:, 256:1280], ID, ["av1"], ["W1", "W2", "W3", "Wx", "Wb1", "Wb2", "Wb3"],
+                bias=128.0, scale=0.0)
+            act(T.W[:, 1376:1672], T.avs[:, 256:552], ID, ["av1"], ["Wg1", "Wg2", "Wg3", "Wy"], bias=128.0, scale=0.0)
+            act(T.AD[:, AB:AB + 1280], T.avs[:], ID, ["av0", "av1"], ["ADa0", "ADa"], bias=-AOFF)
+            act(T.CU[:, 0:128], T.J[:], ID, ["J"], ["CU0"], bias=1024.0, scale=2.0)
+        cp(T.dh[:], links[:, lo_:lo_ + 768].indirect(T.bd2[:, 0:12]), [ltok] + BD2, ["dh"])
+        cp(T.dupo[:, 192:288], links[:, lo_:lo_ + 768].indirect(T.bd2[:, 12:18]), [ltok] + BD2, ["dup3"])
+        lh(1)
+        pairs(0, 0, T.dh, 0, 96, "dh")
+        for l in (1, 2, 3):
+            if l > 1:
+                lh(l)
+            pair_mm(l)
+        if t > 0:
+            act(T.W[:, 0:256], T.AD[:, AB:AB + 256], ID, ["ADa0"], ["W0"], bias=AFR)
+            act(T.adup[:], T.AD[:, AB + 256:AB + 1024].indirect(T.bd2[:, 0:18]), ID, ["ADa"] + BD2, ["adup"], bias=AFR)
+        act(ps[2][:, 256:384], T.AD[:, AB + 1024 + par:AB + 1280:2], ID, ["ADa"], ["ps2"], bias=-AFR)
+        for l in (1, 2, 3):
+            whole(l)
+        cp(T.du[:, 768:896], links[:, lo_ + 768 + par:lo_ + 1024:2], [ltok], ["dut"])
+        cp(T.dupo[:, 0:192], ps[0][:, 0:192], ["ps0"], ["dupo"])
+        for l in (1, 2, 3):
+            pair_cp(l)
+        if last:
+            cp(T.du[:, 896:1024], T.AD[:, 1025 - par:1280:2], ["ADd"], ["duo"])
+        if t == 0:
+            setup_sub()
         CUp = T.CU[:, 128 * par:128 * par + 128]
         CUt = "CU%d" % par
-
-        def first_links(part):
-            if part == 0:
-                mm("ps3", ps[3][:, 0:128], [(T.IDh[:], CUp, ["IDh", CUt])])
-                act(T.yg[:], T.AD[:, 1024 + par:1280:2], ACT.Identity, ["ADd"], ["yg_0", "yg_1"], bias=-2048.0)
-            else:
-                tt(yp, T.yg[:], ps[3][:, 0:128], SUB, ["yg_0", "yg_1", "ps3"], ["yp_0", "yp_1"])
-
-        if t > 0:
-            first_links(0)
-            first_links(1)
+        mm("ps3", ps[3][:, 0:128], [(T.IDh[:], CUp, ["IDh", CUt])])
+        tt(yp, links[:, lo_ + 768 + par:lo_ + 1024:2], ps[3][:, 0:128], SUB, [ltok, "ps3"], ["yp_0", "yp_1"])
         landed(x)
         ghosts(x, 0)
 
         for l in (1, 2, 3):
             xl = x + l
             o = 96 * (l - 1)
-            cuts = LCUT
             b = 256 * (l - 1)
+            ne = size["e"]
+            going = [0]
 
-            def gm(e, i):
-                gat(e, T.gm[:, 16 * cuts[i]:16 * cuts[i + 1]], T.du[:, b + cuts[i]:b + cuts[i + 1]], ["du"], ["gm%d" % i])
+            def span(ks, m):
+                a = at[ks[0]] - (0 if m == 8 else 2 * npair)
+                return m * a, m * (a + sum(size[j] for j in ks))
 
-            def sm(i):
-                n = 16 * (cuts[i + 1] - cuts[i])
-                scan(T.sm[:, 16 * cuts[i]:16 * cuts[i + 1]], T.d0t[:, 0:n], T.gm[:, 16 * cuts[i]:16 * cuts[i + 1]],
-                     ADD, MIN, ["d0t", "gm%d" % i] + (["gmx", "gmy"] if i == 0 else []), ["sm%d" % i])
-
-            def mn(c0, c1, rd, wr):
-                ab, ao = (1, 256 * (l - 1)) if l < 3 else (2, 0)
-                tt(T.K[:, 256 * l + c0:256 * l + c1], T.sm[:, 16 * c0 + 15:16 * c1:16],
-                   ps[ab][:, ao + c0:ao + c1], MIN, rd + ["ps%d" % ab], wr)
-
-            if STAG:
-                def rel(d, part):
+            def step(w):
+                k = w[1:]
+                if w[0] in "hlcrvk":
+                    d = int(k)
                     c0 = 32 * (d - 1)
-                    if part == 0:
-                        scan(T.sd[:, 16 * c0:16 * c0 + 512], T.d0p[:, 0:512], T.gd[:, 16 * c0:16 * c0 + 512], ADD, MIN,
-                             ["d0p", "gd%d" % d], ["sd%d" % d])
-                        return
-                    tt(T.rl[:, 96 * xl + c0:96 * xl + c0 + 32], T.sd[:, 16 * c0 + 15:16 * c0 + 512:16],
-                       T.adup[:, o + c0:o + c0 + 32], MIN, ["sd%d" % d, "adup"], ["rl%d_%d" % (xl, d)])
+                    c = 32 * (l - 1) + 16 * (d - 1)
+                    e0, e1 = 8 * c0, 8 * c0 + 256
+                    if w[0] == "h":
+                        gat("a", T.gd[:, e0:e1], T.dupo[:, 96 + c:112 + c], ["dupo"], ["gd" + k])
+                    elif w[0] == "l":
+                        tt(T.gd[:, 512 + e0:512 + e1], Wall.indirect(T.dupo[:, c:c + 16]), T.gd[:, e0:e1], MIN,
+                           WT + ["dupo", "gd" + k], ["gl_" + k])
+                    elif w[0] == "c":
+                        scan(T.sd[:, e0:e1], T.d0p[:], T.gd[:, 512 + e0:512 + e1], ADD, MIN, ["d0p", "gl_" + k], ["sd" + k])
+                    elif w[0] == "v":
+                        gat("v", T.gd[:, 1024:1536], T.dupo[:, 160 + 32 * l:192 + 32 * l], ["dup3"], ["gl_3"])
+                    elif w[0] == "k":
+                        scan(T.sd[:, 512:1024], T.d0z[:], T.gd[:, 1024:1536], ADD, MIN, ["d0z", "gl_3"], ["sd3"])
+                    else:
+                        src, a = (T.sd[:, e0 + 7:e1:8], 2 * c) if d < 3 else (T.sd[:, 527:1024:16], 160 + 32 * l)
+                        tt(T.rl[:, 96 * xl + c0:96 * xl + c0 + 32], src, T.adup[:, a:a + 32],
+                           MIN, ["sd" + k, "adup"], ["rl%d_%d" % (xl, d)])
+                        n = send1(xl, d)
+                        going[0] += n
+                        sent[0] += n
+                        tok["gl%d" % xl] = {"w": ("arr%d" % xl, going[0]), "r": {}}
+                elif w == "S":
+                    if t == 0:
+                        setup_g(l)
+                        setup_s(l)
+                elif w[0] == "H":
+                    e0, e1 = span(k, 8)
+                    c = b + npair
+                    gat("a", T.hi[:, e0:e1], T.du[:, c + e0 // 16:c + e1 // 16], ["du%d" % l], ["hi" + k], bias=0.5)
+                elif w[0] == "L":
+                    e0, e1 = span(k, 8)
+                    tt(T.lo[:, e0:e1], Wall.indirect(T.du[:, b + e0 // 16:b + e1 // 16]), T.hi[:, e0:e1], MIN,
+                       WT + ["du%d" % l, "hi" + k], ["lo" + k])
+                elif w == "Pe":
+                    gat("a", T.h32[:, 0:16 * ne], T.du[:, b + 256 - ne:b + 256], ["dw%d" % l], ["loe"], bias=AFR)
+                elif w[0] in "PU":
+                    e0, e1 = span(k, 16)
+                    c = b + 2 * npair
+                    gat("a" if w[0] == "P" else "v", T.gm[:, e0:e1], T.du[:, c + e0 // 16:c + e1 // 16], ["dw%d" % l],
+                        ["lo" + k])
+                elif w == "Ce":
+                    scan(T.s32[:, 0:16 * ne], T.d0t[:, 0:16 * ne], T.h32[:, 0:16 * ne], ADD, MIN, ["d0t", "loe"], ["spe"])
+                elif w[0] == "C":
+                    m = 8 if k[0] in PAIRS else 16
+                    e0, e1 = span(k, m)
+                    src, dst, d0 = (T.lo, T.sp, T.d0e) if m == 8 else (T.gm, T.sm, T.d0t)
+                    scan(dst[:, e0:e1], d0[:, 0:e1 - e0], src[:, e0:e1], ADD, MIN, ["d0e", "d0t"] + ["lo" + j for j in k],
+                         ["sp" + j for j in k])
+                elif w[0] == "G":
+                    ks, bank = GRP[k]
+                    for js, m in (([j for j in ks if j in PAIRS], 8), ([j for j in ks if j not in PAIRS], 16)):
+                        if js:
+                            e0, e1 = span(js, m)
+                            a, n = at[js[0]], (e1 - e0) // m
+                            mm("ps%d" % bank, ps[bank][:, a - at[ks[0]]:a - at[ks[0]] + n],
+                               [(T.one[0:1, :], T.cst[0:1, a:a + n], ["one", "cst", "cst0"]),
+                                (T.IDh[:], (T.sp if m == 8 else T.sm)[:, e0 + m - 1:e1:m], ["IDh"] + ["sp" + j for j in js])])
+                elif w == "Me":
+                    a = 256 * l + 256 - ne
+                    tt(T.K[:, a:a + ne], T.s32[:, 15:16 * ne:16], T.AD[:, AB + a:AB + a + ne], MIN, ["spe", "ADa"], ["Ke%d" % l])
+                elif w[0] == "M":
+                    ks, bank = GRP[k]
+                    a, n = 256 * l + at[ks[0]], sum(size[j] for j in ks)
+                    tt(T.K[:, a:a + n], ps[bank][:, 0:n], T.AD[:, AB + a:AB + a + n], MIN, ["ps%d" % bank, "ADa"],
+                       ["K%s%d" % (k, l)])
+                elif w == "A":
+                    landed(xl)
+                elif w == "Wg":
+                    ghosts(xl, l)
+                elif w == "W":
+                    a, n = 256 * l, 256 - ne
+                    ts(T.W[:, a:a + n], T.K[:, a:a + n], MAG, ADD, ["Ka%d" % l, "Kb%d" % l], ["W%d" % l], -MAG, ADD)
+                elif w == "We":
+                    a = 256 * l + 256 - ne
+                    ts(T.W[:, a:a + ne], T.K[:, a:a + ne], MAG, ADD, ["Ke%d" % l], ["Wb%d" % l], -MAG, ADD)
 
-                for e, d in (("v", 3), ("a", 1), ("a", 2)):
-                    c0 = 32 * (d - 1)
-                    gat(e, T.gd[:, 16 * c0:16 * c0 + 512], T.dupo[:, o + c0:o + c0 + 32], ["dupo"], ["gd%d" % d])
-                gat("v", T.gm[:, 0:8 * PRE], T.du[:, b:b + PRE // 2], ["du"], ["gmx"])
-                rel(3, 0)
-                rel(1, 0)
-                rel(3, 1)
-                n = send1(xl, 3)
-                rel(2, 0)
-                rel(1, 1)
-                n += send1(xl, 1)
-                gm("a", 1)
-                gat("v", T.gm[:, 8 * PRE:16 * PRE], T.du[:, b + PRE // 2:b + PRE], ["du"], ["gmy"])
-                rel(2, 1)
-                n += send1(xl, 2)
-                tok["gl%d" % xl] = {"w": ("arr%d" % xl, n), "r": {}}
-                sent[0] += n
-            if t == 0:
-                setup_g(l)
-            gm("a", 2)
-            gm("a", 3)
-            gm("a", 4)
-            gat("v", T.gm[:, 16 * PRE:16 * cuts[1]], T.du[:, b + PRE:b + cuts[1]], ["du"], ["gm0"])
-            sm(1)
-            sm(0)
-            sm(2)
-            sm(3)
-            c4 = cuts[3]
-            mn(0, c4, ["sm0", "sm1", "sm2"], ["Ka%d" % l])
-            sm(4)
-            ts(T.wt[:, 0:c4], T.K[:, 256 * l:256 * l + c4], 0.4921875, ADD, ["Ka%d" % l], ["wt"], MAG, ADD)
-            landed(xl)
-            ghosts(xl, l)
-            act(T.W[:, 256 * l:256 * l + c4], T.wt[:, 0:c4], ACT.Identity, ["wt"], ["W%d" % l])
-            if t == 0 and l < 3:
-                first_links(l - 1)
-            mn(c4, 256, ["sm3", "sm4"], ["K%d" % l])
-            ts(T.W[:, 256 * l + c4:256 * l + 256], T.K[:, 256 * l + c4:256 * l + 256], 0.4921875, ADD,
-               ["K%d" % l], ["Wb%d" % l], MAG, ADD)
+            for w in ORDER.split():
+                step(w)
 
         cuts = TCUT
-        for e, i in (("v", 0), ("a", 1), ("v", 2), ("a", 3)):
+        for e, i in (("v", 0), ("a", 1), ("a", 2), ("a", 3)):
             gat(e, T.gt[:, 16 * cuts[i]:16 * cuts[i + 1]], T.du[:, 768 + cuts[i]:768 + cuts[i + 1]], ["dut"],
                 ["gt%d" % i])
 
@@ -479,71 +547,88 @@ def rank_program(g, core, T, topo):
             scan(T.st[:, 16 * cuts[i]:16 * cuts[i + 1]], T.d0t[:, 0:n], T.gt[:, 16 * cuts[i]:16 * cuts[i + 1]],
                  ADD, MIN, ["d0t", "gt%d" % i], ["st%d" % i])
 
-        spare = []
+        spare, vspare = [], []
         if t == 0:
-            def sr_part(c0, n, dst, nft):
+            def sr_part(c0, n, dst):
                 def run():
-                    mm("ps7", ps[7][:, 0:n], [(T.sel[0:8, :], T.s16[0:8, c0:c0 + n], ["sel", "s16"]),
-                                              (T.one32[0:1, :], T.nf[0:1, c0:c0 + n], ["one32", nft])])
-                    act(T.SR[:, dst:dst + n], ps[7][:, 0:n], ACT.Identity, ["ps7"], ["SR%d" % c0])
+                    mm("ps7", ps[7][:, 0:n], [(T.sel[0:8, :], T.s16[0:8, c0:c0 + n], ["sel", "s16"])])
+                    act(T.SR[:, dst:dst + n], ps[7][:, 0:n], ID, ["ps7"], ["SR%d" % c0])
                 return run
-            spare = [sr_part(0, 512, 0, "nf0"), sr_part(512, 512, 512, "nf0"), sr_part(1024, 384, 1280, "nf1")]
+            spare = [sr_part(0, 512, 0), sr_part(512, 512, 512), sr_part(1024, 384, 1280)]
         if last:
             def ex_part(i):
                 def run():
-                    gat("a", T.ge[:, 512 * i:512 + 512 * i], T.du[:, 896 + 32 * i:928 + 32 * i], ["duo"], ["ge%d" % i])
+                    gat("a", T.ge[:, 256 * i:256 + 256 * i], T.du[:, 896 + 16 * i:912 + 16 * i], ["duo"], ["ge%d" % i],
+                        bias=127.0)
                 return run
-            spare = [ex_part(i) for i in range(4)]
 
-        def gap():
-            if spare:
-                spare.pop(0)()
+            def ex_scan(i):
+                def run():
+                    scan(T.lo[:, 512 * i:512 * i + 512], T.d0z[:], T.ge[:, 512 * i:512 + 512 * i], ADD, MIN,
+                         ["d0z", "ge%d" % (2 * i), "ge%d" % (2 * i + 1)], ["se%d" % i] + ["lo" + k for k in PAIRS if i == 0])
+                return run
 
-        gap()
-        gap()
-        if t == 0:
-            gap()
+            def ex_min(i):
+                def run():
+                    c = 64 * i + 1 - par
+                    tt(T.yrb[:, c:c + 63:2], T.lo[:, 512 * i + 15:512 * i + 512:16], T.yab[:, 32 * i:32 * i + 32],
+                       MIN, ["se%d" % i, "yab0"], ["yr1%d" % i])
+                return run
+            spare = [ex_part(i) for i in range(8)]
+            vspare = [f(i) for i in range(4) for f in (ex_scan, ex_min)]
+            act(T.yab[:, 0:128], T.AD[:, AB + 1025 - par:AB + 1280:2], ID, ["ADa"], ["yab0"], bias=AOFF)
+
+        def gap(n=1):
+            for i in range(n):
+                if spare:
+                    spare.pop(0)()
+
+        def vgap(n=1):
+            for i in range(n):
+                if vspare:
+                    vspare.pop(0)()
+
+        gap(5)
+
         def date(h):
             a, b = 64 * h, 64 * h + 64
-            mth, k2h, s = ps[4][:, a:b], ps[4][:, 128 + a:128 + b], "_%d" % h
+            mth, s = ps[4][:, a:b], "_%d" % h
+
+            def top():
+                scan(T.ss[:, a:b], T.d0n[:, 0:64], T.tt[:, a:b], ADD, MAX, ["d0n", "tt" + s], ["ss" + s])
+                tt(T.adj[:, a:b], T.tt[:, a:b], ps[4][:, 384:448], ADD, ["tt" + s, "ramp"], ["adj" + s])
+
+            def turn():
+                op("v", lambda: V.transpose(T.tt[:, a:b], T.wtm[:, a:b]), ["wtm" + s], ["tt" + s])
+                ts(T.vr[:, a:b], T.wtm[:, a:b], -VOFF, ADD, ["wtm" + s], ["vr" + s])
+
+            def same():
+                tt(T.mT[:, a:b], T.ss[:, a:b].indirect(T.l15[:, 0:4]), T.adj[:, a:b], EQ, ["ss" + s, "l15", "adj" + s], ["mT" + s])
+                tt(mth, mth, T.vr[:, a:b], SUB, ["mt" + s, "vr" + s], ["mt" + s])
             return [
                 lambda: tt(mth, T.st[:, 16 * a + 15:16 * b:16], ps[2][:, 256 + a:256 + b], MIN,
-                           ["st%d" % (2 * h), "st%d" % (2 * h + 1), "ps2"], ["mt" + s]),
-                lambda: ts(T.wtm[:, a:b], mth, 0.4921875, ADD, ["mt" + s], ["wtm" + s], MAG, ADD),
-                lambda: ts(k2h, T.wtm[:, a:b], MAG, SUB, ["wtm" + s, "c_p16"], ["k2" + s], c_p16, SUB),
-                lambda: op("v", lambda: V.transpose(T.tt[:, a:b], k2h), ["k2" + s], ["tt" + s]),
-                lambda: scan(T.ss[:, a:b], T.d0n[:, 0:64], T.tt[:, a:b], ADD, MAX, ["d0n", "tt" + s], ["ss" + s]),
-                lambda: tt(T.mT[:, a:b], T.ss[:, a:b].indirect(T.l15[:, 0:4]), T.tt[:, a:b], EQ,
-                           ["ss" + s, "l15", "tt" + s], ["mT" + s]),
+                           ["st%d" % i for i in range(4) if cuts[i] < b and cuts[i + 1] > a] + ["ps2"], ["mt" + s]),
+                lambda: ts(T.wtm[:, a:b], mth, VOFF + AFR, ADD, ["mt" + s], ["wtm" + s]),
+                turn,
+                top,
+                same,
                 lambda: op("v", lambda: V.transpose(T.mask[:, a:b], T.mT[:, a:b]), ["mT" + s], ["mask" + s]),
             ]
 
         d0, d1 = date(0), date(1)
-        for f in (lambda: st(0), lambda: st(1), lambda: st(2), d0[0], lambda: st(3), d0[1], d1[0], d0[2], d1[1], d0[3],
-                  d1[2], d0[4], d1[3], d0[5], d1[4], d0[6], d1[5]):
+        for f in (lambda: st(1), lambda: st(0), lambda: st(2), d0[0], lambda: st(3), d0[1], d1[0], d0[2], d1[1], d0[3],
+                  d1[2], d0[4], d1[3], d0[5], d1[4]):
             f()
-        tt(T.xv[:, 0:64], ps[4][:, 128:192], T.mask[:, 0:64], MUL, ["k2_0", "mask_0"], ["xv_0"])
-        d1[6]()
         tt(T.xs[:, 0:64], ps[4][:, 0:64], T.mask[:, 0:64], MUL, ["mt_0", "mask_0"], ["xs_0"])
-        tt(T.xv[:, 64:128], ps[4][:, 192:256], T.mask[:, 64:128], MUL, ["k2_1", "mask_1"], ["xv"])
+        d1[5]()
+        tt(T.xv[:, 0:64], T.vr[:, 0:64], T.mask[:, 0:64], MUL, ["vr_0", "mask_0"], ["xv_0"])
         tt(T.xs[:, 64:128], ps[4][:, 64:128], T.mask[:, 64:128], MUL, ["mt_1", "mask_1"], ["xs"])
+        tt(T.xv[:, 64:128], T.vr[:, 64:128], T.mask[:, 64:128], MUL, ["vr_1", "mask_1"], ["xv"])
 
         CUm = (T.IDh[:], CUp, ["IDh", CUt])
         thm = (T.sel[0:8, :], T.th16[0:8, par::2], ["sel", "th16"])
-        IA = (T.IDb[:], T.ia2[:], ["IDb", "ia2"])
-        NM = (T.IDb[:], T.nm[:], ["IDb", "nm"])
-
-        def E(s):
-            return T.md1[:, s - 1::6]
-
-        def Zm(s):
-            return (T.BO[:], T.z[:, 128 * (s - 1):128 * s], ["BO", "z%d" % s])
-
-        def ym(s):
-            return [CUm, IA] + [Zm(j) for j in range(1, s)]
-
-        def En(s):
-            return (T.BOn[:], E(s), ["BOn", "E%d" % s])
+        IA = (T.P3[:], T.ia2[:], ["P3", "ia2"])
+        NM = (T.P3[:], T.nm[:], ["P3", "nm"])
 
         BB, FB = (0, 3), (1, 2)
         XV, XS = ("xv_0", "xv"), ("xs_0", "xs")
@@ -552,10 +637,10 @@ def rank_program(g, core, T, topo):
             return [n + "_0", n + "_1"]
 
         def Ef(s, m, mt_):
-            return (m, E(s), [mt_] + both("E%d" % s))
+            return (m, T.md1[:, s - 1::6], [mt_] + both("E%d" % s))
 
-        def yf(s):
-            return [CUm, IA] + [(T.BO[:], T.z[:, 128 * (j - 1):128 * j], ["BO"] + both("z%d" % j)) for j in range(1, s)]
+        def FS(s):
+            return (T.IDh[:], T.fs[:, 128 * (s - 1):128 * s], ["IDh"] + both("fs%d" % s))
 
         def half(s, h):
             a, b, x = 64 * h, 64 * h + 64, "_%d" % h
@@ -566,25 +651,26 @@ def rank_program(g, core, T, topo):
                 return (T.BO[:], T.z[:, 128 * (j - 1) + a:128 * (j - 1) + b], ["BO", "z%d" % j + x])
 
             def nv():
-                mm(tB, pB, [(T.BOm[:], T.xv[:, a:b], ["BOm", XV[h]]), (T.BOp[:], T.mask[:, a:b], ["BOp", "mask" + x])], stop=False)
+                mm(tB, pB, [(T.BOm[:], T.xv[:, a:b], ["BOm", XV[h]])], stop=False)
 
             def A():
                 if s > 1:
                     tt(T.xs[:, a:b], T.K[:, 0:1664].indirect(lst), T.mask[:, a:b], MUL, KT + ["fl" + x, "mask" + x], [XS[h]])
-                    act(T.yg[:, a:b], T.AD[:, 0:1664].indirect(lst), ACT.Identity, ADT[0:4] + ["fl" + x], ["yg" + x],
-                        bias=-2048.0)
-                else:
-                    nv()
-                mm(tB, pB, [(T.BO[:], T.xs[:, a:b], ["BO", XS[h]])], start=False)
+                    act(T.yg[:, a:b], T.AD[:, 0:1664].indirect(lst), ID, ADT[0:4] + ["fl" + x], ["yg" + x])
+                mm(tB, pB, [(T.BO[:], T.xs[:, a:b], ["BO", XS[h]])], start=s == 1)
 
             def Y():
                 if s > 1:
                     tt(yph, T.yg[:, a:b], pF, SUB, ["yg" + x, tF], ["yp" + x])
-                mm(tF, pF, [(T.IDh[:], T.CU[:, 128 * par + a:128 * par + b], ["IDh", CUt])] + [zm(j) for j in range(1, s)],
-                   stop=False)
+                    mm(tF, pF, [(T.IDh[:], T.fs[:, 128 * (s - 2) + a:128 * (s - 2) + b], ["IDh", "fs%d" % (s - 1) + x])], stop=False)
+                else:
+                    mm(tF, pF, [(T.IDh[:], T.CU[:, 128 * par + a:128 * par + b], ["IDh", CUt])], stop=False)
 
             def Eq():
-                ts(Eh, pB, c_k, EQ, [tB, "c_k"], ["E%d" % s + x])
+                if s == 1:
+                    ts(Eh, pB, c_k, EQ, [tB, "c_k"], ["E%d" % s + x])
+                else:
+                    ts(Eh, pB, M16, ADD, [tB, "c_k2"], ["E%d" % s + x], c_k2, EQ)
                 if s < 4:
                     nv()
 
@@ -596,17 +682,18 @@ def rank_program(g, core, T, topo):
                 scan(T.sf[:, a:b], T.DD[:, 0:64], pF, ADD, MIN, ["DD", tF], ["sf" + x])
 
             def L():
-                ts(lst, T.sf[:, a + 15:b:16], c_fix, ADD, ["sf" + x, "c_fix"], ["fl" + x], 2048.0, ADD)
+                ts(lst, T.sf[:, a + 15:b:16], c_fix, ADD, ["sf" + x, "c_fix"], ["fl" + x])
+                cp(T.fs[:, 128 * (s - 1) + a:128 * (s - 1) + b], pF, [tF], ["fs%d" % s + x])
             return A, Y, Eq, Z, S, L
 
         def nstep(s, c0):
             mm("ps5", ps[5][:, c0:c0 + 128], [Ef(s, T.BOb[:], "BOb")])
 
         def nact(s, c0):
-            act(T.md0[:, s - 1::6], ps[5][:, c0:c0 + 128], ACT.Identity, ["ps5"], ["md0%d" % (s - 1)], bias=1.0, scale=-1.0)
+            act(T.md0[:, s - 1::6], ps[5][:, c0:c0 + 128], ID, ["ps5"], ["md0%d" % (s - 1)], bias=1.0, scale=-1.0)
 
-        def qmin(bank):
-            tt(T.q[:], T.q[:], ps[bank][:, 0:128], MIN, ["q", "ps%d" % bank], ["q"])
+        def qmin(c0):
+            tt(T.q[:], T.q[:], ps[6][:, c0:c0 + 128], MIN, ["q", "ps6"], ["q"])
 
         for s in (1, 2, 3, 4):
             h0, h1 = half(s, 0), half(s, 1)
@@ -621,152 +708,112 @@ def rank_program(g, core, T, topo):
                 act(T.r16[:], ps[5][:, 0:128], ACT.Relu, ["ps5"], ["r16"], scale=16.0)
                 act(T.mn[:], ps[5][:, 128:256], ACT.Relu, ["ps5"], ["mn"], bias=-111.0)
                 act(T.md0[:, 4::6], T.r16[:], ACT.Sign, ["r16"], ["md04"])
-                act(T.nm[:], T.mask[:], ACT.Identity, ["mask_0", "mask_1"], ["nm"], bias=-512.0, scale=512.0)
+                act(T.nm[:], T.mask[:], ID, ["mask_0", "mask_1"], ["nm"], bias=-512.0, scale=512.0)
             else:
                 if s == 2:
                     act(T.na[:], ps[7][:, 0:128], ACT.Relu, ["ps7"], ["na"], bias=-1.0)
-                    act(T.ia2[:], T.na[:], ACT.Identity, ["na"], ["ia2"], bias=4096.0, scale=-3328.0)
+                    act(T.ia2[:], T.na[:], ID, ["na"], ["ia2"], bias=4096.0, scale=-3328.0)
                 if s == 3:
-                    act(T.q[:], ps[7][:, 0:128], ACT.Identity, ["ps7"], ["q"])
+                    act(T.q[:], ps[7][:, 0:128], ID, ["ps7"], ["q"])
+                    act(T.md1[:, 5::6], ps[7][:, 256:384], ACT.Relu, ["ps7"], ["md15"], bias=16.0)
                     act(T.md1[:, 4::6], ps[5][:, 0:128], ACT.Relu, ["ps5"], ["md14"])
+                    act(T.ok[:], T.md0[:, 4::6], ID, ["md04"], ["ok"], bias=1.0, scale=-1.0)
                 if s == 4:
-                    act(T.md1[:, 5::6], ps[7][:, 0:128], ACT.Relu, ["ps7"], ["md15"], bias=16.0)
-                    act(T.ia[:], T.na[:], ACT.Identity, ["na"], ["ia"], bias=-384.0, scale=-1664.0)
                     nact(2, 0)
                     nact(3, 128)
-                h0[1]()
-                h1[1]()
+                    act(T.ia[:], T.na[:], ID, ["na"], ["ia"], bias=1664.0, scale=-1664.0)
+                    tt(T.oky[:], T.AD[:, 0:1664].indirect(T.fl[:, 0:8]), T.ok[:], MUL, ADT[0:4] + both("fl") + ["ok"], ["oky"])
+                    tt(ps[4][:, 128:256], T.oky[:], ps[6][:, 128:256], ADD, ["oky", "ps6"], ["d4"])
+                    for bank, i in ((6, 0), (7, 128)):
+                        mm("ps%d" % bank, ps[bank][:, 0:128], [(T.row[0:1, i:i + 128], T.one[0:1, :], ["row", "row0", "one"]),
+                                                               (T.IDh[:], T.t3[:], ["IDh"] + both("t3"))], stop=False)
+                gap()
+                if s < 4:
+                    h0[1]()
+                    h1[1]()
             h0[2]()
+            if s == 3:
+                qmin(0)
             h1[2]()
             if s == 4:
-                mm("ps7", ps[7][:, 0:128], yf(4) + [Ef(4, T.BOn[:], "BOn")])
+                h0[1]()
+                h1[1]()
+                for a, x in ((0, "_0"), (64, "_1")):
+                    tt(T.w4[:, a:a + 64], T.md1[:, 6 * a + 3:6 * a + 384:6], ps[4][:, 128 + a:192 + a], MUL, ["E4" + x, "d4"], ["w4" + x])
+                for bank in (6, 7):
+                    mm("ps%d" % bank, ps[bank][:, 0:128], [(T.BO[:], T.w4[:], ["BO"] + both("w4"))], start=False)
             h0[3]()
+            if s == 3:
+                mm("ps6", ps[6][:, 128:256], [FS(2), IA, Ef(3, T.BOn[:], "BOn")])
             h1[3]()
+            if s < 4:
+                vgap(1 if s == 1 else 2)
+            else:
+                vgap()
             if s == 1:
-                mm("ps7", ps[7][:, 0:128], [Ef(1, T.BOb[:], "BOb"), (T.IDb[:], T.md0[:, 4::6], ["IDb", "md04"])])
+                mm("ps7", ps[7][:, 0:128], [Ef(1, T.BOb[:], "BOb"), (T.P3[:], T.md0[:, 4::6], ["P3", "md04"])])
                 if last:
-                    ts(T.yrb[:, par::2], T.wtm[:], 127.0 - MAG, ADD, ["wtm_0", "wtm_1"], ["yr0"])
+                    act(T.yrb[:, par::2], T.wtm[:], ID, ["wtm_0", "wtm_1"], ["yr0"], bias=127.0 - VOFF)
             if s == 2:
                 mm("ps5", ps[5][:, 0:128], [thm] + negv() + [Ef(1, T.BOn[:], "BOn"), NM])
                 mm("ps7", ps[7][:, 0:128], [CUm, Ef(1, T.BOn[:], "BOn"), IA])
-                mm("ps6", ps[6][:, 0:128], [Ef(2, T.BOn[:], "BOn")] + yf(2))
+                mm("ps7", ps[7][:, 256:384], [(T.IDn[:], T.mn[:], ["IDn", "mn"]), (T.IDn[:], T.r16[:], ["IDn", "r16"]), NM])
+                mm("ps6", ps[6][:, 0:128], [Ef(2, T.BOn[:], "BOn"), FS(1), IA])
             if s == 3:
-                qmin(6)
-                mm("ps7", ps[7][:, 0:128], [(T.IDn[:], T.mn[:], ["IDn", "mn"]), (T.IDn[:], T.r16[:], ["IDn", "r16"]), NM])
-                mm("ps6", ps[6][:, 0:128], yf(3) + [Ef(3, T.BOn[:], "BOn")])
+                mm("ps7", ps[7][:, 128:256], [(T.IDp[:], T.md0[:, 4::6], ["IDp", "md04"]), FS(2),
+                                              (T.BO[:], T.z[:, 256:384], ["BO"] + both("z3"))])
                 nstep(2, 0)
                 nstep(3, 128)
+                act(T.n3[:], ps[7][:, 128:256], ACT.Relu, ["ps7"], ["n3"], bias=-4096.0)
             if s == 4:
-                nstep(4, 0)
-                nact(4, 0)
-                qmin(6)
-                qmin(7)
+                nstep(4, 256)
+                nact(4, 256)
             else:
                 h0[4]()
                 h1[4]()
+                if s == 3:
+                    qmin(128)
                 h0[5]()
                 h1[5]()
-
-        for s in ():
-            fb = 1 + (s + 1) % 2
-            pb = 1 + s % 2
-            if s > 1:
-                tt(T.xs[:], T.K[:, 0:1664].indirect(T.fl[:, 0:8]), T.mask[:], MUL, KT + ["fl", "mask_0", "mask_1"], ["xs", "xs_0"])
-                act(T.yg[:], T.AD[:, 0:1664].indirect(T.fl[:, 0:8]), ACT.Identity, ADT[0:4] + ["fl"], ["yg"], bias=-2048.0)
-            else:
-                mm("ps0", ps[0][:, 0:128], negv(), stop=False)
-            mm("ps0", ps[0][:, 0:128], [(T.BO[:], T.xs[:], ["BO", "xs", "xs_0"])], start=False)
-            if s == 1:
-                mm("ps5", ps[5][:, 0:128], [thm] + negv())
-                mm("ps5", ps[5][:, 128:256], negv())
-                mm("ps1", ps[1][:, 0:128], [CUm], stop=False)
-                act(T.r16[:], ps[5][:, 0:128], ACT.Relu, ["ps5"], ["r16"], scale=16.0)
-                act(T.md0[:, 4::6], T.r16[:], ACT.Sign, ["r16"], ["md04"])
-                act(T.mn[:], ps[5][:, 128:256], ACT.Relu, ["ps5"], ["mn"], bias=-111.0)
-                act(T.nm[:], T.mask[:], ACT.Identity, ["mask_0", "mask_1"], ["nm"], bias=-512.0, scale=512.0)
-            if s == 2:
-                mm("ps6", ps[6][:, 0:128], [(T.BOb[:], E(1), ["BOb", "E1"]), (T.IDb[:], T.md0[:, 4::6], ["IDb", "md04"])])
-                act(T.na[:], ps[6][:, 0:128], ACT.Relu, ["ps6"], ["na"], bias=-1.0)
-                act(T.ia2[:], T.na[:], ACT.Identity, ["na"], ["ia2"], bias=4096.0, scale=-3328.0)
-                mm("ps7", ps[7][:, 0:128], [thm] + negv() + [En(1), NM])
-                act(T.md1[:, 4::6], ps[7][:, 0:128], ACT.Relu, ["ps7"], ["md14"])
-            if s == 3:
-                mm("ps6", ps[6][:, 0:128], [CUm, En(1), IA])
-                act(T.q[:], ps[6][:, 0:128], ACT.Identity, ["ps6"], ["q"])
-                mm("ps3", ps[3][:, 0:128], [En(2)] + ym(2))
-                act(T.md1[:, 5::6], ps[7][:, 0:128], ACT.Relu, ["ps7"], ["md15"], bias=16.0)
-            if s == 4:
-                mm("ps6", ps[6][:, 0:128], ym(4), stop=False)
-                act(T.ia[:], T.na[:], ACT.Identity, ["na"], ["ia"], bias=-384.0, scale=-1664.0)
-            if s > 1:
-                tt(yp, T.yg[:], ps[pb][:, 0:128], SUB, ["yg", "ps%d" % pb], ["yp"])
-            ts(E(s), ps[0][:, 0:128], c_k, EQ, ["ps0", "c_k"], ["E%d" % s])
-            if s == 4:
-                mm("ps6", ps[6][:, 0:128], [En(4)], start=False)
-            tt(T.z[:, 128 * (s - 1):128 * s], E(s), yp, MUL, ["E%d" % s, "yp"], ["z%d" % s])
-            mm("ps%d" % fb, ps[fb][:, 0:128], [Zm(s)], start=False)
-            if s > 1:
-                mm("ps5", ps[5][:, 0:128], [(T.BOb[:], E(s), ["BOb", "E%d" % s])])
-                act(T.md0[:, s - 1::6], ps[5][:, 0:128], ACT.Identity, ["ps5"], ["md0%d" % (s - 1)], bias=1.0, scale=-1.0)
-            if s == 1 and last:
-                ts(T.yrb[:, par::2], T.wtm[:], 127.0 - MAG, ADD, ["wtm_0", "wtm_1"], ["yr0"])
-            if s >= 3:
-                tt(T.q[:], T.q[:], ps[3][:, 0:128], MIN, ["q", "ps3"], ["q"])
-            if s == 4:
-                tt(T.q[:], T.q[:], ps[6][:, 0:128], MIN, ["q", "ps6"], ["q"])
-            if s < 4:
-                mm("ps0", ps[0][:, 0:128], negv(), stop=False)
-                mm("ps%d" % pb, ps[pb][:, 0:128], [CUm] + [Zm(j) for j in range(1, s + 1)], stop=False)
-                if s == 2:
-                    mm("ps7", ps[7][:, 0:128], [(T.IDn[:], T.mn[:], ["IDn", "mn"]), (T.IDn[:], T.r16[:], ["IDn", "r16"]), NM])
                 if s == 3:
-                    mm("ps3", ps[3][:, 0:128], ym(3) + [En(3)])
-                scan(T.sf[:], T.DD[:, 0:128], ps[fb][:, 0:128], ADD, MIN, ["DD", "ps%d" % fb], ["sf"])
-                ts(T.fl[:], T.sf[:, 15::16], c_fix, ADD, ["sf", "c_fix"], ["fl"], 2048.0, ADD)
+                    for h, x in enumerate(both("t3")):
+                        tt(T.t3[:, 64 * h:64 * h + 64], T.q[:, 64 * h:64 * h + 64], ps[FB[h]][:, 0:64], MIN,
+                           ["q", "ps%d" % FB[h]], [x])
+                    mm("ps6", ps[6][:, 128:256], [(T.IDm[:], T.md0[:, 4::6], ["IDm", "md04"]), (T.IDh[:], T.n3[:], ["IDh", "n3"]),
+                                                  (T.IDk[:], T.t3[:], ["IDk"] + both("t3"))])
 
-        tt(T.tf[:, 0:64], T.q[:, 0:64], ps[1][:, 0:64], MIN, ["q", "ps1"], ["tf0a"])
-        tt(T.tf[:, 64:128], T.q[:, 64:128], ps[2][:, 0:64], MIN, ["q", "ps2"], ["tf0"])
-        tt(T.tf[:, 128:192], T.ia[:, 0:64], ps[1][:, 0:64], MAX, ["ia", "ps1"], ["tf1a"])
-        scan(T.tfs[:, 0:128], T.DD[:], T.tf[:, 0:128], ADD, MIN, ["DD", "tf0", "tf0a"], ["tfs"])
-        tt(T.tf[:, 192:256], T.ia[:, 64:128], ps[2][:, 0:64], MAX, ["ia", "ps2"], ["tf1"])
-        ts(T.tw[:], T.tfs[:, 15:128:16], c_fix, ADD, ["tfs", "c_fix"], ["tw"])
-        for a in range(NVC, 8):
-            o, n = 8 * a * (a + 1), 16 * (a + 1)
-            op("a", lambda: g.scalar.activation(T.cmp[:, o:o + n], T.tf[:, 0:n], ACT.Abs, bias=T.tw[:, a:a + 1], scale=-1.0),
-               ["tf0", "tf0a", "tw"], ["cmp%d" % a])
-        ts(T.tl[:, 0:8], T.tfs[:, 15:128:16], c_fix, ADD, ["tfs", "c_fix"], ["tl"], 3328.0, ADD)
-        scan(T.tfs[:, 128:256], T.DD[:], T.tf[:, 128:256], ADD, MIN, ["DD", "tf1", "tf1a"], ["tfs2"])
-        tt(T.wd1[:, 0::2], T.tw[:], T.dum2[:], SUB, ["tw", "dum2"], ["wd1"])
-        ts(T.tl[:, 8:16], T.tfs[:, 143::16], c_fix, ADD, ["tfs2", "c_fix"], ["tl2"], 2048.0, ADD)
-        act(T.old[:], T.AD[:, 0:2944].indirect(T.tl[:, 0:8]), ACT.Identity, ADT + ["tl"], ["old"])
-        gap()
-        gap()
-        for a in range(NVC):
-            o, n = 8 * a * (a + 1), 16 * (a + 1)
-            ts(T.cmp[:, o:o + n], T.tf[:, 0:n], T.tw[:, a:a + 1], NE, ["tf0", "tw"], ["cmp%d" % a])
+        scan(T.tfs[:, 0:128], T.DD[:], ps[6][:, 0:128], ADD, MIN, ["DD", "ps6"], ["tfs"])
+        tt(T.tf[:, 0:64], T.ia[:, 0:64], ps[1][:, 0:64], MAX, ["ia", "ps1"], ["tf1a"])
+        tt(T.tf[:, 64:128], T.ia[:, 64:128], ps[2][:, 0:64], MAX, ["ia", "ps2"], ["tf1"])
+        for a in range(8):
+            o, n, own = 8 * a * (a + 1), 16 * (a + 1), T.tfs[:, 16 * a + 15:16 * a + 16]
+            if a < 8 - NVC:
+                act(T.cmp[:, o:o + n], ps[7][:, 0:n], ACT.Abs, ["ps7", "tfs"], ["cmp%d" % a], bias=own, scale=-1.0)
+            else:
+                ts(T.cmp[:, o:o + n], ps[6][:, 0:n], own, SUB, ["ps6", "tfs", "c_fix"], ["cmp%d" % a], c_fix, NE)
+        ts(T.tl[:, 0:8], T.tfs[:, 15:128:16], 8192.0 + AB, ADD, ["tfs"], ["tl"])
+        scan(T.tfs[:, 128:256], T.DD[:], T.tf[:], ADD, MIN, ["DD", "tf1", "tf1a"], ["tfs2"])
+        act(T.old[:], T.AD[:, 0:2944].indirect(T.tl[:, 0:8]), ID, ADT + ["tl"], ["old"])
+        tt(T.wd1[:, 0::2], T.tfs[:, 15:128:16], T.dum2[:], SUB, ["tfs", "dum2"], ["wd1"])
+        ts(T.tl[:, 8:16], T.tfs[:, 143::16], c_fix, ADD, ["tfs2", "c_fix"], ["tl2"])
+        scan(T.cs[:], T.DQ[:], T.cmp[:], ADD, MIN, DQT + ["cmp%d" % a for a in range(8)], ["cs"])
         scan(T.ms[:], T.md0[:], T.md1[:], MUL, ADD,
              ["md0c", "md0d", "md01", "md02", "md03", "md04", "md14", "md15"] + both("E1") + both("E2") + both("E3") + both("E4"), ["ms"])
-        tt(T.yy[:], T.SR[:, 0:1672].indirect(T.tl[:, 8:16]), T.ms[:, 5::6], MUL, SRT + ["tl2", "ms"], ["yy"])
-        scan(T.cs[:], T.DQ[:], T.cmp[:], ADD, MIN, DQT + ["cmp%d" % a for a in range(8)], ["cs"])
         ts(T.wd0[:, 1::2], T.cs[:, 0:576].indirect(T.lend[:, 0:1]), c_win, EQ, ["cs", "lend", "c_win"], ["win"])
+        vgap()
         scan(T.win[:], T.wd0[:, 0:16], T.wd1[:], MUL, ADD, ["win", "wd0c", "wd1", "wd1c"], ["l2"])
+        tt(T.yy[:], T.SR[:, 0:1672].indirect(T.tl[:, 8:16]), T.ms[:, 5::6], MUL, SRT + ["tl2", "ms"], ["yy"])
+        vgap()
+        if last:
+            dma("s", T.yr[:], T.yrb[:], "st", ["yr0"] + ["yr1%d" % i for i in range(4)], [], 16)
         cp(T.ll[:], T.win[:, 1::2], ["l2"], ["ll"])
         tt(T.AD[:, 0:2944].indirect(T.ll[:, 0:8]), T.old[:], T.yy[:], SUB, ["ll", "old", "yy"] + ADT, ADT)
 
-    dma("s", T.yd[:], T.AD[:, 256:1280], "st", ["ADd"], [], 16)
-    for i in range(2):
-        act(T.yab[:, 640 * i:640 * i + 640], T.AD[:, AB + 640 * i:AB + 640 * i + 640], ACT.Identity, ["ADa0", "ADa"],
-            ["yab%d" % i], bias=AOFF)
-        dma("s", T.ya[:, 640 * i:640 * i + 640], T.yab[:, 640 * i:640 * i + 640], "st", ["yab%d" % i], [], 32 + 16 * i)
-    for i in range(2):
-        scan(T.sm[:, 1024 * i:1024 * i + 1024], T.d0t[:, 0:1024], T.ge[:, 1024 * i:1024 + 1024 * i], ADD, MIN,
-             ["d0t", "ge%d" % (2 * i), "ge%d" % (2 * i + 1)], ["se%d" % i])
-    opar = 1 - ((NP - 1) & 1)
-    tt(mt, T.sm[:, 15:2048:16], T.AD[:, AB + 1024 + opar:AB + 1280:2], MIN, ["se0", "se1", "ADa"], ["mt", "mt_0", "mt_1"])
-    ts(T.wtm[:], mt, 0.4921875, ADD, ["mt"], ["wtm", "wtm_0", "wtm_1"], MAG, ADD)
-    ts(T.yrb[:, opar::2], T.wtm[:], 127.0 - MAG, ADD, ["wtm"], ["yr1"])
-    dma("a", T.yr[:], T.yrb[:], "st", ["yr0", "yr1"], [], 64)
+    dma("s", T.yd[:], T.AD[:, 256:1280], "st", ["ADd"], [], 32)
+    ts(T.yab[:, 0:672], T.AD[:, AB:AB + 672], AOFF, ADD, ["ADa0", "ADa"], ["yab0"])
+    act(T.yab[:, 672:1280], T.AD[:, AB + 672:AB + 1280], ID, ["ADa"], ["yab1"], bias=AOFF)
+    dma("a", T.ya[:], T.yab[:], "st", ["yab0", "yab1"], [], 48)
     g.wait_ge(T.sem.sent, sent[0])
     for e in ("v", "a", "p", "g"):
         g.wait_ge(T.sem[SEM[e]], cnt[e])
-    g.wait_ge(T.sem.st, 64)
+    g.wait_ge(T.sem.st, 48)

@@ -13,13 +13,16 @@ VOFF = 1152.0
 M16 = 786432.0
 AB = 1280
 NP = 4
-NVC = 3
+WORDER = "B4 B5 own A0 A1 B2 B3 R3 S0 S1 S2 S3 S4 S5 S6 n4 R1 R2 I3 V7 I1 I2 tl Z3 wd Z1 Z2 old cs f4 ms win tl2 sel yy ll put"
+WLAST = "own n4 S0 S1 S2 S3 V7 V6 V5 V4 tl f4 old wd tl2 cs ms win gap sel yy gap yr ll put"
 PAIRS = "ab"
 SEG = [("a", 88), ("b", 68), ("w", 76), ("e", 24)]
 GRP = {"a": ("ab", 0), "b": ("w", 1)}
-ORDER = "v3 h2 h1 l2 k3 l1 c2 r3 c1 r2 Ha Hb Pw La Pe r1 S Lb Ca Cb Ga Cw Gb Ma Ce Mb A Me W We Wg"
-LH = "a"
-TCUT = [0, 48, 84, 112, 128]
+FIRST = "s1 v3 Da v2 k1 k3 Ha Hb r1 k2 r3 Pw La Pe r2 "
+START = "v3 h2 h1 l2 k3 l1 c2 r3 c1 r2 Ha Hb Pw La Pe r1 "
+ORDER = "Ds Dr S Lb Ca Cb Ga Cw Gb Dp Ka Ce A Dm Wa Wb Dq We Wg Kb Ke Dv"
+WSZ = 1680
+TCUT = [0, 52, 88, 112, 128]
 
 f32, bf, i32, u16 = "float32", "bfloat16", "int32", "uint16"
 
@@ -31,28 +34,30 @@ def _sb(n, d):
 SCRATCH = {
     "avs": _sb(1280, bf), "dpi": _sb(1024, i32), "bdi": _sb(24, i32), "sbi": _sb(88, i32), "thi": _sb(16, i32),
     "s16a": _sb(88, H), "th16a": _sb(16, H), "wd0": _sb(32, f32), "wd1": _sb(16, f32),
-    "AD": _sb(2944, f32), "W": _sb(1672, f32), "K": _sb(1664, f32), "SR": _sb(1672, f32),
+    "AD": _sb(2944, f32), "W": _sb(2 * WSZ, i32), "K": _sb(1664, f32), "SR": _sb(1672, f32),
     "s16": _sb(1408, H), "th16": _sb(256, H), "nf": _sb(88, f32), "nf2": _sb(88, f32), "nf3": _sb(88, f32),
-    "one": _sb(128, bf), "cst": _sb(256, bf), "lh": _sb(768, H), "hi": _sb(2048, bf), "lo": _sb(2048, bf),
-    "h32": _sb(512, f32), "l32": _sb(512, f32), "s32": _sb(512, f32), "SL": _sb(512, H), "d0e": _sb(704, bf),
-    "bdu": _sb(24, u16), "bd2": _sb(24, u16), "du": _sb(1024, u16), "dupo": _sb(288, u16), "dh": _sb(192, H), "adup": _sb(288, bf),
+    "one": _sb(128, bf), "cst": _sb(256, bf), "lh": _sb(352, H), "hi": _sb(2048, bf), "lo": _sb(2048, bf),
+    "h32": _sb(512, f32), "s32": _sb(512, f32), "SL": _sb(512, H), "d0e": _sb(704, bf),
+    "bdu": _sb(24, u16), "bd2": _sb(24, u16), "du": _sb(1024, u16), "dupo": _sb(288, u16), "adup": _sb(288, bf),
     "gd": _sb(1536, bf), "sd": _sb(1536, bf), "gm": _sb(2048, bf), "sm": _sb(2048, H), "sp": _sb(2048, H),
     "gt": _sb(2048, bf), "st": _sb(2048, H), "ge": _sb(2048, bf),
     "rl": _sb(16 * 96, bf), "gl": _sb(16 * 96, bf),
     "J": _sb(128, bf), "JG": _sb(128, bf), "JR": _sb(128, bf),
-    "pi": _sb(8, i32), "col": _sb(24, f32), "tmp": _sb(128, f32), "tmp2": _sb(128, f32),
+    "pi": _sb(8, i32), "col": _sb(24, f32),
     "BO": _sb(128, H), "BOm": _sb(128, H), "IDh": _sb(128, H), "sel": _sb(128, H), "CU": _sb(256, H),
-    "BOb": _sb(128, bf), "BOn": _sb(128, bf), "BOp": _sb(128, H), "IDb": _sb(128, bf), "IDn": _sb(128, bf),
+    "BOb": _sb(128, bf), "BOn": _sb(128, bf), "IDn": _sb(128, bf),
     "P1": _sb(128, bf), "P2": _sb(128, bf), "P3": _sb(128, bf), "ia2": _sb(128, bf), "dum2": _sb(8, f32),
     "d0t": _sb(1216, bf), "d0z": _sb(512, bf), "d0p": _sb(256, bf), "d0n": _sb(64, bf), "DD": _sb(128, bf), "DQ": _sb(576, bf),
-    "l15": _sb(8, u16), "lend": _sb(8, u16), "dum": _sb(8, f32),
+    "l15": _sb(8, u16), "lend": _sb(8, u16),
     "wtm": _sb(128, H), "tt": _sb(128, H), "ss": _sb(128, f32), "adj": _sb(128, f32),
     "mT": _sb(128, H), "mask": _sb(128, H), "xv": _sb(128, H), "xs": _sb(128, H),
     "yg": _sb(128, f32), "z": _sb(512, H), "sf": _sb(128, f32), "fl": _sb(8, u16),
     "md0": _sb(768, bf), "md1": _sb(768, bf), "ms": _sb(768, bf),
     "r16": _sb(128, bf), "mn": _sb(128, bf), "nm": _sb(128, bf), "na": _sb(128, bf),
-    "ia": _sb(128, bf), "q": _sb(128, f32), "tf": _sb(128, f32), "tfs": _sb(256, f32),
+    "ia": _sb(128, bf), "q": _sb(128, f32), "tfs": _sb(256, f32),
     "IDm": _sb(128, bf), "IDp": _sb(128, bf), "IDk": _sb(128, H), "row": _sb(256, bf), "ok": _sb(128, bf),
+    "rc": _sb(768, bf), "rs": _sb(768, bf), "d0r": _sb(256, bf), "ri": _sb(8, u16), "bk": _sb(432, bf), "bdf": _sb(16, f32),
+    "rz": _sb(384, i32), "PX": _sb(512, H),
     "fs": _sb(384, H), "vr": _sb(128, bf), "t3": _sb(128, H), "n3": _sb(128, H), "oky": _sb(128, H), "w4": _sb(128, H),
     "tl": _sb(16, u16), "cmp": _sb(576, bf), "cs": _sb(576, bf), "win": _sb(16, f32),
     "ll": _sb(8, u16), "old": _sb(128, f32), "yy": _sb(128, f32),
@@ -180,10 +185,11 @@ def rank_program(g, core, T, topo):
     ID = ACT.Identity
     ps = [T["ps%d" % b] for b in range(8)]
     ADT = ["ADj", "ADd", "ADa0", "ADa", "ADk"]
-    WT = ["W0", "W1", "W2", "W3", "Wg0", "Wg1", "Wg2", "Wg3", "Wx", "Wy", "Wb1", "Wb2", "Wb3"]
+    WL = ["W%s%d" % (k, l) for k in "abe" for l in (1, 2, 3)] + ["Wx"]
+    WT = ["W0", "Wg0", "Wg1", "Wg2", "Wg3", "Wy"] + WL
     KT = ["Kx0", "Kx"] + ["K%s%d" % (k, l) for k in "abe" for l in (1, 2, 3)]
     SRT = ["SR0", "SR512", "SR1024", "SRa", "SRb"]
-    BD2 = ["bd20", "bd21", "bd22", "bd30", "bd31", "bd32"]
+    BD2 = ["bd20", "bd21", "bd22"]
 
     at, size = {}, dict(SEG)
     c0 = 0
@@ -217,9 +223,8 @@ def rank_program(g, core, T, topo):
             m |= 1 << e
         return m
 
-    def send(x):
-        r0 = 96 * x
-        sync("g", ["rl%d" % x], [])
+    def send(x, src, dst, rd, wr):
+        sync("g", rd, [])
         trs = []
         n = len(topo.engines(core, peers[2]))
         for d in (1, 2):
@@ -230,26 +235,33 @@ def rank_program(g, core, T, topo):
             rid, pid = topo.addr(peers[d - 1], core)
             trs.append(RemoteDMATransfer(dst_ids=[DstId(rid=rid, pnc=pid)], dma_engine_mask=emask(es),
                                          remote_sem=T.sem["arr%d" % x],
-                                         src=T.rl[:, r0 + 32 * (d - 1):r0 + 32 * d],
-                                         dst=T.gl[:, r0 + 32 * (d - 1):r0 + 32 * d]))
+                                         src=src(d), dst=dst(d)))
         g.remote_dma_fused(trs, local_sem=T.sem.sent)
         rid, pid = topo.addr(peers[2], core)
-        g.remote_dma(T.gl[:, r0 + 64:r0 + 96], T.rl[:, r0 + 64:r0 + 96], T.sem["arr%d" % x], T.sem.sent,
-                     pid, rid, topo.mask(core, peers[2]))
-        tok["gl%d" % x] = {"w": ("arr%d" % x, n), "r": {}}
+        g.remote_dma(dst(3), src(3), T.sem["arr%d" % x], T.sem.sent, pid, rid, topo.mask(core, peers[2]))
+        tok[wr] = {"w": ("arr%d" % x, n), "r": {}}
         return n
 
-    def send1(x, d):
-        c0 = 32 * (d - 1)
-        src = T.rl[:, 96 * x + c0:96 * x + c0 + 32]
+    def block(buf, c0):
+        return lambda d: buf[:, c0 + 32 * (d - 1):c0 + 32 * d]
+
+    def send1(x, d, src, dst, rd):
         rid, pid = topo.addr(peers[d - 1], core)
-        sync("g", ["rl%d_%d" % (x, d)], [])
-        g.remote_dma(T.gl[:, 96 * x + c0:96 * x + c0 + 32], src, T.sem["arr%d" % x], T.sem.sent,
-                     pid, rid, topo.mask(core, peers[d - 1]))
+        sync("g", [rd], [])
+        g.remote_dma(dst, src, T.sem["arr%d" % x], T.sem.sent, pid, rid, topo.mask(core, peers[d - 1]))
         return len(topo.engines(core, peers[d - 1]))
 
     def ghosts(x, l):
-        act(T.W[:, 1280 + 96 * l:1376 + 96 * l], ps[7][:, 0:96], ID, ["ps7"], ["Wg%d" % l])
+        a = WSZ * win[0] + 1280 + 96 * l
+        act(T.W[:, a:a + 96], ps[7][:, 0:96], ID, ["ps7"], wt("Wg%d" % l))
+
+    def fill(w):
+        for a, n, names in ((256, 1024, WL), (1376, 296, ("Wg1", "Wg2", "Wg3", "Wy"))):
+            out, names = T.W[:, WSZ * w + a:WSZ * w + a + n], [x + "/%d" % w for x in names]
+            if w == 0:
+                act(out, T.avs[:, 256:256 + n], ID, ["av1"], names, bias=128.0, scale=0.0)
+            else:
+                iota(out, [[0, n]], 128, 0, names, fl=False)
 
     def landed(x):
         for d in (1, 2, 3):
@@ -257,13 +269,19 @@ def rank_program(g, core, T, topo):
             mm("ps7", ps[7][:, c0:c0 + 32], [(T["P%d" % d][:], T.gl[:, 96 * x + c0:96 * x + c0 + 32],
                                               ["P%d" % d, "gl%d" % x])])
 
-    Wall = T.W[:, 0:1672]
+    win = [0]
+
+    def wt(*names):
+        return [n + "/%d" % win[0] for n in names]
+
+    def worth(offs):
+        return T.W[:, WSZ * win[0]:WSZ * win[0] + 1672].indirect(offs)
 
     def gat(e, out, offs, otok, wtok, bias=0.0):
         if e == "v":
-            cp(out, Wall.indirect(offs), WT + otok, wtok)
+            cp(out, worth(offs), wt(*WT) + otok, wtok)
         else:
-            act(out, Wall.indirect(offs), ID, WT + otok, wtok, bias=bias)
+            act(out, worth(offs), ID, wt(*WT) + otok, wtok, bias=bias)
 
     col = T.col
     c_pr, c_pg, c_sb, c_p16, c_k, c_fix, c_win, c_pr1, c_np16 = [col[:, i:i + 1] for i in range(9)]
@@ -290,8 +308,7 @@ def rank_program(g, core, T, topo):
         ts(c_lo, c_pr, 8.0, ALU.is_lt, ["c_r"], ["c_lo"])
         ts(c_hi, c_pr, 8.0, ALU.is_ge, ["c_r"], ["c_hi"])
         for l in range(3):
-            ts(T.bd2[:, 4 * l:4 * l + 4], T.bdi[:, 6 * l + 6:6 * l + 10], float(256 * l), ADD, ["bdi"], ["bd2%d" % l])
-            ts(T.bd2[:, 12 + 2 * l:14 + 2 * l], T.bdi[:, 6 * l + 10:6 * l + 12], float(256 * l), ADD, ["bdi"], ["bd3%d" % l])
+            ts(T.bd2[:, 6 * l:6 * l + 6], T.bdi[:, 6 * l + 6:6 * l + 12], float(256 * l), ADD, ["bdi"], ["bd2%d" % l])
         for i, (a, b) in enumerate(((c_p, c_lo), (c_up, c_lo), (c_dn, c_hi), (c_p, c_hi))):
             ts(T.SL[:, 128 * i:128 * i + 128], T.J[:], a, EQ, ["J", "c_p", "c_lo", "c_hi"], ["SL%d" % i], b, MUL)
         ts(c_g1, c_pr, 2.0, MUL, ["c_r", "c_p"], ["c_g1"], c_p, SUB)
@@ -322,13 +339,27 @@ def rank_program(g, core, T, topo):
         if part == 1:
             mm("ps3", ps[3][:, 128:256], [(T.P3[:], T.r16[:], ["P3", "r16"]), (T.P3[:], T.mn[:], ["P3", "mn"])])
             act(T.DD[:], ps[3][:, 128:256], ID, ["ps3"], ["DD"])
+            for d in (1, 2):
+                act(T.PX[:, 128 * d - 128:128 * d], T["P%d" % d][:], ID, ["P%d" % d], ["PX%d" % d])
+        if part == 4:
+            for d in (1, 2):
+                mm("ps6", ps[6][:, 2 * d - 2:2 * d], [(T["P%d" % d][:], T.na[:, 2 * d - 2:2 * d], ["P%d" % d, "na"])])
+                mm("ps6", ps[6][:, 32 * d:32 * d + 32], [(T["P%d" % d][:], block(T.rl, 0)(d), ["P%d" % d, "rl0"])])
+                mm("ps6", ps[6][:, 128 * d:128 * d + 128], [(T.BO[:], T.PX[:, 128 * d - 128:128 * d], ["BO", "PX%d" % d])])
+            act(T.bdf[:, 8:12], ps[6][:, 0:4], ID, ["ps6"], ["bdf0"], scale=-128.0)
+            act(T.bdf[:, 0:4], ps[6][:, 0:4], ID, ["ps6"], ["bdf1"])
+            act(T.rz[:, 0:64], ps[6][:, 32:96], ID, ["ps6"], ["rz0_1", "rz0_2"])
+            act(T.rz[:, 64:96], T.rl[:, 64:96], ID, ["rl0"], ["rz0_3"])
+            act(T.PX[:, 256:512], ps[6][:, 128:384], ID, ["ps6"], ["PB1", "PB2"])
             act(T.CU[:, 128:256], T.J[:], ID, ["J"], ["CU1"], bias=1025.0, scale=2.0)
-        made = ((("IDk", "P3", -1.0), ("IDn", "P3", -1.0)), (("BOm", "BO", -1.0), ("BOb", "BO", 1.0), ("BOn", "BO", -2048.0)),
-                (("IDm", "P3", -float(AB)), ("IDp", "P3", 4096.0)))
+        made = ((), (("BOm", "BO", -1.0), ("BOb", "BO", 1.0), ("BOn", "BO", -2048.0)),
+                (("IDk", "P3", -1.0), ("IDn", "P3", -1.0), ("IDm", "P3", -float(AB)), ("IDp", "P3", 4096.0)), ())
         for nme, src, c in made[part - 1]:
             act(T[nme][:], T[src][:], ID, [src], [nme], scale=c)
 
     def setup_sub():
+        ts(T.bdf[:, 4:6], T.bdi[:, 4:6], c_fix, ADD, ["bdi", "c_fix"], ["bdf2"], -8192.0, ADD)
+        cp(T.na[:, 0:4], T.bdi[:, 0:4], ["bdi"], ["na"])
         ts(T.th16a[:], T.thi[:], -127.0, ADD, ["thi"], ["th16a"])
         ts(T.nf[:], T.nf2[:], 1024.0, ALU.is_ge, ["nf2"], ["nf"], 256.0, MUL)
         tt(T.nf3[:], T.sbi[:], T.nf2[:], SUB, ["sbi", "nf2"], ["nf3"])
@@ -352,10 +383,14 @@ def rank_program(g, core, T, topo):
             iota(T.md0[:, 0::6], [[0, 128]], 0, 0, ["md0c"])
             iota(T.md0[:, 5::6], [[0, 128]], -1, 0, ["md0d"])
             iota(T.wd0[:, 0::2], [[0, 16]], 0, 0, ["wd0c"])
+            iota(T.bk[:], [[0, 432]], 0, 0, ["bk0", "bk1", "bk2", "bk3"])
+            iota(T.d0r[:], [[0, 256]], -1, 0, ["d0r"])
+            iota(T.d0r[:, 0::128], [[0, 2]], 1 << 20, 0, ["d0r"])
             iota(T.DQ[:], [[0, 576]], 8192, 0, ["DQ"])
             for a in range(8):
                 o, n = 8 * a * (a + 1), 16 * (a + 1)
                 sel(T.DQ[:, o:o + n], T.DQ[:, o:o + n], [[1, n]], EQ, -1.0 / 128, 0, 0, ["DQ"], ["DQ%d" % a])
+            fill(1)
 
     mt, yp = ps[4][:, 0:128], ps[4][:, 256:384]
     DQT = ["DQ%d" % a for a in range(8)]
@@ -370,77 +405,92 @@ def rank_program(g, core, T, topo):
                [(T.SL[:, 128 * (2 * half + i):128 * (2 * half + i) + 128], src[:, b + i:b + 2 * n:2],
                  ["SL%d" % (2 * half + i), tk]) for i in (0, 1)])
 
-    def pair_mm(l):
-        bank, o, b = (5, 0, 0) if l == 1 else (6, 256 * (l - 2), 256 * (l - 1))
-        pairs(bank, o, T.lh, b, npair, "lh%d" % l)
-
-    def pair_cp(l):
-        bank, o, b = (5, 0, 0) if l == 1 else (6, 256 * (l - 2), 256 * (l - 1))
-        cp(T.du[:, b:b + 2 * npair], ps[bank][:, o:o + 2 * npair], ["ps%d" % bank], ["du%d" % l])
-
     for t in range(NP):
         par = t & 1
         x = 4 * t
         last = t == NP - 1
+        win[0] = par
+        wo = WSZ * par
         if t == 0:
             cp(T.bdu[:], T.bdi[:], ["bdi"], ["bdu"])
             setup_first()
             ts(T.rl[:, 0:96], T.avs[:, 0:256].indirect(T.bdu[:, 0:6]), -127.0, ADD, ["av0", "bdu"], ["rl0"])
-        else:
-            ts(T.rl[:, 96 * x:96 * x + 96], T.AD[:, AB:AB + 256].indirect(T.bdu[:, 0:6]), AFR, ADD,
-               ["ADa0", "bdu"], ["rl%d" % x])
-        sent[0] += send(x)
+            sent[0] += send(x, block(T.rl, 0), block(T.gl, 0), ["rl0"], "gl0")
         links, lo_, ltok = (T.dpi, 0, "dpi") if t == 0 else (T.AD, 256, "ADd")
 
-        def lh(l):
-            a, n = 256 * (l - 1), 2 * npair
-            if t == 0 or LH == "v":
-                cp(T.lh[:, a:a + n], links[:, lo_ + a:lo_ + a + n], [ltok], ["lh%d" % l])
-            else:
-                act(T.lh[:, a:a + n], links[:, lo_ + a:lo_ + a + n], ID, [ltok], ["lh%d" % l])
-
-        def whole(l):
-            a = 256 * (l - 1) + 2 * npair
-            cp(T.du[:, a:256 * l], links[:, lo_ + a:lo_ + 256 * l], [ltok], ["dw%d" % l])
-
         if t == 0:
-            act(T.W[:, 0:256], T.avs[:, 0:256], ID, ["av0"], ["W0"], bias=-127.0)
+            act(T.W[:, 0:256], T.avs[:, 0:256], ID, ["av0"], wt("W0"), bias=-127.0)
             setup_cols()
             setup_lists()
-            act(T.adup[:], T.avs[:, 256:1024].indirect(T.bd2[:, 0:18]), ID, ["av1"] + BD2, ["adup"], bias=-127.0)
-            act(T.W[:, 256:1280], T.avs[:, 256:1280], ID, ["av1"], ["W1", "W2", "W3", "Wx", "Wb1", "Wb2", "Wb3"],
-                bias=128.0, scale=0.0)
-            act(T.W[:, 1376:1672], T.avs[:, 256:552], ID, ["av1"], ["Wg1", "Wg2", "Wg3", "Wy"], bias=128.0, scale=0.0)
+            act(T.adup[:], T.avs[:, 256:1024].indirect(T.bd2[:, 0:18]), ID, ["av1"] + BD2,
+                ["adup1", "adup2", "adup3"], bias=-127.0)
+            fill(0)
             act(T.AD[:, AB:AB + 1280], T.avs[:], ID, ["av0", "av1"], ["ADa0", "ADa"], bias=-AOFF)
             act(T.CU[:, 0:128], T.J[:], ID, ["J"], ["CU0"], bias=1024.0, scale=2.0)
-        cp(T.dh[:], links[:, lo_:lo_ + 768].indirect(T.bd2[:, 0:12]), [ltok] + BD2, ["dh"])
-        cp(T.dupo[:, 192:288], links[:, lo_:lo_ + 768].indirect(T.bd2[:, 12:18]), [ltok] + BD2, ["dup3"])
-        lh(1)
-        pairs(0, 0, T.dh, 0, 96, "dh")
-        for l in (1, 2, 3):
-            if l > 1:
-                lh(l)
-            pair_mm(l)
-        if t > 0:
-            act(T.W[:, 0:256], T.AD[:, AB:AB + 256], ID, ["ADa0"], ["W0"], bias=AFR)
-            act(T.adup[:], T.AD[:, AB + 256:AB + 1024].indirect(T.bd2[:, 0:18]), ID, ["ADa"] + BD2, ["adup"], bias=AFR)
-        act(ps[2][:, 256:384], T.AD[:, AB + 1024 + par:AB + 1280:2], ID, ["ADa"], ["ps2"], bias=-AFR)
-        for l in (1, 2, 3):
-            whole(l)
-        cp(T.du[:, 768:896], links[:, lo_ + 768 + par:lo_ + 1024:2], [ltok], ["dut"])
-        cp(T.dupo[:, 0:192], ps[0][:, 0:192], ["ps0"], ["dupo"])
-        for l in (1, 2, 3):
-            pair_cp(l)
-        if last:
-            cp(T.du[:, 896:1024], T.AD[:, 1025 - par:1280:2], ["ADd"], ["duo"])
-        if t == 0:
-            setup_sub()
+        else:
+            act(T.W[:, wo:wo + 256], T.AD[:, AB:AB + 256], ID, ["ADa0"], wt("W0"), bias=AFR)
+
+        def first_pairs():
+            cp(T.du[:, 0:2 * npair], ps[5][:, 0:2 * npair], ["ps5"], ["du1"])
+
+        cp(T.lh[:, 0:2 * npair], links[:, lo_:lo_ + 2 * npair], [ltok], ["lh"])
+        cp(T.dupo[:, 0:96], links[:, lo_:lo_ + 768].indirect(T.bd2[:, 0:6]), [ltok] + BD2, ["dupo1"])
+        pairs(5, 0, T.lh, 0, npair, "lh")
+        cp(T.du[:, 2 * npair:256], links[:, lo_ + 2 * npair:lo_ + 256], [ltok], ["dw1"])
         CUp = T.CU[:, 128 * par:128 * par + 128]
         CUt = "CU%d" % par
-        mm("ps3", ps[3][:, 0:128], [(T.IDh[:], CUp, ["IDh", CUt])])
-        tt(yp, links[:, lo_ + 768 + par:lo_ + 1024:2], ps[3][:, 0:128], SUB, [ltok, "ps3"], ["yp_0", "yp_1"])
-        landed(x)
-        ghosts(x, 0)
+        if t == 0:
+            first_pairs()
+            setup_sub()
+            landed(x)
+            ghosts(x, 0)
+
+        def top_lists(part):
+            if part == 0:
+                cp(T.du[:, 768:896], links[:, lo_ + 768 + par:lo_ + 1024:2], [ltok], ["dut"])
+            elif part == 1:
+                tt(yp, links[:, lo_ + 768 + par:lo_ + 1024:2], ps[3][:, 0:128], SUB, [ltok, "ps3"], ["yp_0", "yp_1"])
+            elif last:
+                cp(T.du[:, 896:1024], T.AD[:, 1025 - par:1280:2], ["ADd"], ["duo"])
+
+        def own_a(l):
+            act(T.adup[:, 96 * l - 96:96 * l], T.AD[:, AB + 256:AB + 1024].indirect(T.bd2[:, 6 * l - 6:6 * l]), ID,
+                ["ADa"] + BD2, ["adup%d" % l], bias=AFR)
+
+        def later(l, k):
+            if k == "a":
+                if l == 1 and t > 0:
+                    own_a(1)
+                    first_pairs()
+            elif k == "r":
+                if l < 3 and t > 0:
+                    own_a(l + 1)
+            elif k == "s":
+                if l == 3:
+                    act(ps[2][:, 256:384], T.AD[:, AB + 1024 + par:AB + 1280:2], ID, ["ADa"], ["ps2"], bias=-AFR)
+                else:
+                    act(T.lh[:, 256:352], T.AD[:, 256:1024].indirect(T.bd2[:, 6 * l:6 * l + 6]), ID, ["ADd"] + BD2, ["lhr"])
+                    act(T.lh[:, 0:256], T.AD[:, 256 * l + 256:256 * l + 512], ID, ["ADd"], ["lh"])
+            elif k == "p":
+                if l < 3:
+                    pairs(5, 0, T.lh, 256, 32, "lhr")
+                    mm("ps5", ps[5][:, 64:96], [(T.IDh[:], T.lh[:, 320:352], ["IDh", "lhr"])])
+            elif k == "m":
+                if l < 3:
+                    pairs(6, 0, T.lh, 0, npair, "lh")
+                    mm("ps6", ps[6][:, 2 * npair:256], [(T.IDh[:], T.lh[:, 2 * npair:256], ["IDh", "lh"])])
+                else:
+                    mm("ps3", ps[3][:, 0:128], [(T.IDh[:], CUp, ["IDh", CUt])])
+            elif k == "q":
+                if l < 3:
+                    cp(T.dupo[:, 96 * l:96 * l + 96], ps[5][:, 0:96], ["ps5"], ["dupo%d" % (l + 1)])
+                else:
+                    top_lists(0)
+            elif l == 3:
+                top_lists(1)
+                top_lists(2)
+            else:
+                cp(T.du[:, 256 * l:256 * l + 256], ps[6][:, 0:256], ["ps6"], ["du%d" % (l + 1), "dw%d" % (l + 1)])
 
         for l in (1, 2, 3):
             xl = x + l
@@ -455,30 +505,32 @@ def rank_program(g, core, T, topo):
 
             def step(w):
                 k = w[1:]
-                if w[0] in "hlcrvk":
+                if w[0] in "svkhlcr":
                     d = int(k)
                     c0 = 32 * (d - 1)
-                    c = 32 * (l - 1) + 16 * (d - 1)
-                    e0, e1 = 8 * c0, 8 * c0 + 256
-                    if w[0] == "h":
-                        gat("a", T.gd[:, e0:e1], T.dupo[:, 96 + c:112 + c], ["dupo"], ["gd" + k])
-                    elif w[0] == "l":
-                        tt(T.gd[:, 512 + e0:512 + e1], Wall.indirect(T.dupo[:, c:c + 16]), T.gd[:, e0:e1], MIN,
-                           WT + ["dupo", "gd" + k], ["gl_" + k])
-                    elif w[0] == "c":
-                        scan(T.sd[:, e0:e1], T.d0p[:], T.gd[:, 512 + e0:512 + e1], ADD, MIN, ["d0p", "gl_" + k], ["sd" + k])
-                    elif w[0] == "v":
-                        gat("v", T.gd[:, 1024:1536], T.dupo[:, 160 + 32 * l:192 + 32 * l], ["dup3"], ["gl_3"])
+                    e0, e1, e2 = 16 * c0, 16 * c0 + 256, 16 * c0 + 512
+                    if w[0] in "sv":
+                        gat("a" if w[0] == "s" else "v", T.gd[:, e0:e2], T.dupo[:, o + c0:o + c0 + 32],
+                            ["dupo%d" % l], ["gd" + k, "gh" + k])
                     elif w[0] == "k":
-                        scan(T.sd[:, 512:1024], T.d0z[:], T.gd[:, 1024:1536], ADD, MIN, ["d0z", "gl_3"], ["sd3"])
+                        scan(T.sd[:, e0:e2], T.d0z[:], T.gd[:, e0:e2], ADD, MIN, ["d0z", "gd" + k], ["sd" + k])
+                    elif w[0] == "h":
+                        gat("a", T.gd[:, e0:e1], T.dupo[:, o + 16 + 16 * d:o + 32 + 16 * d], ["dupo%d" % l], ["gh" + k])
+                    elif w[0] == "l":
+                        tt(T.gd[:, e1:e2], worth(T.dupo[:, o + 16 * d - 16:o + 16 * d]), T.gd[:, e0:e1], MIN,
+                           wt(*WT) + ["dupo%d" % l, "gh" + k], ["gd" + k])
+                    elif w[0] == "c":
+                        scan(T.sd[:, e0:e1], T.d0p[:], T.gd[:, e1:e2], ADD, MIN, ["d0p", "gd" + k], ["sd" + k])
                     else:
-                        src, a = (T.sd[:, e0 + 7:e1:8], 2 * c) if d < 3 else (T.sd[:, 527:1024:16], 160 + 32 * l)
-                        tt(T.rl[:, 96 * xl + c0:96 * xl + c0 + 32], src, T.adup[:, a:a + 32],
-                           MIN, ["sd" + k, "adup"], ["rl%d_%d" % (xl, d)])
-                        n = send1(xl, d)
+                        src = T.sd[:, e0 + 15:e2:16] if l == 1 or d == 3 else T.sd[:, e0 + 7:e1:8]
+                        tt(T.rl[:, 96 * xl + c0:96 * xl + c0 + 32], src, T.adup[:, o + c0:o + c0 + 32],
+                           MIN, ["sd" + k, "adup%d" % l], ["rl%d_%d" % (xl, d)])
+                        n = send1(xl, d, block(T.rl, 96 * xl)(d), block(T.gl, 96 * xl)(d), "rl%d_%d" % (xl, d))
                         going[0] += n
                         sent[0] += n
                         tok["gl%d" % xl] = {"w": ("arr%d" % xl, going[0]), "r": {}}
+                elif w[0] == "D":
+                    later(l, k)
                 elif w == "S":
                     if t == 0:
                         setup_g(l)
@@ -489,8 +541,8 @@ def rank_program(g, core, T, topo):
                     gat("a", T.hi[:, e0:e1], T.du[:, c + e0 // 16:c + e1 // 16], ["du%d" % l], ["hi" + k], bias=0.5)
                 elif w[0] == "L":
                     e0, e1 = span(k, 8)
-                    tt(T.lo[:, e0:e1], Wall.indirect(T.du[:, b + e0 // 16:b + e1 // 16]), T.hi[:, e0:e1], MIN,
-                       WT + ["du%d" % l, "hi" + k], ["lo" + k])
+                    tt(T.lo[:, e0:e1], worth(T.du[:, b + e0 // 16:b + e1 // 16]), T.hi[:, e0:e1], MIN,
+                       wt(*WT) + ["du%d" % l, "hi" + k], ["lo" + k])
                 elif w == "Pe":
                     gat("a", T.h32[:, 0:16 * ne], T.du[:, b + 256 - ne:b + 256], ["dw%d" % l], ["loe"], bias=AFR)
                 elif w[0] in "PU":
@@ -515,26 +567,22 @@ def rank_program(g, core, T, topo):
                             mm("ps%d" % bank, ps[bank][:, a - at[ks[0]]:a - at[ks[0]] + n],
                                [(T.one[0:1, :], T.cst[0:1, a:a + n], ["one", "cst", "cst0"]),
                                 (T.IDh[:], (T.sp if m == 8 else T.sm)[:, e0 + m - 1:e1:m], ["IDh"] + ["sp" + j for j in js])])
-                elif w == "Me":
-                    a = 256 * l + 256 - ne
-                    tt(T.K[:, a:a + ne], T.s32[:, 15:16 * ne:16], T.AD[:, AB + a:AB + a + ne], MIN, ["spe", "ADa"], ["Ke%d" % l])
-                elif w[0] == "M":
-                    ks, bank = GRP[k]
-                    a, n = 256 * l + at[ks[0]], sum(size[j] for j in ks)
-                    tt(T.K[:, a:a + n], ps[bank][:, 0:n], T.AD[:, AB + a:AB + a + n], MIN, ["ps%d" % bank, "ADa"],
-                       ["K%s%d" % (k, l)])
                 elif w == "A":
                     landed(xl)
                 elif w == "Wg":
                     ghosts(xl, l)
-                elif w == "W":
-                    a, n = 256 * l, 256 - ne
-                    ts(T.W[:, a:a + n], T.K[:, a:a + n], MAG, ADD, ["Ka%d" % l, "Kb%d" % l], ["W%d" % l], -MAG, ADD)
-                elif w == "We":
-                    a = 256 * l + 256 - ne
-                    ts(T.W[:, a:a + ne], T.K[:, a:a + ne], MAG, ADD, ["Ke%d" % l], ["Wb%d" % l], -MAG, ADD)
+                elif w[0] in "KW":
+                    if k == "e":
+                        a, n, src, tk = 256 * l + 256 - ne, ne, T.s32[:, 15:16 * ne:16], "spe"
+                    else:
+                        ks, bank = GRP[k]
+                        a, n = 256 * l + at[ks[0]], sum(size[j] for j in ks)
+                        src, tk = ps[bank][:, 0:n], "ps%d" % bank
+                    out, wr = (T.K[:, a:a + n], ["K%s%d" % (k, l)]) if w[0] == "K" else \
+                        (T.W[:, wo + a:wo + a + n], wt("W%s%d" % (k, l)))
+                    tt(out, src, T.AD[:, AB + a:AB + a + n], MIN, [tk, "ADa"], wr)
 
-            for w in ORDER.split():
+            for w in ((FIRST if l == 1 else START) + ORDER).split():
                 step(w)
 
         cuts = TCUT
@@ -554,7 +602,8 @@ def rank_program(g, core, T, topo):
                     mm("ps7", ps[7][:, 0:n], [(T.sel[0:8, :], T.s16[0:8, c0:c0 + n], ["sel", "s16"])])
                     act(T.SR[:, dst:dst + n], ps[7][:, 0:n], ID, ["ps7"], ["SR%d" % c0])
                 return run
-            spare = [sr_part(0, 512, 0), sr_part(512, 512, 512), sr_part(1024, 384, 1280)]
+            spare = [lambda: setup_s(4), sr_part(0, 512, 0), sr_part(512, 512, 512)] + [lambda: None] * 2 + \
+                    [sr_part(1024, 384, 1280)]
         if last:
             def ex_part(i):
                 def run():
@@ -598,32 +647,28 @@ def rank_program(g, core, T, topo):
                 scan(T.ss[:, a:b], T.d0n[:, 0:64], T.tt[:, a:b], ADD, MAX, ["d0n", "tt" + s], ["ss" + s])
                 tt(T.adj[:, a:b], T.tt[:, a:b], ps[4][:, 384:448], ADD, ["tt" + s, "ramp"], ["adj" + s])
 
-            def turn():
-                op("v", lambda: V.transpose(T.tt[:, a:b], T.wtm[:, a:b]), ["wtm" + s], ["tt" + s])
-                ts(T.vr[:, a:b], T.wtm[:, a:b], -VOFF, ADD, ["wtm" + s], ["vr" + s])
-
-            def same():
-                tt(T.mT[:, a:b], T.ss[:, a:b].indirect(T.l15[:, 0:4]), T.adj[:, a:b], EQ, ["ss" + s, "l15", "adj" + s], ["mT" + s])
-                tt(mth, mth, T.vr[:, a:b], SUB, ["mt" + s, "vr" + s], ["mt" + s])
             return [
                 lambda: tt(mth, T.st[:, 16 * a + 15:16 * b:16], ps[2][:, 256 + a:256 + b], MIN,
                            ["st%d" % i for i in range(4) if cuts[i] < b and cuts[i + 1] > a] + ["ps2"], ["mt" + s]),
                 lambda: ts(T.wtm[:, a:b], mth, VOFF + AFR, ADD, ["mt" + s], ["wtm" + s]),
-                turn,
+                lambda: op("v", lambda: V.transpose(T.tt[:, a:b], T.wtm[:, a:b]), ["wtm" + s], ["tt" + s]),
                 top,
-                same,
+                lambda: tt(T.mT[:, a:b], T.ss[:, a:b].indirect(T.l15[:, 0:4]), T.adj[:, a:b], EQ,
+                           ["ss" + s, "l15", "adj" + s], ["mT" + s]),
                 lambda: op("v", lambda: V.transpose(T.mask[:, a:b], T.mT[:, a:b]), ["mT" + s], ["mask" + s]),
+                lambda: tt(T.xs[:, a:b], mth, T.mask[:, a:b], MUL, ["mt" + s, "mask" + s], [("xs_0", "xs")[h]]),
             ]
 
-        d0, d1 = date(0), date(1)
-        for f in (lambda: st(1), lambda: st(0), lambda: st(2), d0[0], lambda: st(3), d0[1], d1[0], d0[2], d1[1], d0[3],
-                  d1[2], d0[4], d1[3], d0[5], d1[4]):
-            f()
-        tt(T.xs[:, 0:64], ps[4][:, 0:64], T.mask[:, 0:64], MUL, ["mt_0", "mask_0"], ["xs_0"])
-        d1[5]()
-        tt(T.xv[:, 0:64], T.vr[:, 0:64], T.mask[:, 0:64], MUL, ["vr_0", "mask_0"], ["xv_0"])
-        tt(T.xs[:, 64:128], ps[4][:, 64:128], T.mask[:, 64:128], MUL, ["mt_1", "mask_1"], ["xs"])
-        tt(T.xv[:, 64:128], T.vr[:, 64:128], T.mask[:, 64:128], MUL, ["vr_1", "mask_1"], ["xv"])
+        for i in (1, 0, 2, 3):
+            st(i)
+        for i, (f0, f1) in enumerate(zip(date(0), date(1))):
+            f0()
+            f1()
+            if i == 2:
+                ts(T.vr[:], T.wtm[:], -VOFF, ADD, ["wtm_0", "wtm_1"], ["vr"])
+            if i == 3:
+                tt(mt, mt, T.vr[:], SUB, ["vr", "mt_0", "mt_1"], ["mt_0", "mt_1"])
+        tt(T.xv[:], T.vr[:], T.mask[:], MUL, ["vr", "mask_0", "mask_1"], ["xv_0", "xv"])
 
         CUm = (T.IDh[:], CUp, ["IDh", CUt])
         thm = (T.sel[0:8, :], T.th16[0:8, par::2], ["sel", "th16"])
@@ -662,7 +707,8 @@ def rank_program(g, core, T, topo):
             def Y():
                 if s > 1:
                     tt(yph, T.yg[:, a:b], pF, SUB, ["yg" + x, tF], ["yp" + x])
-                    mm(tF, pF, [(T.IDh[:], T.fs[:, 128 * (s - 2) + a:128 * (s - 2) + b], ["IDh", "fs%d" % (s - 1) + x])], stop=False)
+                    mm(tF, pF, [(T.IDh[:], T.fs[:, 128 * (s - 2) + a:128 * (s - 2) + b], ["IDh", "fs%d" % (s - 1) + x])] +
+                       [(T.P3[:], T.ia[:, a:b], ["P3", "ia"])] * (s == 4), stop=False)
                 else:
                     mm(tF, pF, [(T.IDh[:], T.CU[:, 128 * par + a:128 * par + b], ["IDh", CUt])], stop=False)
 
@@ -713,6 +759,7 @@ def rank_program(g, core, T, topo):
                 if s == 2:
                     act(T.na[:], ps[7][:, 0:128], ACT.Relu, ["ps7"], ["na"], bias=-1.0)
                     act(T.ia2[:], T.na[:], ID, ["na"], ["ia2"], bias=4096.0, scale=-3328.0)
+                    act(T.ia[:], T.na[:], ID, ["na"], ["ia"], bias=4096.0, scale=-4096.0)
                 if s == 3:
                     act(T.q[:], ps[7][:, 0:128], ID, ["ps7"], ["q"])
                     act(T.md1[:, 5::6], ps[7][:, 256:384], ACT.Relu, ["ps7"], ["md15"], bias=16.0)
@@ -721,7 +768,6 @@ def rank_program(g, core, T, topo):
                 if s == 4:
                     nact(2, 0)
                     nact(3, 128)
-                    act(T.ia[:], T.na[:], ID, ["na"], ["ia"], bias=1664.0, scale=-1664.0)
                     tt(T.oky[:], T.AD[:, 0:1664].indirect(T.fl[:, 0:8]), T.ok[:], MUL, ADT[0:4] + both("fl") + ["ok"], ["oky"])
                     tt(ps[4][:, 128:256], T.oky[:], ps[6][:, 128:256], ADD, ["oky", "ps6"], ["d4"])
                     for bank, i in ((6, 0), (7, 128)):
@@ -735,13 +781,27 @@ def rank_program(g, core, T, topo):
             if s == 3:
                 qmin(0)
             h1[2]()
+            if s == 3 and not last:
+                for d in (1, 2):
+                    mm("ps5", ps[5][:, 128 + 128 * d:256 + 128 * d], [(T["P%d" % d][:], T.md1[:, 5::6], ["P%d" % d, "md15"])])
+                act(T.bk[:, 288:416], T.md1[:, 5::6], ID, ["md15"], ["bk3"], scale=-1.0)
+                for d in (1, 2):
+                    act(T.bk[:, 144 * d - 144:144 * d - 16], ps[5][:, 128 + 128 * d:256 + 128 * d], ID, ["ps5"], ["bk%d" % d],
+                        scale=-1.0)
             if s == 4:
                 h0[1]()
                 h1[1]()
+                if not last:
+                    for d in (1, 2):
+                        mm("ps%d" % BB[d - 1], ps[BB[d - 1]][:, 0:128],
+                           [(T.PX[:, 128 * d - 128:128 * d], T.t3[:], ["PX%d" % d] + both("t3"))], stop=False)
                 for a, x in ((0, "_0"), (64, "_1")):
                     tt(T.w4[:, a:a + 64], T.md1[:, 6 * a + 3:6 * a + 384:6], ps[4][:, 128 + a:192 + a], MUL, ["E4" + x, "d4"], ["w4" + x])
-                for bank in (6, 7):
-                    mm("ps%d" % bank, ps[bank][:, 0:128], [(T.BO[:], T.w4[:], ["BO"] + both("w4"))], start=False)
+                sums = [(6, T.BO[:], "BO"), (7, T.BO[:], "BO")]
+                if not last:
+                    sums[1:1] = [(BB[d - 1], T.PX[:, 128 + 128 * d:256 + 128 * d], "PB%d" % d) for d in (1, 2)]
+                for bank, m, tk in sums:
+                    mm("ps%d" % bank, ps[bank][:, 0:128], [(m, T.w4[:], [tk] + both("w4"))], start=False)
             h0[3]()
             if s == 3:
                 mm("ps6", ps[6][:, 128:256], [FS(2), IA, Ef(3, T.BOn[:], "BOn")])
@@ -766,8 +826,7 @@ def rank_program(g, core, T, topo):
                 nstep(3, 128)
                 act(T.n3[:], ps[7][:, 128:256], ACT.Relu, ["ps7"], ["n3"], bias=-4096.0)
             if s == 4:
-                nstep(4, 256)
-                nact(4, 256)
+                nstep(4, 0)
             else:
                 h0[4]()
                 h1[4]()
@@ -782,32 +841,79 @@ def rank_program(g, core, T, topo):
                     mm("ps6", ps[6][:, 128:256], [(T.IDm[:], T.md0[:, 4::6], ["IDm", "md04"]), (T.IDh[:], T.n3[:], ["IDh", "n3"]),
                                                   (T.IDk[:], T.t3[:], ["IDk"] + both("t3"))])
 
-        scan(T.tfs[:, 0:128], T.DD[:], ps[6][:, 0:128], ADD, MIN, ["DD", "ps6"], ["tfs"])
-        tt(T.tf[:, 0:64], T.ia[:, 0:64], ps[1][:, 0:64], MAX, ["ia", "ps1"], ["tf1a"])
-        tt(T.tf[:, 64:128], T.ia[:, 64:128], ps[2][:, 0:64], MAX, ["ia", "ps2"], ["tf1"])
-        for a in range(8):
-            o, n, own = 8 * a * (a + 1), 16 * (a + 1), T.tfs[:, 16 * a + 15:16 * a + 16]
-            if a < 8 - NVC:
-                act(T.cmp[:, o:o + n], ps[7][:, 0:n], ACT.Abs, ["ps7", "tfs"], ["cmp%d" % a], bias=own, scale=-1.0)
-            else:
-                ts(T.cmp[:, o:o + n], ps[6][:, 0:n], own, SUB, ["ps6", "tfs", "c_fix"], ["cmp%d" % a], c_fix, NE)
-        ts(T.tl[:, 0:8], T.tfs[:, 15:128:16], 8192.0 + AB, ADD, ["tfs"], ["tl"])
-        scan(T.tfs[:, 128:256], T.DD[:], T.tf[:], ADD, MIN, ["DD", "tf1", "tf1a"], ["tfs2"])
-        act(T.old[:], T.AD[:, 0:2944].indirect(T.tl[:, 0:8]), ID, ADT + ["tl"], ["old"])
-        tt(T.wd1[:, 0::2], T.tfs[:, 15:128:16], T.dum2[:], SUB, ["tfs", "dum2"], ["wd1"])
-        ts(T.tl[:, 8:16], T.tfs[:, 143::16], c_fix, ADD, ["tfs2", "c_fix"], ["tl2"])
-        scan(T.cs[:], T.DQ[:], T.cmp[:], ADD, MIN, DQT + ["cmp%d" % a for a in range(8)], ["cs"])
-        scan(T.ms[:], T.md0[:], T.md1[:], MUL, ADD,
-             ["md0c", "md0d", "md01", "md02", "md03", "md04", "md14", "md15"] + both("E1") + both("E2") + both("E3") + both("E4"), ["ms"])
-        ts(T.wd0[:, 1::2], T.cs[:, 0:576].indirect(T.lend[:, 0:1]), c_win, EQ, ["cs", "lend", "c_win"], ["win"])
-        vgap()
-        scan(T.win[:], T.wd0[:, 0:16], T.wd1[:], MUL, ADD, ["win", "wd0c", "wd1", "wd1c"], ["l2"])
-        tt(T.yy[:], T.SR[:, 0:1672].indirect(T.tl[:, 8:16]), T.ms[:, 5::6], MUL, SRT + ["tl2", "ms"], ["yy"])
-        vgap()
-        if last:
-            dma("s", T.yr[:], T.yrb[:], "st", ["yr0"] + ["yr1%d" % i for i in range(4)], [], 16)
-        cp(T.ll[:], T.win[:, 1::2], ["l2"], ["ll"])
-        tt(T.AD[:, 0:2944].indirect(T.ll[:, 0:8]), T.old[:], T.yy[:], SUB, ["ll", "old", "yy"] + ADT, ADT)
+        def wstep(w):
+            k = w[1:]
+            if w == "own":
+                scan(T.tfs[:, 0:128], T.DD[:], ps[6][:, 0:128], ADD, MIN, ["DD", "ps6"], ["tfs"])
+            elif w[0] in "SV":
+                a = int(k)
+                o, n, own = 8 * a * (a + 1), 16 * (a + 1), T.tfs[:, 16 * a + 15:16 * a + 16]
+                if w[0] == "S":
+                    act(T.cmp[:, o:o + n], ps[7][:, 0:n], ACT.Abs, ["ps7", "tfs"], ["cmp" + k], bias=own, scale=-1.0)
+                else:
+                    ts(T.cmp[:, o:o + n], ps[6][:, 0:n], own, SUB, ["ps6", "tfs", "c_fix"], ["cmp" + k], c_fix, NE)
+            elif w[0] in "AB":
+                j = int(k)
+                bank = (0, 3, 6)[j // 2]
+                if w[0] == "A":
+                    act(T.rc[:, 128 * j:128 * j + 128], ps[bank][:, 0:128], ACT.Abs, ["ps%d" % bank, "bdf0"], ["rc" + k],
+                        bias=T.bdf[:, 8 + j:9 + j], scale=128.0)
+                else:
+                    ts(T.rc[:, 128 * j:128 * j + 128], ps[bank][:, 0:128], T.bdf[:, j:j + 1], NE,
+                       ["ps%d" % bank, "bdf1", "bdf2"], ["rc" + k], 128.0, MUL)
+            elif w[0] in "RIZ":
+                d = int(k)
+                a = 256 * (d - 1)
+                if w[0] == "R":
+                    scan(T.rs[:, a:a + 256], T.d0r[:], T.rc[:, a:a + 256], ADD, MIN,
+                         ["d0r", "rc%d" % (2 * d - 2), "rc%d" % (2 * d - 1)], ["rs" + k])
+                elif w[0] == "I":
+                    ts(T.ri[:, 2 * d - 2:2 * d], T.rs[:, a + 127:a + 256:128], 1.0, MIN, ["rs" + k], ["ri" + k], 127.0, ADD)
+                else:
+                    tt(block(T.rz, 96 * t + 96)(d), T.bk[:, 144 * (d - 1):144 * d].indirect(T.ri[:, 2 * d - 2:2 * d]),
+                       block(T.rz, 96 * t)(d), ADD, ["bk" + k, "bk0", "ri" + k, "rz%d_%d" % (t, d)], ["rz%d_%d" % (t + 1, d)])
+                    n = send1(4 * t + 4, d, block(T.rz, 96 * t + 96)(d), block(T.W, WSZ * (1 - par) + 1280)(d),
+                              "rz%d_%d" % (t + 1, d))
+                    going[0] += n
+                    sent[0] += n
+                    tok["Wg0/%d" % (1 - par)] = {"w": ("arr%d" % (4 * t + 4), going[0]), "r": {}}
+            elif w == "n4":
+                nact(4, 0)
+            elif w == "tl":
+                ts(T.tl[:, 0:8], T.tfs[:, 15:128:16], 8192.0 + AB, ADD, ["tfs"], ["tl"])
+            elif w == "f4":
+                for h in (0, 1):
+                    scan(T.tfs[:, 128 + 64 * h:192 + 64 * h], T.DD[:, 0:64], ps[FB[h]][:, 0:64], ADD, MIN,
+                         ["DD", "ps%d" % FB[h]], ["tfs2_%d" % h])
+            elif w == "old":
+                act(T.old[:], T.AD[:, 0:2944].indirect(T.tl[:, 0:8]), ID, ADT + ["tl"], ["old"])
+            elif w == "wd":
+                tt(T.wd1[:, 0::2], T.tfs[:, 15:128:16], T.dum2[:], SUB, ["tfs", "dum2"], ["wd1"])
+            elif w == "tl2":
+                ts(T.tl[:, 8:16], T.tfs[:, 143::16], c_fix, ADD, both("tfs2") + ["c_fix"], ["tl2"], 1664.0, MIN)
+            elif w == "cs":
+                scan(T.cs[:], T.DQ[:], T.cmp[:], ADD, MIN, DQT + ["cmp%d" % a for a in range(8)], ["cs"])
+            elif w == "ms":
+                scan(T.ms[:], T.md0[:], T.md1[:], MUL, ADD, ["md0c", "md0d", "md01", "md02", "md03", "md04", "md14", "md15"] +
+                     both("E1") + both("E2") + both("E3") + both("E4"), ["ms"])
+            elif w == "win":
+                ts(T.wd0[:, 1::2], T.cs[:, 0:576].indirect(T.lend[:, 0:1]), c_win, EQ, ["cs", "lend", "c_win"], ["win"])
+            elif w == "sel":
+                scan(T.win[:], T.wd0[:, 0:16], T.wd1[:], MUL, ADD, ["win", "wd0c", "wd1", "wd1c"], ["l2"])
+            elif w == "yy":
+                tt(T.yy[:], T.SR[:, 0:1672].indirect(T.tl[:, 8:16]), T.ms[:, 5::6], MUL, SRT + ["tl2", "ms"], ["yy"])
+            elif w == "gap":
+                vgap()
+            elif w == "yr":
+                dma("s", T.yr[:], T.yrb[:], "st", ["yr0"] + ["yr1%d" % i for i in range(4)], [], 16)
+            elif w == "ll":
+                cp(T.ll[:], T.win[:, 1::2], ["l2"], ["ll"])
+            elif w == "put":
+                tt(T.AD[:, 0:2944].indirect(T.ll[:, 0:8]), T.old[:], T.yy[:], SUB, ["ll", "old", "yy"] + ADT, ADT)
+
+        going = [0]
+        for w in (WLAST if last else WORDER).split():
+            wstep(w)
 
     dma("s", T.yd[:], T.AD[:, 256:1280], "st", ["ADd"], [], 32)
     ts(T.yab[:, 0:672], T.AD[:, AB:AB + 672], AOFF, ADD, ["ADa0", "ADa"], ["yab0"])

from concourse.bass import DstId, RemoteDMATransfer
from concourse.mybir import AluOpType, ActivationFunctionType

ALU = AluOpType
ACT = ActivationFunctionType

H = "float16"
MAG = 12582912.0
AFR = 0.4921875
AOFF = 127.0 + AFR
EPS = 0.0078125
VOFF = 1152.0
M16 = 786432.0
AB = 1280
NP = 4
WORDER = "B4 B5 own A0 A1 B2 B3 R3 S0 S1 S2 S3 S4 S5 S6 n4 R1 R2 I3 V7 I1 I2 tl Z3 wd Z1 Z2 old cs f4 ms win tl2 sel yy ll put"
WLAST = "own n4 S0 S1 S2 S3 V7 V6 V5 V4 tl f4 old wd tl2 cs ms win gap sel yy gap yr ll put"
PAIRS = "ab"
SEG = [("a", 88), ("b", 68), ("w", 76), ("e", 24)]
GRP = {"a": ("ab", 0), "b": ("w", 1)}
FIRST = "s1 v3 Da v2 k1 k3 Ha Hb r1 k2 r3 Pw La Pe r2 "
START = "v3 h2 h1 l2 k3 l1 c2 r3 c1 r2 Ha Hb Pw La Pe r1 "
ORDER = "Ds Dr S Lb Ca Cb Ga Cw Gb Dp Ka Ce A Dm Wa Wb Dq We Wg Kb Ke Dv"
WSZ = 1680
TCUT = [0, 52, 88, 112, 128]

f32, bf, i32, u16 = "float32", "bfloat16", "int32", "uint16"


def _sb(n, d):
    return ("sbuf", [128, n], d)


SCRATCH = {
    "avs": _sb(1280, bf), "dpi": _sb(1024, i32), "bdi": _sb(24, i32), "sbi": _sb(88, i32), "thi": _sb(16, i32),
    "s16a": _sb(88, H), "th16a": _sb(16, H), "wd0": _sb(32, f32), "wd1": _sb(16, f32),
    "AD": _sb(2944, f32), "W": _sb(2 * WSZ, i32), "K": _sb(1664, f32), "SR": _sb(1672, f32),
    "s16": _sb(1408, H), "th16": _sb(256, H), "nf": _sb(88, f32), "nf2": _sb(88, f32), "nf3": _sb(88, f32),
    "one": _sb(128, bf), "cst": _sb(256, bf), "lh": _sb(352, H), "hi": _sb(2048, bf), "lo": _sb(2048, bf),
    "h32": _sb(512, f32), "s32": _sb(512, f32), "SL": _sb(512, H), "d0e": _sb(704, bf),
    "bdu": _sb(24, u16), "bd2": _sb(24, u16), "du": _sb(1024, u16), "dupo": _sb(288, u16), "adup": _sb(288, bf),
    "gd": _sb(1536, bf), "sd": _sb(1536, bf), "gm": _sb(2048, bf), "sm": _sb(2048, H), "sp": _sb(2048, H),
    "gt": _sb(2048, bf), "st": _sb(2048, H), "ge": _sb(2048, bf),
    "rl": _sb(16 * 96, bf), "gl": _sb(16 * 96, bf),
    "J": _sb(128, bf), "JG": _sb(128, bf), "JR": _sb(128, bf),
    "pi": _sb(8, i32), "col": _sb(24, f32),
    "BO": _sb(128, H), "BOm": _sb(128, H), "IDh": _sb(128, H), "sel": _sb(128, H), "CU": _sb(256, H),
    "BOb": _sb(128, bf), "BOn": _sb(128, bf), "IDn": _sb(128, bf),
    "P1": _sb(128, bf), "P2": _sb(128, bf), "P3": _sb(128, bf), "ia2": _sb(128, bf), "dum2": _sb(8, f32),
    "d0t": _sb(1216, bf), "d0z": _sb(512, bf), "d0p": _sb(256, bf), "d0n": _sb(64, bf), "DD": _sb(128, bf), "DQ": _sb(576, bf),
    "l15": _sb(8, u16), "lend": _sb(8, u16),
    "wtm": _sb(128, H), "tt": _sb(128, H), "ss": _sb(128, f32), "adj": _sb(128, f32),
    "mT": _sb(128, H), "mask": _sb(128, H), "xv": _sb(128, H), "xs": _sb(128, H),
    "yg": _sb(128, f32), "z": _sb(512, H), "sf": _sb(128, f32), "fl": _sb(8, u16),
    "md0": _sb(768, bf), "md1": _sb(768, bf), "ms": _sb(768, bf),
    "r16": _sb(128, bf), "mn": _sb(128, bf), "nm": _sb(128, bf), "na": _sb(128, bf),
    "ia": _sb(128, bf), "q": _sb(128, f32), "tfs": _sb(256, f32),
    "IDm": _sb(128, bf), "IDp": _sb(128, bf), "IDk": _sb(128, H), "row": _sb(256, bf), "ok": _sb(128, bf),
    "rc": _sb(768, bf), "rs": _sb(768, bf), "d0r": _sb(256, bf), "ri": _sb(8, u16), "bk": _sb(432, bf), "bdf": _sb(16, f32),
    "rz": _sb(384, i32), "PX": _sb(512, H),
    "fs": _sb(384, H), "vr": _sb(128, bf), "t3": _sb(128, H), "n3": _sb(128, H), "oky": _sb(128, H), "w4": _sb(128, H),
    "tl": _sb(16, u16), "cmp": _sb(576, bf), "cs": _sb(576, bf), "win": _sb(16, f32),
    "ll": _sb(8, u16), "old": _sb(128, f32), "yy": _sb(128, f32),
    "yab": _sb(1280, bf), "yrb": _sb(256, bf),
}
for _b in range(8):
    SCRATCH["ps%d" % _b] = ("psum", [128, 512], f32)

SEMAPHORES = ["cv", "ca", "cp", "cg", "l_av0", "l_av1", "l_dp", "l_bd", "l_sb", "l_th", "r_sb", "r_th", "sent", "st"] + \
             ["arr%d" % i for i in range(16)]


def rank_program(g, core, T, topo):
    rank = T.rank_of(core)
    if rank is None:
        return
    Q = {"v": g.vector, "a": g.scalar, "p": g.tensor, "g": g, "s": g.sync}
    SEM = {"v": "cv", "a": "ca", "p": "cp", "g": "cg"}
    cnt = {"v": 0, "a": 0, "p": 0, "g": 0}
    seen = {e: {} for e in Q}
    tok = {}

    know = {}

    def sync(e, reads, writes):
        need = {}

        def wait(e, ev):
            if ev is not None and need.get(ev[0], 0) < ev[1]:
                need[ev[0]] = ev[1]

        collect(e, reads, writes, wait)
        for s in list(need):
            if any(know.get((s2, v2), {}).get(s, 0) >= need[s] for s2, v2 in need.items() if s2 != s):
                need[s] = 0
        for s, v in need.items():
            if seen[e].get(s, 0) < v:
                Q[e].wait_ge(T.sem[s], v)
                seen[e][s] = v
                for s2, v2 in know.get((s, v), {}).items():
                    if seen[e].get(s2, 0) < v2:
                        seen[e][s2] = v2

    def collect(e, reads, writes, wait):
        own = SEM.get(e)
        for r in reads:
            t = tok.setdefault(r, {"w": None, "r": {}})
            wait(e, t["w"])
            if r.startswith("ps"):
                for s, v in t["r"].items():
                    if s != own:
                        wait(e, (s, v))
        for w in writes:
            t = tok.setdefault(w, {"w": None, "r": {}})
            if t["w"] is not None and (e != "p" or t["w"][0] != own):
                wait(e, t["w"])
            for s, v in t["r"].items():
                if e != "p" or s != own:
                    wait(e, (s, v))

    def mark(ev, reads, writes):
        for r in reads:
            tok.setdefault(r, {"w": None, "r": {}})["r"][ev[0]] = ev[1]
        for w in writes:
            tok[w] = {"w": ev, "r": {}}

    def op(e, fn, reads, writes):
        sync(e, reads, writes)
        ins = fn()
        cnt[e] += 1
        ins.then_inc(T.sem[SEM[e]], 1)
        know[(SEM[e], cnt[e])] = dict(seen[e])
        mark((SEM[e], cnt[e]), reads, writes)

    def mm(bank, out, terms, start=True, stop=True):
        allr = []
        for i, (l, r, rd) in enumerate(terms):
            sync("p", rd, [bank] if i == 0 else [])
            ins = g.tensor.matmul(out, l, r, start and i == 0, stop and i == len(terms) - 1)
            allr += rd
        cnt["p"] += 1
        ins.then_inc(T.sem.cp, 1)
        know[("cp", cnt["p"])] = dict(seen["p"])
        mark(("cp", cnt["p"]), allr, [bank])

    def dma(e, out, in_, sem, reads, writes, val=16):
        sync(e, reads, writes)
        Q[e].dma_start(out, in_).then_inc(T.sem[sem], 16)
        mark((sem, val), reads, writes)

    V = g.vector

    def ts(out, in0, s1, o0, reads, writes, s2=None, o1=None):
        if o1 is None:
            op("v", lambda: V.tensor_scalar(out, in0, s1, None, o0), reads, writes)
        else:
            op("v", lambda: V.tensor_scalar(out, in0, s1, s2, o0, o1), reads, writes)

    def tt(out, a, b, o, reads, writes):
        op("v", lambda: V.tensor_tensor(out, a, b, o), reads, writes)

    def cp(out, a, reads, writes):
        op("v", lambda: V.tensor_copy(out, a), reads, writes)

    def scan(out, d0, d1, o0, o1, reads, writes):
        op("v", lambda: V.tensor_tensor_scan(out, d0, d1, 0.0, o0, o1), reads, writes)

    def ms(ap, c, writes):
        op("v", lambda: V.memset(ap, c), [], writes)

    def act(out, in_, func, reads, writes, bias=0.0, scale=1.0):
        op("a", lambda: g.scalar.activation(out, in_, func, bias=bias, scale=scale), reads, writes)

    def iota(out, pat, base, cm, writes, fl=True):
        if fl:
            op("g", lambda: g.iota(out, pat, base, cm, allow_small_or_imprecise_dtypes=True), [], writes)
        else:
            op("g", lambda: g.iota(out, pat, base, cm), [], writes)

    def sel(out, in_, pat, cmp_, fill, base, cm, reads, writes):
        op("g", lambda: g.affine_select(out, in_, pat, cmp_, fill, base, cm), reads, writes)

    ADD, SUB, MUL, MAX, MIN = ALU.add, ALU.subtract, ALU.mult, ALU.max, ALU.min
    EQ, NE = ALU.is_equal, ALU.not_equal
    ID = ACT.Identity
    ps = [T["ps%d" % b] for b in range(8)]
    ADT = ["ADj", "ADd", "ADa0", "ADa", "ADk"]
    WL = ["W%s%d" % (k, l) for k in "abe" for l in (1, 2, 3)] + ["Wx"]
    WT = ["W0", "Wg0", "Wg1", "Wg2", "Wg3", "Wy"] + WL
    KT = ["Kx0", "Kx"] + ["K%s%d" % (k, l) for k in "abe" for l in (1, 2, 3)]
    SRT = ["SR0", "SR512", "SR1024", "SRa", "SRb"]
    BD2 = ["bd20", "bd21", "bd22"]

    at, size = {}, dict(SEG)
    c0 = 0
    for k, n in SEG:
        at[k] = c0
        c0 += n
    npair = sum(size[k] for k in PAIRS if k in size) // 2

    dma("s", T.avs[:, 0:256], T.av[:, 0:256], "l_av0", [], ["av0"])
    dma("a", T.bdi[:], T.bd[:], "l_bd", [], ["bdi"])
    dma("s", T.dpi[:], T.dp[:], "l_dp", [], ["dpi"])
    dma("a", T.avs[:, 256:1280], T.av[:, 256:1280], "l_av1", [], ["av1"])
    dma("s", T.sbi[:], T.sb[:], "l_sb", [], ["sbi"])
    dma("s", T.thi[:], T.th[:], "l_th", [], ["thi"])

    iota(T.pi[:, 0:1], [[1, 1]], 0, 1, ["pi0"], fl=False)
    iota(T.col[:, 20:23], [[8, 3]], -8, 1, ["c_p"])
    iota(T.J[:], [[1, 128]], 0, 0, ["J"])
    iota(T.JG[:], [[1, 8], [0, 16]], 0, 0, ["JG"])
    iota(T.JR[:], [[0, 8], [1, 16]], 0, 0, ["JR"])
    iota(T.nf[:], [[1, 88]], 0, 88, ["nf"])
    steps = (("d0p", 0.0, 8), ("d0z", 0.0, 16), ("d0t", -0.0625, 16), ("d0e", -0.0625, 8))
    for nme, c, m in steps:
        ms(T[nme][:], c, [nme])

    peers = [T.cores[rank ^ d] for d in (1, 2, 3)]

    def emask(es):
        m = 0
        for e in es:
            m |= 1 << e
        return m

    def send(x, src, dst, rd, wr):
        sync("g", rd, [])
        trs = []
        n = len(topo.engines(core, peers[2]))
        for d in (1, 2):
            es = topo.engines(core, peers[d - 1])
            h = len(es) // 2
            es = es[:h] if d == 1 else es[h:]
            n += len(es)
            rid, pid = topo.addr(peers[d - 1], core)
            trs.append(RemoteDMATransfer(dst_ids=[DstId(rid=rid, pnc=pid)], dma_engine_mask=emask(es),
                                         remote_sem=T.sem["arr%d" % x],
                                         src=src(d), dst=dst(d)))
        g.remote_dma_fused(trs, local_sem=T.sem.sent)
        rid, pid = topo.addr(peers[2], core)
        g.remote_dma(dst(3), src(3), T.sem["arr%d" % x], T.sem.sent, pid, rid, topo.mask(core, peers[2]))
        tok[wr] = {"w": ("arr%d" % x, n), "r": {}}
        return n

    def block(buf, c0):
        return lambda d: buf[:, c0 + 32 * (d - 1):c0 + 32 * d]

    def send1(x, d, src, dst, rd):
        rid, pid = topo.addr(peers[d - 1], core)
        sync("g", [rd], [])
        g.remote_dma(dst, src, T.sem["arr%d" % x], T.sem.sent, pid, rid, topo.mask(core, peers[d - 1]))
        return len(topo.engines(core, peers[d - 1]))

    def ghosts(x, l):
        a = WSZ * win[0] + 1280 + 96 * l
        act(T.W[:, a:a + 96], ps[7][:, 0:96], ID, ["ps7"], wt("Wg%d" % l))

    def fill(w):
        for a, n, names in ((256, 1024, WL), (1376, 296, ("Wg1", "Wg2", "Wg3", "Wy"))):
            out, names = T.W[:, WSZ * w + a:WSZ * w + a + n], [x + "/%d" % w for x in names]
            if w == 0:
                act(out, T.avs[:, 256:256 + n], ID, ["av1"], names, bias=128.0, scale=0.0)
            else:
                iota(out, [[0, n]], 128, 0, names, fl=False)

    def landed(x):
        for d in (1, 2, 3):
            c0 = 32 * (d - 1)
            mm("ps7", ps[7][:, c0:c0 + 32], [(T["P%d" % d][:], T.gl[:, 96 * x + c0:96 * x + c0 + 32],
                                              ["P%d" % d, "gl%d" % x])])

    win = [0]

    def wt(*names):
        return [n + "/%d" % win[0] for n in names]

    def worth(offs):
        return T.W[:, WSZ * win[0]:WSZ * win[0] + 1672].indirect(offs)

    def gat(e, out, offs, otok, wtok, bias=0.0):
        if e == "v":
            cp(out, worth(offs), wt(*WT) + otok, wtok)
        else:
            act(out, worth(offs), ID, wt(*WT) + otok, wtok, bias=bias)

    col = T.col
    c_pr, c_pg, c_sb, c_p16, c_k, c_fix, c_win, c_pr1, c_np16 = [col[:, i:i + 1] for i in range(9)]
    c_lo, c_hi, c_k2, c_g1, c_g2 = [col[:, i:i + 1] for i in range(12, 17)]
    c_dn, c_p, c_up = [col[:, i:i + 1] for i in range(20, 23)]

    def setup_first():
        ts(T.pi[:, 1:2], T.pi[:, 0:1], 15, ALU.bitwise_and, ["pi0"], ["pi1"])
        ts(T.pi[:, 2:3], T.pi[:, 0:1], 4, ALU.arith_shift_right, ["pi0"], ["pi2"])
        ts(T.IDh[:], T.J[:], c_p, EQ, ["J", "c_p"], ["IDh"])

    def setup_cols():
        cp(col[:, 0:2], T.pi[:, 1:3], ["pi1", "pi2"], ["c_r"])
        for nme, c, m in steps:
            ms(T[nme][:, 0::m], 8192.0, [nme])
        for c, scale, bias, nme in ((c_k, 0.0625, -0.9375, "c_k"), (c_k2, 0.0625, M16 - 0.4375, "c_k2"),
                                    (c_win, 1.0 / 128, -15.0 / 128, "c_win"), (c_pr1, 1.0, 1.0, "c_pr1")):
            act(c, c_pr, ID, ["c_r"], [nme], bias=bias, scale=scale)
        act(c_sb, c_pg, ID, ["c_r"], ["c_sb"], scale=-1408.0)
        act(T.wd1[:, 1::2], T.J[:, 0::16], ID, ["J", "c_r"], ["wd1c"], bias=c_pr)
        act(T.dum2[:], T.wd1[:, 1::2], ID, ["wd1c"], ["dum2"], bias=-8192.0 - AB)

    def setup_lists():
        ts(c_lo, c_pr, 8.0, ALU.is_lt, ["c_r"], ["c_lo"])
        ts(c_hi, c_pr, 8.0, ALU.is_ge, ["c_r"], ["c_hi"])
        for l in range(3):
            ts(T.bd2[:, 6 * l:6 * l + 6], T.bdi[:, 6 * l + 6:6 * l + 12], float(256 * l), ADD, ["bdi"], ["bd2%d" % l])
        for i, (a, b) in enumerate(((c_p, c_lo), (c_up, c_lo), (c_dn, c_hi), (c_p, c_hi))):
            ts(T.SL[:, 128 * i:128 * i + 128], T.J[:], a, EQ, ["J", "c_p", "c_lo", "c_hi"], ["SL%d" % i], b, MUL)
        ts(c_g1, c_pr, 2.0, MUL, ["c_r", "c_p"], ["c_g1"], c_p, SUB)
        ts(c_g2, c_pg, 0.0, EQ, ["c_r"], ["c_g2"], -128.0, MUL)
        ts(col[:, 9:10], c_pr, 7.0, MIN, ["c_r"], ["c9"], 1.0, ADD)
        ms(T.cst[0:1, 0:2 * npair], -EPS, ["cst0"])
        ms(T.one[0:1, :], 1.0, ["one"])
        ms(T.cst[0:1, 2 * npair:256], AFR, ["cst"])
        ts(T.P3[:], T.J[:], c_p, EQ, ["J", "c_p"], ["P3"])
        ts(T.P1[:], T.J[:], -112.0, ADD, ["J", "c_g1"], ["P1"], c_g1, EQ)
        ts(c_g2, c_g2, c_g1, ADD, ["c_g1", "c_g2"], ["c_g2"])
        ts(col[:, 10:11], col[:, 9:10], 1.0, ADD, ["c9"], ["c10"], 8.0, MUL)
        ts(c_fix, c_pr, 15.0, ALU.is_lt, ["c_r"], ["c_fix"], 8192.0, MUL)
        ts(T.BO[:], T.JG[:], c_pg, EQ, ["JG", "c_r"], ["BO"])
        ts(ps[4][:, 384:448], T.JR[:, 0:64], -0.0625, MUL, ["JR"], ["ramp"], 0.9375, ADD)
        ts(T.sel[:], T.JG[:], c_p, EQ, ["JG", "c_p"], ["sel"])
        ts(T.P2[:], T.J[:], -128.0, ADD, ["J", "c_g2"], ["P2"], c_g2, EQ)
        ts(col[:, 11:12], col[:, 9:10], col[:, 10:11], MUL, ["c9", "c10"], ["c11"], -1.0, ADD)
        ts(T.row[0:1, 0:128], T.JR[0:1, :], 15.0, EQ, ["JR"], ["row0"], -8192.0, MUL)
        ms(T.row[0:1, 128:256], -8192.0, ["row"])
        cp(T.l15[:], T.J[:, 15::16], ["J"], ["l15"])
        ts(T.r16[:], T.JR[:], c_pr, EQ, ["JR", "c_r"], ["r16"], 16384.0, MUL)
        ts(T.mn[:], T.JR[:], c_pr1, EQ, ["JR", "c_pr1"], ["mn"], -8192.0, MUL)
        cp(T.lend[:, 0:1], col[:, 11:12], ["c11"], ["lend"])
        ts(T.nf2[:], T.nf[:], c_sb, ADD, ["nf", "c_sb"], ["nf2"])

    def setup_s(part):
        if part == 1:
            mm("ps3", ps[3][:, 128:256], [(T.P3[:], T.r16[:], ["P3", "r16"]), (T.P3[:], T.mn[:], ["P3", "mn"])])
            act(T.DD[:], ps[3][:, 128:256], ID, ["ps3"], ["DD"])
            for d in (1, 2):
                act(T.PX[:, 128 * d - 128:128 * d], T["P%d" % d][:], ID, ["P%d" % d], ["PX%d" % d])
        if part == 4:
            for d in (1, 2):
                mm("ps6", ps[6][:, 2 * d - 2:2 * d], [(T["P%d" % d][:], T.na[:, 2 * d - 2:2 * d], ["P%d" % d, "na"])])
                mm("ps6", ps[6][:, 32 * d:32 * d + 32], [(T["P%d" % d][:], block(T.rl, 0)(d), ["P%d" % d, "rl0"])])
                mm("ps6", ps[6][:, 128 * d:128 * d + 128], [(T.BO[:], T.PX[:, 128 * d - 128:128 * d], ["BO", "PX%d" % d])])
            act(T.bdf[:, 8:12], ps[6][:, 0:4], ID, ["ps6"], ["bdf0"], scale=-128.0)
            act(T.bdf[:, 0:4], ps[6][:, 0:4], ID, ["ps6"], ["bdf1"])
            act(T.rz[:, 0:64], ps[6][:, 32:96], ID, ["ps6"], ["rz0_1", "rz0_2"])
            act(T.rz[:, 64:96], T.rl[:, 64:96], ID, ["rl0"], ["rz0_3"])
            act(T.PX[:, 256:512], ps[6][:, 128:384], ID, ["ps6"], ["PB1", "PB2"])
            act(T.CU[:, 128:256], T.J[:], ID, ["J"], ["CU1"], bias=1025.0, scale=2.0)
        made = ((), (("BOm", "BO", -1.0), ("BOb", "BO", 1.0), ("BOn", "BO", -2048.0)),
                (("IDk", "P3", -1.0), ("IDn", "P3", -1.0), ("IDm", "P3", -float(AB)), ("IDp", "P3", 4096.0)), ())
        for nme, src, c in made[part - 1]:
            act(T[nme][:], T[src][:], ID, [src], [nme], scale=c)

    def setup_sub():
        ts(T.bdf[:, 4:6], T.bdi[:, 4:6], c_fix, ADD, ["bdi", "c_fix"], ["bdf2"], -8192.0, ADD)
        cp(T.na[:, 0:4], T.bdi[:, 0:4], ["bdi"], ["na"])
        ts(T.th16a[:], T.thi[:], -127.0, ADD, ["thi"], ["th16a"])
        ts(T.nf[:], T.nf2[:], 1024.0, ALU.is_ge, ["nf2"], ["nf"], 256.0, MUL)
        tt(T.nf3[:], T.sbi[:], T.nf2[:], SUB, ["sbi", "nf2"], ["nf3"])
        dma("s", T.th16[0:8, :], T.th16a[:], "r_th", ["th16a"], ["th16"])
        cp(T.AD[:, 256:1280], T.dpi[:], ["dpi"], ["ADd"])
        tt(T.s16a[:], T.nf3[:], T.nf[:], SUB, ["nf3", "nf"], ["s16a"])
        dma("s", T.s16[0:8, :], T.s16a[:], "r_sb", ["s16a"], ["s16"])

    def setup_g(part):
        if part == 1:
            iota(T.K[:, 0:256], [[0, 256]], 1000, 0, ["Kx0"])
            iota(T.K[:, 1024:1664], [[0, 640]], 1000, 0, ["Kx"])
        if part == 2:
            iota(T.AD[:, 0:256], [[0, 256]], 0, 0, ["ADj"])
            iota(T.AD[:, AB + 1280:2944], [[0, 384]], 0, 0, ["ADk"])
            iota(T.d0n[:], [[0, 64]], -8192, 0, ["d0n"])
            sel(T.d0n[:], T.d0n[:], [[0, 4], [1, 16]], EQ, 0.0625, 0, 0, ["d0n"], ["d0n"])
        if part == 3:
            iota(T.SR[:, 1024:1280], [[0, 256]], 1, 0, ["SRa"])
            iota(T.SR[:, 1664:1672], [[0, 8]], 1, 0, ["SRb"])
            iota(T.md0[:, 0::6], [[0, 128]], 0, 0, ["md0c"])
            iota(T.md0[:, 5::6], [[0, 128]], -1, 0, ["md0d"])
            iota(T.wd0[:, 0::2], [[0, 16]], 0, 0, ["wd0c"])
            iota(T.bk[:], [[0, 432]], 0, 0, ["bk0", "bk1", "bk2", "bk3"])
            iota(T.d0r[:], [[0, 256]], -1, 0, ["d0r"])
            iota(T.d0r[:, 0::128], [[0, 2]], 1 << 20, 0, ["d0r"])
            iota(T.DQ[:], [[0, 576]], 8192, 0, ["DQ"])
            for a in range(8):
                o, n = 8 * a * (a + 1), 16 * (a + 1)
                sel(T.DQ[:, o:o + n], T.DQ[:, o:o + n], [[1, n]], EQ, -1.0 / 128, 0, 0, ["DQ"], ["DQ%d" % a])
            fill(1)

    mt, yp = ps[4][:, 0:128], ps[4][:, 256:384]
    DQT = ["DQ%d" % a for a in range(8)]
    sent = [0]

    def negv():
        return [(T.BOm[:], T.xv[:], ["BOm", "xv", "xv_0"])]

    def pairs(bank, o, src, b, n, tk):
        for half in (0, 1):
            mm("ps%d" % bank, ps[bank][:, o + half * n:o + half * n + n],
               [(T.SL[:, 128 * (2 * half + i):128 * (2 * half + i) + 128], src[:, b + i:b + 2 * n:2],
                 ["SL%d" % (2 * half + i), tk]) for i in (0, 1)])

    for t in range(NP):
        par = t & 1
        x = 4 * t
        last = t == NP - 1
        win[0] = par
        wo = WSZ * par
        if t == 0:
            cp(T.bdu[:], T.bdi[:], ["bdi"], ["bdu"])
            setup_first()
            ts(T.rl[:, 0:96], T.avs[:, 0:256].indirect(T.bdu[:, 0:6]), -127.0, ADD, ["av0", "bdu"], ["rl0"])
            sent[0] += send(x, block(T.rl, 0), block(T.gl, 0), ["rl0"], "gl0")
        links, lo_, ltok = (T.dpi, 0, "dpi") if t == 0 else (T.AD, 256, "ADd")

        if t == 0:
            act(T.W[:, 0:256], T.avs[:, 0:256], ID, ["av0"], wt("W0"), bias=-127.0)
            setup_cols()
            setup_lists()
            act(T.adup[:], T.avs[:, 256:1024].indirect(T.bd2[:, 0:18]), ID, ["av1"] + BD2,
                ["adup1", "adup2", "adup3"], bias=-127.0)
            fill(0)
            act(T.AD[:, AB:AB + 1280], T.avs[:], ID, ["av0", "av1"], ["ADa0", "ADa"], bias=-AOFF)
            act(T.CU[:, 0:128], T.J[:], ID, ["J"], ["CU0"], bias=1024.0, scale=2.0)
        else:
            act(T.W[:, wo:wo + 256], T.AD[:, AB:AB + 256], ID, ["ADa0"], wt("W0"), bias=AFR)

        def first_pairs():
            cp(T.du[:, 0:2 * npair], ps[5][:, 0:2 * npair], ["ps5"], ["du1"])

        cp(T.lh[:, 0:2 * npair], links[:, lo_:lo_ + 2 * npair], [ltok], ["lh"])
        cp(T.dupo[:, 0:96], links[:, lo_:lo_ + 768].indirect(T.bd2[:, 0:6]), [ltok] + BD2, ["dupo1"])
        pairs(5, 0, T.lh, 0, npair, "lh")
        cp(T.du[:, 2 * npair:256], links[:, lo_ + 2 * npair:lo_ + 256], [ltok], ["dw1"])
        CUp = T.CU[:, 128 * par:128 * par + 128]
        CUt = "CU%d" % par
        if t == 0:
            first_pairs()
            setup_sub()
            landed(x)
            ghosts(x, 0)

        def top_lists(part):
            if part == 0:
                cp(T.du[:, 768:896], links[:, lo_ + 768 + par:lo_ + 1024:2], [ltok], ["dut"])
            elif part == 1:
                tt(yp, links[:, lo_ + 768 + par:lo_ + 1024:2], ps[3][:, 0:128], SUB, [ltok, "ps3"], ["yp_0", "yp_1"])
            elif last:
                cp(T.du[:, 896:1024], T.AD[:, 1025 - par:1280:2], ["ADd"], ["duo"])

        def own_a(l):
            act(T.adup[:, 96 * l - 96:96 * l], T.AD[:, AB + 256:AB + 1024].indirect(T.bd2[:, 6 * l - 6:6 * l]), ID,
                ["ADa"] + BD2, ["adup%d" % l], bias=AFR)

        def later(l, k):
            if k == "a":
                if l == 1 and t > 0:
                    own_a(1)
                    first_pairs()
            elif k == "r":
                if l < 3 and t > 0:
                    own_a(l + 1)
            elif k == "s":
                if l == 3:
                    act(ps[2][:, 256:384], T.AD[:, AB + 1024 + par:AB + 1280:2], ID, ["ADa"], ["ps2"], bias=-AFR)
                else:
                    act(T.lh[:, 256:352], T.AD[:, 256:1024].indirect(T.bd2[:, 6 * l:6 * l + 6]), ID, ["ADd"] + BD2, ["lhr"])
                    act(T.lh[:, 0:256], T.AD[:, 256 * l + 256:256 * l + 512], ID, ["ADd"], ["lh"])
            elif k == "p":
                if l < 3:
                    pairs(5, 0, T.lh, 256, 32, "lhr")
                    mm("ps5", ps[5][:, 64:96], [(T.IDh[:], T.lh[:, 320:352], ["IDh", "lhr"])])
            elif k == "m":
                if l < 3:
                    pairs(6, 0, T.lh, 0, npair, "lh")
                    mm("ps6", ps[6][:, 2 * npair:256], [(T.IDh[:], T.lh[:, 2 * npair:256], ["IDh", "lh"])])
                else:
                    mm("ps3", ps[3][:, 0:128], [(T.IDh[:], CUp, ["IDh", CUt])])
            elif k == "q":
                if l < 3:
                    cp(T.dupo[:, 96 * l:96 * l + 96], ps[5][:, 0:96], ["ps5"], ["dupo%d" % (l + 1)])
                else:
                    top_lists(0)
            elif l == 3:
                top_lists(1)
                top_lists(2)
            else:
                cp(T.du[:, 256 * l:256 * l + 256], ps[6][:, 0:256], ["ps6"], ["du%d" % (l + 1), "dw%d" % (l + 1)])

        for l in (1, 2, 3):
            xl = x + l
            o = 96 * (l - 1)
            b = 256 * (l - 1)
            ne = size["e"]
            going = [0]

            def span(ks, m):
                a = at[ks[0]] - (0 if m == 8 else 2 * npair)
                return m * a, m * (a + sum(size[j] for j in ks))

            def step(w):
                k = w[1:]
                if w[0] in "svkhlcr":
                    d = int(k)
                    c0 = 32 * (d - 1)
                    e0, e1, e2 = 16 * c0, 16 * c0 + 256, 16 * c0 + 512
                    if w[0] in "sv":
                        gat("a" if w[0] == "s" else "v", T.gd[:, e0:e2], T.dupo[:, o + c0:o + c0 + 32],
                            ["dupo%d" % l], ["gd" + k, "gh" + k])
                    elif w[0] == "k":
                        scan(T.sd[:, e0:e2], T.d0z[:], T.gd[:, e0:e2], ADD, MIN, ["d0z", "gd" + k], ["sd" + k])
                    elif w[0] == "h":
                        gat("a", T.gd[:, e0:e1], T.dupo[:, o + 16 + 16 * d:o + 32 + 16 * d], ["dupo%d" % l], ["gh" + k])
                    elif w[0] == "l":
                        tt(T.gd[:, e1:e2], worth(T.dupo[:, o + 16 * d - 16:o + 16 * d]), T.gd[:, e0:e1], MIN,
                           wt(*WT) + ["dupo%d" % l, "gh" + k], ["gd" + k])
                    elif w[0] == "c":
                        scan(T.sd[:, e0:e1], T.d0p[:], T.gd[:, e1:e2], ADD, MIN, ["d0p", "gd" + k], ["sd" + k])
                    else:
                        src = T.sd[:, e0 + 15:e2:16] if l == 1 or d == 3 else T.sd[:, e0 + 7:e1:8]
                        tt(T.rl[:, 96 * xl + c0:96 * xl + c0 + 32], src, T.adup[:, o + c0:o + c0 + 32],
                           MIN, ["sd" + k, "adup%d" % l], ["rl%d_%d" % (xl, d)])
                        n = send1(xl, d, block(T.rl, 96 * xl)(d), block(T.gl, 96 * xl)(d), "rl%d_%d" % (xl, d))
                        going[0] += n
                        sent[0] += n
                        tok["gl%d" % xl] = {"w": ("arr%d" % xl, going[0]), "r": {}}
                elif w[0] == "D":
                    later(l, k)
                elif w == "S":
                    if t == 0:
                        setup_g(l)
                        setup_s(l)
                elif w[0] == "H":
                    e0, e1 = span(k, 8)
                    c = b + npair
                    gat("a", T.hi[:, e0:e1], T.du[:, c + e0 // 16:c + e1 // 16], ["du%d" % l], ["hi" + k], bias=0.5)
                elif w[0] == "L":
                    e0, e1 = span(k, 8)
                    tt(T.lo[:, e0:e1], worth(T.du[:, b + e0 // 16:b + e1 // 16]), T.hi[:, e0:e1], MIN,
                       wt(*WT) + ["du%d" % l, "hi" + k], ["lo" + k])
                elif w == "Pe":
                    gat("a", T.h32[:, 0:16 * ne], T.du[:, b + 256 - ne:b + 256], ["dw%d" % l], ["loe"], bias=AFR)
                elif w[0] in "PU":
                    e0, e1 = span(k, 16)
                    c = b + 2 * npair
                    gat("a" if w[0] == "P" else "v", T.gm[:, e0:e1], T.du[:, c + e0 // 16:c + e1 // 16], ["dw%d" % l],
                        ["lo" + k])
                elif w == "Ce":
                    scan(T.s32[:, 0:16 * ne], T.d0t[:, 0:16 * ne], T.h32[:, 0:16 * ne], ADD, MIN, ["d0t", "loe"], ["spe"])
                elif w[0] == "C":
                    m = 8 if k[0] in PAIRS else 16
                    e0, e1 = span(k, m)
                    src, dst, d0 = (T.lo, T.sp, T.d0e) if m == 8 else (T.gm, T.sm, T.d0t)
                    scan(dst[:, e0:e1], d0[:, 0:e1 - e0], src[:, e0:e1], ADD, MIN, ["d0e", "d0t"] + ["lo" + j for j in k],
                         ["sp" + j for j in k])
                elif w[0] == "G":
                    ks, bank = GRP[k]
                    for js, m in (([j for j in ks if j in PAIRS], 8), ([j for j in ks if j not in PAIRS], 16)):
                        if js:
                            e0, e1 = span(js, m)
                            a, n = at[js[0]], (e1 - e0) // m
                            mm("ps%d" % bank, ps[bank][:, a - at[ks[0]]:a - at[ks[0]] + n],
                               [(T.one[0:1, :], T.cst[0:1, a:a + n], ["one", "cst", "cst0"]),
                                (T.IDh[:], (T.sp if m == 8 else T.sm)[:, e0 + m - 1:e1:m], ["IDh"] + ["sp" + j for j in js])])
                elif w == "A":
                    landed(xl)
                elif w == "Wg":
                    ghosts(xl, l)
                elif w[0] in "KW":
                    if k == "e":
                        a, n, src, tk = 256 * l + 256 - ne, ne, T.s32[:, 15:16 * ne:16], "spe"
                    else:
                        ks, bank = GRP[k]
                        a, n = 256 * l + at[ks[0]], sum(size[j] for j in ks)
                        src, tk = ps[bank][:, 0:n], "ps%d" % bank
                    out, wr = (T.K[:, a:a + n], ["K%s%d" % (k, l)]) if w[0] == "K" else \
                        (T.W[:, wo + a:wo + a + n], wt("W%s%d" % (k, l)))
                    tt(out, src, T.AD[:, AB + a:AB + a + n], MIN, [tk, "ADa"], wr)

            for w in ((FIRST if l == 1 else START) + ORDER).split():
                step(w)

        cuts = TCUT
        for e, i in (("v", 0), ("a", 1), ("a", 2), ("a", 3)):
            gat(e, T.gt[:, 16 * cuts[i]:16 * cuts[i + 1]], T.du[:, 768 + cuts[i]:768 + cuts[i + 1]], ["dut"],
                ["gt%d" % i])

        def st(i):
            n = 16 * (cuts[i + 1] - cuts[i])
            scan(T.st[:, 16 * cuts[i]:16 * cuts[i + 1]], T.d0t[:, 0:n], T.gt[:, 16 * cuts[i]:16 * cuts[i + 1]],
                 ADD, MIN, ["d0t", "gt%d" % i], ["st%d" % i])

        spare, vspare = [], []
        if t == 0:
            def sr_part(c0, n, dst):
                def run():
                    mm("ps7", ps[7][:, 0:n], [(T.sel[0:8, :], T.s16[0:8, c0:c0 + n], ["sel", "s16"])])
                    act(T.SR[:, dst:dst + n], ps[7][:, 0:n], ID, ["ps7"], ["SR%d" % c0])
                return run
            spare = [lambda: setup_s(4), sr_part(0, 512, 0), sr_part(512, 512, 512)] + [lambda: None] * 2 + \
                    [sr_part(1024, 384, 1280)]
        if last:
            def ex_part(i):
                def run():
                    gat("a", T.ge[:, 256 * i:256 + 256 * i], T.du[:, 896 + 16 * i:912 + 16 * i], ["duo"], ["ge%d" % i],
                        bias=127.0)
                return run

            def ex_scan(i):
                def run():
                    scan(T.lo[:, 512 * i:512 * i + 512], T.d0z[:], T.ge[:, 512 * i:512 + 512 * i], ADD, MIN,
                         ["d0z", "ge%d" % (2 * i), "ge%d" % (2 * i + 1)], ["se%d" % i] + ["lo" + k for k in PAIRS if i == 0])
                return run

            def ex_min(i):
                def run():
                    c = 64 * i + 1 - par
                    tt(T.yrb[:, c:c + 63:2], T.lo[:, 512 * i + 15:512 * i + 512:16], T.yab[:, 32 * i:32 * i + 32],
                       MIN, ["se%d" % i, "yab0"], ["yr1%d" % i])
                return run
            spare = [ex_part(i) for i in range(8)]
            vspare = [f(i) for i in range(4) for f in (ex_scan, ex_min)]
            act(T.yab[:, 0:128], T.AD[:, AB + 1025 - par:AB + 1280:2], ID, ["ADa"], ["yab0"], bias=AOFF)

        def gap(n=1):
            for i in range(n):
                if spare:
                    spare.pop(0)()

        def vgap(n=1):
            for i in range(n):
                if vspare:
                    vspare.pop(0)()

        gap(5)

        def date(h):
            a, b = 64 * h, 64 * h + 64
            mth, s = ps[4][:, a:b], "_%d" % h

            def top():
                scan(T.ss[:, a:b], T.d0n[:, 0:64], T.tt[:, a:b], ADD, MAX, ["d0n", "tt" + s], ["ss" + s])
                tt(T.adj[:, a:b], T.tt[:, a:b], ps[4][:, 384:448], ADD, ["tt" + s, "ramp"], ["adj" + s])

            return [
                lambda: tt(mth, T.st[:, 16 * a + 15:16 * b:16], ps[2][:, 256 + a:256 + b], MIN,
                           ["st%d" % i for i in range(4) if cuts[i] < b and cuts[i + 1] > a] + ["ps2"], ["mt" + s]),
                lambda: ts(T.wtm[:, a:b], mth, VOFF + AFR, ADD, ["mt" + s], ["wtm" + s]),
                lambda: op("v", lambda: V.transpose(T.tt[:, a:b], T.wtm[:, a:b]), ["wtm" + s], ["tt" + s]),
                top,
                lambda: tt(T.mT[:, a:b], T.ss[:, a:b].indirect(T.l15[:, 0:4]), T.adj[:, a:b], EQ,
                           ["ss" + s, "l15", "adj" + s], ["mT" + s]),
                lambda: op("v", lambda: V.transpose(T.mask[:, a:b], T.mT[:, a:b]), ["mT" + s], ["mask" + s]),
                lambda: tt(T.xs[:, a:b], mth, T.mask[:, a:b], MUL, ["mt" + s, "mask" + s], [("xs_0", "xs")[h]]),
            ]

        for i in (1, 0, 2, 3):
            st(i)
        for i, (f0, f1) in enumerate(zip(date(0), date(1))):
            f0()
            f1()
            if i == 2:
                ts(T.vr[:], T.wtm[:], -VOFF, ADD, ["wtm_0", "wtm_1"], ["vr"])
            if i == 3:
                tt(mt, mt, T.vr[:], SUB, ["vr", "mt_0", "mt_1"], ["mt_0", "mt_1"])
        tt(T.xv[:], T.vr[:], T.mask[:], MUL, ["vr", "mask_0", "mask_1"], ["xv_0", "xv"])

        CUm = (T.IDh[:], CUp, ["IDh", CUt])
        thm = (T.sel[0:8, :], T.th16[0:8, par::2], ["sel", "th16"])
        IA = (T.P3[:], T.ia2[:], ["P3", "ia2"])
        NM = (T.P3[:], T.nm[:], ["P3", "nm"])

        BB, FB = (0, 3), (1, 2)
        XV, XS = ("xv_0", "xv"), ("xs_0", "xs")

        def both(n):
            return [n + "_0", n + "_1"]

        def Ef(s, m, mt_):
            return (m, T.md1[:, s - 1::6], [mt_] + both("E%d" % s))

        def FS(s):
            return (T.IDh[:], T.fs[:, 128 * (s - 1):128 * s], ["IDh"] + both("fs%d" % s))

        def half(s, h):
            a, b, x = 64 * h, 64 * h + 64, "_%d" % h
            pB, pF, tB, tF = ps[BB[h]][:, 0:64], ps[FB[h]][:, 0:64], "ps%d" % BB[h], "ps%d" % FB[h]
            Eh, yph, lst = T.md1[:, 6 * a + s - 1:6 * b:6], ps[4][:, 256 + a:256 + b], T.fl[:, 4 * h:4 * h + 4]

            def zm(j):
                return (T.BO[:], T.z[:, 128 * (j - 1) + a:128 * (j - 1) + b], ["BO", "z%d" % j + x])

            def nv():
                mm(tB, pB, [(T.BOm[:], T.xv[:, a:b], ["BOm", XV[h]])], stop=False)

            def A():
                if s > 1:
                    tt(T.xs[:, a:b], T.K[:, 0:1664].indirect(lst), T.mask[:, a:b], MUL, KT + ["fl" + x, "mask" + x], [XS[h]])
                    act(T.yg[:, a:b], T.AD[:, 0:1664].indirect(lst), ID, ADT[0:4] + ["fl" + x], ["yg" + x])
                mm(tB, pB, [(T.BO[:], T.xs[:, a:b], ["BO", XS[h]])], start=s == 1)

            def Y():
                if s > 1:
                    tt(yph, T.yg[:, a:b], pF, SUB, ["yg" + x, tF], ["yp" + x])
                    mm(tF, pF, [(T.IDh[:], T.fs[:, 128 * (s - 2) + a:128 * (s - 2) + b], ["IDh", "fs%d" % (s - 1) + x])] +
                       [(T.P3[:], T.ia[:, a:b], ["P3", "ia"])] * (s == 4), stop=False)
                else:
                    mm(tF, pF, [(T.IDh[:], T.CU[:, 128 * par + a:128 * par + b], ["IDh", CUt])], stop=False)

            def Eq():
                if s == 1:
                    ts(Eh, pB, c_k, EQ, [tB, "c_k"], ["E%d" % s + x])
                else:
                    ts(Eh, pB, M16, ADD, [tB, "c_k2"], ["E%d" % s + x], c_k2, EQ)
                if s < 4:
                    nv()

            def Z():
                tt(T.z[:, 128 * (s - 1) + a:128 * (s - 1) + b], Eh, yph, MUL, ["E%d" % s + x, "yp" + x], ["z%d" % s + x])
                mm(tF, pF, [zm(s)], start=False)

            def S():
                scan(T.sf[:, a:b], T.DD[:, 0:64], pF, ADD, MIN, ["DD", tF], ["sf" + x])

            def L():
                ts(lst, T.sf[:, a + 15:b:16], c_fix, ADD, ["sf" + x, "c_fix"], ["fl" + x])
                cp(T.fs[:, 128 * (s - 1) + a:128 * (s - 1) + b], pF, [tF], ["fs%d" % s + x])
            return A, Y, Eq, Z, S, L

        def nstep(s, c0):
            mm("ps5", ps[5][:, c0:c0 + 128], [Ef(s, T.BOb[:], "BOb")])

        def nact(s, c0):
            act(T.md0[:, s - 1::6], ps[5][:, c0:c0 + 128], ID, ["ps5"], ["md0%d" % (s - 1)], bias=1.0, scale=-1.0)

        def qmin(c0):
            tt(T.q[:], T.q[:], ps[6][:, c0:c0 + 128], MIN, ["q", "ps6"], ["q"])

        for s in (1, 2, 3, 4):
            h0, h1 = half(s, 0), half(s, 1)
            h0[0]()
            if s == 1:
                h0[1]()
            h1[0]()
            if s == 1:
                h1[1]()
                mm("ps5", ps[5][:, 0:128], [thm] + negv())
                mm("ps5", ps[5][:, 128:256], negv())
                act(T.r16[:], ps[5][:, 0:128], ACT.Relu, ["ps5"], ["r16"], scale=16.0)
                act(T.mn[:], ps[5][:, 128:256], ACT.Relu, ["ps5"], ["mn"], bias=-111.0)
                act(T.md0[:, 4::6], T.r16[:], ACT.Sign, ["r16"], ["md04"])
                act(T.nm[:], T.mask[:], ID, ["mask_0", "mask_1"], ["nm"], bias=-512.0, scale=512.0)
            else:
                if s == 2:
                    act(T.na[:], ps[7][:, 0:128], ACT.Relu, ["ps7"], ["na"], bias=-1.0)
                    act(T.ia2[:], T.na[:], ID, ["na"], ["ia2"], bias=4096.0, scale=-3328.0)
                    act(T.ia[:], T.na[:], ID, ["na"], ["ia"], bias=4096.0, scale=-4096.0)
                if s == 3:
                    act(T.q[:], ps[7][:, 0:128], ID, ["ps7"], ["q"])
                    act(T.md1[:, 5::6], ps[7][:, 256:384], ACT.Relu, ["ps7"], ["md15"], bias=16.0)
                    act(T.md1[:, 4::6], ps[5][:, 0:128], ACT.Relu, ["ps5"], ["md14"])
                    act(T.ok[:], T.md0[:, 4::6], ID, ["md04"], ["ok"], bias=1.0, scale=-1.0)
                if s == 4:
                    nact(2, 0)
                    nact(3, 128)
                    tt(T.oky[:], T.AD[:, 0:1664].indirect(T.fl[:, 0:8]), T.ok[:], MUL, ADT[0:4] + both("fl") + ["ok"], ["oky"])
                    tt(ps[4][:, 128:256], T.oky[:], ps[6][:, 128:256], ADD, ["oky", "ps6"], ["d4"])
                    for bank, i in ((6, 0), (7, 128)):
                        mm("ps%d" % bank, ps[bank][:, 0:128], [(T.row[0:1, i:i + 128], T.one[0:1, :], ["row", "row0", "one"]),
                                                               (T.IDh[:], T.t3[:], ["IDh"] + both("t3"))], stop=False)
                gap()
                if s < 4:
                    h0[1]()
                    h1[1]()
            h0[2]()
            if s == 3:
                qmin(0)
            h1[2]()
            if s == 3 and not last:
                for d in (1, 2):
                    mm("ps5", ps[5][:, 128 + 128 * d:256 + 128 * d], [(T["P%d" % d][:], T.md1[:, 5::6], ["P%d" % d, "md15"])])
                act(T.bk[:, 288:416], T.md1[:, 5::6], ID, ["md15"], ["bk3"], scale=-1.0)
                for d in (1, 2):
                    act(T.bk[:, 144 * d - 144:144 * d - 16], ps[5][:, 128 + 128 * d:256 + 128 * d], ID, ["ps5"], ["bk%d" % d],
                        scale=-1.0)
            if s == 4:
                h0[1]()
                h1[1]()
                if not last:
                    for d in (1, 2):
                        mm("ps%d" % BB[d - 1], ps[BB[d - 1]][:, 0:128],
                           [(T.PX[:, 128 * d - 128:128 * d], T.t3[:], ["PX%d" % d] + both("t3"))], stop=False)
                for a, x in ((0, "_0"), (64, "_1")):
                    tt(T.w4[:, a:a + 64], T.md1[:, 6 * a + 3:6 * a + 384:6], ps[4][:, 128 + a:192 + a], MUL, ["E4" + x, "d4"], ["w4" + x])
                sums = [(6, T.BO[:], "BO"), (7, T.BO[:], "BO")]
                if not last:
                    sums[1:1] = [(BB[d - 1], T.PX[:, 128 + 128 * d:256 + 128 * d], "PB%d" % d) for d in (1, 2)]
                for bank, m, tk in sums:
                    mm("ps%d" % bank, ps[bank][:, 0:128], [(m, T.w4[:], [tk] + both("w4"))], start=False)
            h0[3]()
            if s == 3:
                mm("ps6", ps[6][:, 128:256], [FS(2), IA, Ef(3, T.BOn[:], "BOn")])
            h1[3]()
            if s < 4:
                vgap(1 if s == 1 else 2)
            else:
                vgap()
            if s == 1:
                mm("ps7", ps[7][:, 0:128], [Ef(1, T.BOb[:], "BOb"), (T.P3[:], T.md0[:, 4::6], ["P3", "md04"])])
                if last:
                    act(T.yrb[:, par::2], T.wtm[:], ID, ["wtm_0", "wtm_1"], ["yr0"], bias=127.0 - VOFF)
            if s == 2:
                mm("ps5", ps[5][:, 0:128], [thm] + negv() + [Ef(1, T.BOn[:], "BOn"), NM])
                mm("ps7", ps[7][:, 0:128], [CUm, Ef(1, T.BOn[:], "BOn"), IA])
                mm("ps7", ps[7][:, 256:384], [(T.IDn[:], T.mn[:], ["IDn", "mn"]), (T.IDn[:], T.r16[:], ["IDn", "r16"]), NM])
                mm("ps6", ps[6][:, 0:128], [Ef(2, T.BOn[:], "BOn"), FS(1), IA])
            if s == 3:
                mm("ps7", ps[7][:, 128:256], [(T.IDp[:], T.md0[:, 4::6], ["IDp", "md04"]), FS(2),
                                              (T.BO[:], T.z[:, 256:384], ["BO"] + both("z3"))])
                nstep(2, 0)
                nstep(3, 128)
                act(T.n3[:], ps[7][:, 128:256], ACT.Relu, ["ps7"], ["n3"], bias=-4096.0)
            if s == 4:
                nstep(4, 0)
            else:
                h0[4]()
                h1[4]()
                if s == 3:
                    qmin(128)
                h0[5]()
                h1[5]()
                if s == 3:
                    for h, x in enumerate(both("t3")):
                        tt(T.t3[:, 64 * h:64 * h + 64], T.q[:, 64 * h:64 * h + 64], ps[FB[h]][:, 0:64], MIN,
                           ["q", "ps%d" % FB[h]], [x])
                    mm("ps6", ps[6][:, 128:256], [(T.IDm[:], T.md0[:, 4::6], ["IDm", "md04"]), (T.IDh[:], T.n3[:], ["IDh", "n3"]),
                                                  (T.IDk[:], T.t3[:], ["IDk"] + both("t3"))])

        def wstep(w):
            k = w[1:]
            if w == "own":
                scan(T.tfs[:, 0:128], T.DD[:], ps[6][:, 0:128], ADD, MIN, ["DD", "ps6"], ["tfs"])
            elif w[0] in "SV":
                a = int(k)
                o, n, own = 8 * a * (a + 1), 16 * (a + 1), T.tfs[:, 16 * a + 15:16 * a + 16]
                if w[0] == "S":
                    act(T.cmp[:, o:o + n], ps[7][:, 0:n], ACT.Abs, ["ps7", "tfs"], ["cmp" + k], bias=own, scale=-1.0)
                else:
                    ts(T.cmp[:, o:o + n], ps[6][:, 0:n], own, SUB, ["ps6", "tfs", "c_fix"], ["cmp" + k], c_fix, NE)
            elif w[0] in "AB":
                j = int(k)
                bank = (0, 3, 6)[j // 2]
                if w[0] == "A":
                    act(T.rc[:, 128 * j:128 * j + 128], ps[bank][:, 0:128], ACT.Abs, ["ps%d" % bank, "bdf0"], ["rc" + k],
                        bias=T.bdf[:, 8 + j:9 + j], scale=128.0)
                else:
                    ts(T.rc[:, 128 * j:128 * j + 128], ps[bank][:, 0:128], T.bdf[:, j:j + 1], NE,
                       ["ps%d" % bank, "bdf1", "bdf2"], ["rc" + k], 128.0, MUL)
            elif w[0] in "RIZ":
                d = int(k)
                a = 256 * (d - 1)
                if w[0] == "R":
                    scan(T.rs[:, a:a + 256], T.d0r[:], T.rc[:, a:a + 256], ADD, MIN,
                         ["d0r", "rc%d" % (2 * d - 2), "rc%d" % (2 * d - 1)], ["rs" + k])
                elif w[0] == "I":
                    ts(T.ri[:, 2 * d - 2:2 * d], T.rs[:, a + 127:a + 256:128], 1.0, MIN, ["rs" + k], ["ri" + k], 127.0, ADD)
                else:
                    tt(block(T.rz, 96 * t + 96)(d), T.bk[:, 144 * (d - 1):144 * d].indirect(T.ri[:, 2 * d - 2:2 * d]),
                       block(T.rz, 96 * t)(d), ADD, ["bk" + k, "bk0", "ri" + k, "rz%d_%d" % (t, d)], ["rz%d_%d" % (t + 1, d)])
                    n = send1(4 * t + 4, d, block(T.rz, 96 * t + 96)(d), block(T.W, WSZ * (1 - par) + 1280)(d),
                              "rz%d_%d" % (t + 1, d))
                    going[0] += n
                    sent[0] += n
                    tok["Wg0/%d" % (1 - par)] = {"w": ("arr%d" % (4 * t + 4), going[0]), "r": {}}
            elif w == "n4":
                nact(4, 0)
            elif w == "tl":
                ts(T.tl[:, 0:8], T.tfs[:, 15:128:16], 8192.0 + AB, ADD, ["tfs"], ["tl"])
            elif w == "f4":
                for h in (0, 1):
                    scan(T.tfs[:, 128 + 64 * h:192 + 64 * h], T.DD[:, 0:64], ps[FB[h]][:, 0:64], ADD, MIN,
                         ["DD", "ps%d" % FB[h]], ["tfs2_%d" % h])
            elif w == "old":
                act(T.old[:], T.AD[:, 0:2944].indirect(T.tl[:, 0:8]), ID, ADT + ["tl"], ["old"])
            elif w == "wd":
                tt(T.wd1[:, 0::2], T.tfs[:, 15:128:16], T.dum2[:], SUB, ["tfs", "dum2"], ["wd1"])
            elif w == "tl2":
                ts(T.tl[:, 8:16], T.tfs[:, 143::16], c_fix, ADD, both("tfs2") + ["c_fix"], ["tl2"], 1664.0, MIN)
            elif w == "cs":
                scan(T.cs[:], T.DQ[:], T.cmp[:], ADD, MIN, DQT + ["cmp%d" % a for a in range(8)], ["cs"])
            elif w == "ms":
                scan(T.ms[:], T.md0[:], T.md1[:], MUL, ADD, ["md0c", "md0d", "md01", "md02", "md03", "md04", "md14", "md15"] +
                     both("E1") + both("E2") + both("E3") + both("E4"), ["ms"])
            elif w == "win":
                ts(T.wd0[:, 1::2], T.cs[:, 0:576].indirect(T.lend[:, 0:1]), c_win, EQ, ["cs", "lend", "c_win"], ["win"])
            elif w == "sel":
                scan(T.win[:], T.wd0[:, 0:16], T.wd1[:], MUL, ADD, ["win", "wd0c", "wd1", "wd1c"], ["l2"])
            elif w == "yy":
                tt(T.yy[:], T.SR[:, 0:1672].indirect(T.tl[:, 8:16]), T.ms[:, 5::6], MUL, SRT + ["tl2", "ms"], ["yy"])
            elif w == "gap":
                vgap()
            elif w == "yr":
                dma("s", T.yr[:], T.yrb[:], "st", ["yr0"] + ["yr1%d" % i for i in range(4)], [], 16)
            elif w == "ll":
                cp(T.ll[:], T.win[:, 1::2], ["l2"], ["ll"])
            elif w == "put":
                tt(T.AD[:, 0:2944].indirect(T.ll[:, 0:8]), T.old[:], T.yy[:], SUB, ["ll", "old", "yy"] + ADT, ADT)

        going = [0]
        for w in (WLAST if last else WORDER).split():
            wstep(w)

    dma("s", T.yd[:], T.AD[:, 256:1280], "st", ["ADd"], [], 32)
    ts(T.yab[:, 0:672], T.AD[:, AB:AB + 672], AOFF, ADD, ["ADa0", "ADa"], ["yab0"])
    act(T.yab[:, 672:1280], T.AD[:, AB + 672:AB + 1280], ID, ["ADa"], ["yab1"], bias=AOFF)
    dma("a", T.ya[:], T.yab[:], "st", ["yab0", "yab1"], [], 48)
    g.wait_ge(T.sem.sent, sent[0])
    for e in ("v", "a", "p", "g"):
        g.wait_ge(T.sem[SEM[e]], cnt[e])
    g.wait_ge(T.sem.st, 48)
